import numpy as np, ml_dtypes
CORES = [23,119,17,113]
N = 4
BF = ml_dtypes.bfloat16
V, SQ, M, S, J = 3840, 8, 32, 4, 256
PAR = [0, 0, 0, 0, 0, 0, 0, 0, 0, 0, 0, 1, 1, 1, 1, 2, 2, 2, 3, 3, 4, 4, 11, 11, 11, 15, 15, 18, 22, 22, 23, 25]
ROW = [0, 0, 1, 2, 3, 4, 5, 6, 7, 8, 9, 0, 10, 11, 1, 0, 12, 13, 0, 14, 0, 15, 0, 1, 2, 0, 3, 0, 0, 5, 0, 0]
C = 64
def parts(rng):
    gi = np.arange(8)[:, None, None]
    od = np.argsort(rng.random((8, V)), axis=1); blk = ((np.argsort(od, axis=1) // C) * C)[:, None, :]
    base = od[gi, blk + rng.integers(0, C, (8, 16, V))]
    turn = (rng.integers(0, 8, (N, 8, 1, V)) * 2 + 1) * np.arange(16)[:, None] + rng.integers(0, 16, (N, 8, 1, V))
    q = np.take_along_axis(base[None], turn & 15, 2)
    own = rng.random(q.shape, dtype=np.float32)
    q = np.where(own < 0.2, od[gi, blk + rng.integers(0, C, q.shape)], q); q = np.where(own > 0.9, rng.integers(0, V, q.shape), q)
    size = np.exp2(rng.integers(-1, 2, (8, 16, 1))).astype(np.float32)
    k = (0.8 * rng.standard_normal((8, 16, V), dtype=np.float32) + 0.6 * rng.standard_normal((N, 8, 16, V), dtype=np.float32)) * size
    x = rng.standard_normal((N, 8, 16, SQ), dtype=np.float32) * size
    kp = (1.5 * rng.random((N, 8, 16, 1)) - 0.25) * size
    cm = np.take_along_axis(rng.integers(0, V // C, (N, 8, 4)), rng.integers(0, 4, (N, 8, SQ)), 2)
    tk = od[np.arange(8)[:, None], C * cm + rng.integers(0, C, (N, 8, SQ))]
    return q, k, x, kp, tk
def tidy(v):
    return np.where(np.abs(v) < 2.0 ** -60, 0, v)
def pack(q, k, x, kp, tk):
    return {"qt": np.ascontiguousarray(q.reshape(N, 128, V)).astype(np.int32), "kt": np.ascontiguousarray(tidy(k).reshape(N, 128, V)).astype(np.float32).astype(BF),
            "x0": np.ascontiguousarray(tidy(x).reshape(N, 128, SQ)).astype(np.float32), "kap": np.ascontiguousarray(tidy(kp).reshape(N, 128, 1)).astype(np.float32),
            "tok": np.ascontiguousarray(tk).astype(np.int32)}
def branch(rng, q, tk, g, e):
    w = rng.permutation(V)[:SQ * (e + 3)].reshape(e + 3, SQ); dep = [0]
    for n in range(1, M): dep.append(dep[PAR[n]] + 1)
    rows = sorted({ROW[n] for n in range(1, M) if dep[n] == e + 1}, reverse=True)
    tk[:, g] = w[0]
    for s in range(SQ):
        for i in range(e + 1): q[:, g, :, int(w[i, s])] = w[i + 1, s]
        for n in range(0, N, 2):
            q[n, g, :, int(w[e, s])] = w[e + 2, s]; q[n, g, rows[(s + SQ * (n // 2)) % len(rows)], int(w[e, s])] = w[e + 1, s]
def setup_inputs(rng):
    return pack(*parts(rng))
def setup_inputs_spread(rng):
    q, k, x, kp, tk = parts(rng)
    k = k * np.exp2(rng.integers(-3, 4, (8, 1, V))) * (rng.random((8, 1, V)) > 0.0625)
    x = x * np.exp2(rng.integers(-3, 4, (N, 8, 1, SQ))); kp = kp * np.exp2(rng.integers(-3, 3, (N, 8, 16, 1)))
    g = rng.permutation(8); z = np.ones((8, 1, 1)); z[g[:3]] = np.array([2.0 ** 12, 2.0 ** -50, 2.0 ** -57])[:, None, None]
    k = np.clip(k * z, -65536, 65536); x = np.clip(x * z, -65536, 65536); kp = np.clip(kp * z, -65536, 65536)
    branch(rng, q, tk, int(g[3]), 2); branch(rng, q, tk, int(g[4]), 1)
    return pack(q, k, x, kp, tk)
def setup_inputs_ends(rng):
    q, k, x, kp, tk = parts(rng)
    q = np.where(rng.random(q.shape, dtype=np.float32) < 0.72, rng.integers(0, 2, q.shape) * (V - 1), q)
    q[:, :, 15, V - 1] = V - 1; q[:, :, 14, V - 1] = 0; q[:, :, 0, 0] = 0; q[:, :, 1, 0] = V - 1
    tk = rng.integers(0, 2, tk.shape) * (V - 1); tk[:, :, 0] = 0; tk[:, :, SQ - 1] = V - 1
    k = np.clip(np.rint(2 * k) * 0.5, -4, 4); x = np.clip(np.rint(2 * x) * 0.5, -4, 4); kp = np.rint(2 * kp) * 0.5
    k[:, ::2, :, V - 1] = k[:, ::2, :, 0]
    k[:, 5, :, V - 1] = 40; k[:, 5, :, 0] = -40; k[:, 1, :, V - 1] = -40; k[:, 1, :, 0] = 40
    kp[N - 1, 7] = 64; kp[0, 7] = -64; kp[0, 4] = 64; kp[1, 4] = -64
    return pack(q, k, x, kp, tk)
def setup_inputs_corners(rng):
    q, k, x, kp, tk = parts(rng); ar = np.arange(V); g = rng.permutation(8)
    q[:, g[0]] = ar
    q[:, g[1]] = (ar + 1) % V; tk[:, g[1]] = V - 1 - rng.integers(0, 4, (N, SQ))
    q[:, g[2], 0::2] = (ar - 1) % V; q[:, g[2], 1::2] = ar; tk[:, g[2]] = rng.integers(0, 4, (N, SQ))
    for n in range(N): q[n, g[3]] = (q[n, g[3]] // N) * N + n
    tk[:, g[4]] = tk[:, g[4], :1]
    q[:, g[5]] = rng.permutation(V)
    q[:, g[6]] = np.where(rng.random((N, 16, V)) < 0.3, ar, rng.integers(0, 2, (N, 16, V)) * (V - 1))
    tk[:, g[7]] = rng.integers(0, 2, (N, SQ)) * (V - 1)
    return pack(q, k, x, kp, tk)
def setup_inputs_crowd(rng):
    q, k, x, kp, tk = parts(rng); g = rng.permutation(8)
    size = np.ones(M, np.int64); full = 256 // M; left = 256 - full * M; rows = []
    for n in range(M - 1, 0, -1): size[PAR[n]] += size[n]
    for n in range(1, M):
        if PAR[n] == 0 and size[n] <= left: left -= int(size[n]); rows.append(ROW[n])
    for i in range(4):
        h = int(g[i]); v = (V - 1, int(rng.integers(1, V - 1)), 0, int(rng.integers(1, V - 1)))[i]
        w = rng.permutation(V); w = w[w != v][:19]; u, p, z = int(w[0]), int(w[1]), int(w[2])
        q[:, h, :, v] = v; q[:, h, :, u] = v; q[:, h, :, z] = z; q[:, h, :, p] = z
        for c in rows: q[:, h, c, p] = v
        for c in w[3:]: q[:, h, :, int(c)] = v
        q[1::2, h, :, v] = w[3:][np.argsort(rng.random((N // 2, 16)), axis=1)]
        tk[:, h] = v
        for n in range(N):
            o = rng.permutation(SQ)
            if i % 2 == 1 and full < SQ: tk[n, h, o[full:]] = z; tk[n, h, o[full]] = p
            if i > 1: tk[n, h, o[0]] = u
    for i in (4, 5):
        w = rng.permutation(V)[:3]
        if i == 4: w = np.array([0, V - 1, 1 + int(rng.integers(0, V - 2))])
        for c in w: q[:, g[i], :, int(c)] = w[rng.integers(0, 3, (N, 16))]
        tk[:, g[i]] = w[rng.integers(0, 3, (N, SQ))]
    tk[:, g[6]] = tk[:, g[6], :1]; tk[:, g[7]] = tk[0, g[7], 0]
    return pack(q, k, x, kp, tk)
def setup_inputs_ties(rng):
    q, k, x, kp, tk = parts(rng)
    e = rng.integers(1, 4, (8, 16, 1)) * 2.0 ** -12 * np.where(rng.random((8, 16, 1)) < 0.6, -1, 1)
    k = np.clip(np.rint(4 * k) * 0.25, -2, 2); x = np.clip(np.rint(4 * x) * 0.25, -2, 2) + e
    kp = np.zeros((N, 1, 1, 1)) + e
    g = rng.permutation(8)[:4]; m = 2.0 ** -14 * np.array([1, 2, 3, 8, 16, 24, -1, -3])
    k[:, g] = np.where(rng.random((N, 4, 16, V), dtype=np.float32) < 0.3, 4096.0, 0.0)
    x[:, g] = rng.choice(m, (N, 4, 16, SQ))
    kp[:, g] = -4096.0
    x[:, g[3]] = 4096.0; kp[:, g[3]] = -rng.choice(m, (N, 16, 1))
    return pack(q, k, x, kp, tk)
def check_inputs(d):
    bad = []
    for k in ("qt", "tok"):
        if np.min(d[k]) < 0 or np.max(d[k]) > V - 1: bad.append("range of " + k)
    for k in ("kt", "x0", "kap"):
        v = np.asarray(d[k]).astype(np.float32)
        if not np.all(np.isfinite(v)) or not np.all(np.abs(v) <= 65536) or not np.all((v == 0) | (np.abs(v) >= 2.0 ** -60)): bad.append("size of " + k)
    return bad
def reference(qt, kt, x0, kap, tok):
    Q = qt.astype(np.int64).reshape(N, 8, 16, V); K = kt.astype(np.float32).reshape(N, 8, 16, V)
    x = np.array(x0, np.float32).reshape(N, 8, 16, SQ); kp = kap.astype(np.float32).reshape(N, 8, 16, 1, 1)
    A = np.array(Q); s = np.array(tok, np.int64); half = np.float32(0.5); gi = np.arange(8); trace = []; yn = np.zeros((N, 8, 16, M, SQ), np.float32)
    for t in range(S):
        for r in range(N):
            q = (r + 1 + t % (N - 1)) % N
            node = [s[r]]
            for n in range(1, M): node.append(np.take_along_axis(A[r][:, ROW[n]], node[PAR[n]], 1))
            tk = np.stack(node, axis=1)
            flat = tk.reshape(8, 1, J)
            kn = np.take_along_axis(K[q], flat, 2).reshape(8, 16, M, SQ)
            xs = [x[r]]
            for n in range(1, M): xs.append(xs[PAR[n]] * half + kn[:, :, n])
            xn = np.stack(xs, axis=2)
            th = (xn - kp[q]).reshape(8, 16, 1, J)
            cand = np.take_along_axis(Q[q], flat, 2)
            kc = np.take_along_axis(K[q], cand.reshape(8, 1, 16 * J), 2).reshape(8, 16, 16, J)
            score = np.add.reduce((kc >= th).astype(np.int64), axis=1)
            cols = np.take_along_axis(cand, np.argsort(-score, axis=1, kind="stable"), 1)
            top = cols[:, 0].reshape(8, M, SQ)
            ok = np.zeros((8, M, SQ), bool); ok[:, 0] = True; best = np.zeros((8, SQ), np.int64)
            for n in range(1, M):
                ok[:, n] = ok[:, PAR[n]] & (tk[:, n] == top[:, PAR[n]]); best = np.where(ok[:, n], n, best)
            s[r] = np.take_along_axis(top, best[:, None, :], 1)[:, 0]
            x[r] = np.take_along_axis(xn, best[:, None, None, :], 2)[:, :, 0]
            if t < S - 1:
                for j in range(J): A[r][gi, :, flat[:, 0, j]] = cols[:, :, j]
            else: yn[r] = xn
        trace.append(np.array(s))
    return {"yt": np.stack(trace, axis=2).reshape(N, 8, S * SQ).astype(np.float32), "yx": x.reshape(N, 128, SQ), "yn": yn.reshape(N, 128, J)}

@@ -1,0 +1,724 @@
+from concourse.mybir import AluOpType as Op, AxisListType as Ax, ActivationFunctionType as Fn
+
+V, S = 3840, 4
+PAR = [0, 0, 0, 0, 0, 0, 0, 0, 0, 0, 0, 1, 1, 1, 1, 2, 2, 2, 3, 3, 4, 4, 11, 11, 11, 15, 15, 18, 22, 22, 23, 25]
+ROW = [0, 0, 1, 2, 3, 4, 5, 6, 7, 8, 9, 0, 10, 11, 1, 0, 12, 13, 0, 14, 0, 15, 0, 1, 2, 0, 3, 0, 0, 5, 0, 0]
+DEP = [0]
+for _n in range(1, 32):
+    DEP.append(DEP[PAR[_n]] + 1)
+LV3 = [28, 29, 30, 31]
+LV2 = [PAR[n] for n in LV3] + list(range(22, 28))
+LV1 = list(range(10, 22)) + [11, 11, 11, 15, 15, 18]
+LV0 = list(range(0, 10)) + [1, 1, 1, 2, 2, 2, 3, 3, 4, 4]
+LEVELS = [LV0, LV1, LV2, LV3]
+
+
+def _blocks(lv, nxt):
+    have = [tuple(lv[i:i + 2]) for i in range(0, len(lv), 2)]
+    return [have.index((PAR[nxt[i]], PAR[nxt[i + 1]])) for i in range(0, len(nxt), 2)]
+
+
+TAKE = [_blocks(LV0, LV1) + [0] + list(range(5)) + [0], list(range(6)) + _blocks(LV1, LV2) + [0] * 5]
+LOFF = [0, 160, 304, 384]
+CH = [(0, 5), (5, 13), (13, 16)]
+PC = [(0, 5), (5, 11), (11, 16)]
+RL = V + 16
+PICK = 30720 + 65536
+QCUT = 2560
+NE = 8
+
+SCRATCH = {
+    "Q": ("sbuf", [128, V], "int32"), "K": ("sbuf", [128, V], "bfloat16"), "AW": ("sbuf", [128, RL + 264], "int32"),
+    "IO": ("sbuf", [128, V], "float32"), "IOb": ("sbuf", [128, 144], "bfloat16"),
+    "xs": ("sbuf", [128, 8], "float32"), "IK": ("sbuf", [128, 256], "bfloat16"), "IG": ("sbuf", [128, 128], "bfloat16"),
+    "BO": ("sbuf", [128, 128], "float16"), "BO16": ("sbuf", [128, 128], "float16"), "Ib": ("sbuf", [128, 128], "bfloat16"),
+    "D1": ("sbuf", [128, 256], "bfloat16"), "CKa": ("sbuf", [128, 416], "bfloat16"), "F2": ("sbuf", [128, 416], "bfloat16"),
+    "RZ": ("sbuf", [128, 160], "bfloat16"), "sc": ("sbuf", [128, 416], "float32"), "GL": ("sbuf", [128, 4], "uint16"), "TM": ("sbuf", [128, 256], "bfloat16"),
+    "kp": ("sbuf", [128, 4], "float32"), "pi": ("sbuf", [128, 32], "int32"), "pj": ("sbuf", [128, 32], "int32"),
+    "C": ("sbuf", [128, 16], "float32"), "CJ": ("sbuf", [128, 16], "float32"),
+    "Zb": ("sbuf", [128, 144], "bfloat16"), "Zh": ("sbuf", [128, 144], "float16"), "Z2": ("sbuf", [128, 136], "float16"),
+    "Ih": ("sbuf", [128, 128], "float16"), "DM": ("sbuf", [128, 2048], "bfloat16"),
+    "XC": ("sbuf", [128, 80], "float32"), "CB": ("sbuf", [128, 96], "float32"), "cc": ("sbuf", [128, 12], "uint16"),
+    "ccu": ("sbuf", [128, 16], "uint16"), "thx": ("sbuf", [128, 128], "float32"),
+    "cb": ("sbuf", [128, 128], "float16"), "hx": ("sbuf", [128, 16], "float32"),
+    "tkT": ("sbuf", [128, 128], "float32"), "cv": ("sbuf", [128, 128], "float32"), "cm": ("sbuf", [128, 2], "float32"),
+    "TIE": ("sbuf", [128, 128], "bfloat16"),
+    "DL": ("sbuf", [128, 16], "uint16"), "DL2": ("sbuf", [128, 6], "uint16"), "JD": ("sbuf", [128, 32], "float32"),
+    "ch": ("sbuf", [128, 256], "float16"),
+    "F": ("sbuf", [128, 1152], "bfloat16"),
+    "PL": ("sbuf", [128, 16], "uint16"), "PL2": ("sbuf", [128, 12], "uint16"), "PP": ("sbuf", [128, 6], "uint16"),
+    "CX": ("sbuf", [128, 8], "uint16"), "SCL": ("sbuf", [128, 256], "float32"), "ISC": ("sbuf", [128, 256], "float32"),
+    "JT": ("sbuf", [128, 32], "float32"), "RM": ("sbuf", [128, 32], "float32"), "RS0": ("sbuf", [128, 112], "float32"),
+    "bf": ("sbuf", [128, 4], "float32"), "M": ("sbuf", [128, 16], "float32"),
+    "bu": ("sbuf", [128, 2], "uint16"), "w1": ("sbuf", [128, 16], "float16"), "l0": ("sbuf", [128, 16], "uint16"),
+    "wf": ("sbuf", [128, 256], "float32"), "wh": ("sbuf", [128, 256], "float16"),
+    "O0": ("sbuf", [128, 64], "uint16"), "O1": ("sbuf", [128, 64], "uint16"), "O2": ("sbuf", [128, 32], "uint16"),
+    "LM": ("sbuf", [128, 96], "uint16"), "Y": ("sbuf", [128, 4 * 272], "float32"),
+    "cu": ("sbuf", [128, 256], "uint16"), "kn": ("sbuf", [128, 256], "float32"),
+    "kc": ("sbuf", [128, 4096], "bfloat16"), "bits": ("sbuf", [128, 4096], "float16"),
+    "key": ("sbuf", [128, 256], "bfloat16"), "sg": ("sbuf", [128, 2048], "bfloat16"),
+    "R": ("sbuf", [128, 3 * 264], "int32"), "B": ("sbuf", [128, 256], "float32"), "eq": ("sbuf", [128, 256], "float16"),
+    "E": ("sbuf", [128, 96], "float32"), "t1": ("sbuf", [128, 64], "float32"), "t2": ("sbuf", [128, 32], "float32"),
+    "bq": ("sbuf", [128, 4], "uint16"), "ig": ("sbuf", [128, 16], "float32"), "X": ("sbuf", [128, 4 * 32], "float32"),
+    "lf": ("sbuf", [128, 24], "float32"), "Bo": ("sbuf", [128, 3 * 96], "float32"),
+    "de": ("sbuf", [128, 3 * 112], "float32"), "ds": ("sbuf", [128, 3 * 112], "float32"),
+    "OF": ("sbuf", [128, 32], "uint16"), "yb": ("sbuf", [128, 48], "float32"),
+    "YN": ("sbuf", [128, 288], "float32"), "YL": ("sbuf", [128, 288], "float32"),
+    "pth": ("psum", [128, 512], "float32"), "psl": ("psum", [128, 512], "float32"),
+    "ps0": ("psum", [128, 512], "float32"), "ps1": ("psum", [128, 512], "float32"),
+    "pa0": ("psum", [128, 512], "float32"), "pb0": ("psum", [128, 512], "float32"),
+    "pa1": ("psum", [128, 512], "float32"), "pb1": ("psum", [128, 512], "float32"),
+}
+SEMAPHORES = (["sv", "sa", "sp", "sq", "sent", "dtok", "dx", "dkap", "dk", "dout", "yn0", "fin", "dq0", "dq1", "dq2", "sent0"]
+              + ["m%d%d" % (t, i) for t in range(S) for i in range(3)] + ["r%d%d" % (t, i) for t in range(3) for i in range(3)]
+              + ["x%d" % t for t in range(S)])
+
+
+def runs(vals):
+    out, a = [], 0
+    for i in range(1, len(vals) + 1):
+        if i == len(vals) or vals[i] != vals[a]:
+            out.append((a, i, vals[a]))
+            a = i
+    return out
+
+
+def rank_program(g, core, T, topo):
+    rank = T.rank_of(core)
+    if rank is None:
+        return
+    n_ranks = len(T.cores)
+    qu = {"V": g.vector, "A": g.scalar, "P": g.tensor, "G": g, "S": g.sync}
+    semof = {"V": "sv", "A": "sa", "P": "sp", "G": "sq"}
+    cnt = {}
+    waited = {e: {} for e in qu}
+    wr, rd, bank = {}, {}, {}
+
+    def need(e, tok):
+        if tok is not None and waited[e].get(tok[0], 0) < tok[1]:
+            qu[e].wait_ge(T.sem[tok[0]], tok[1])
+            waited[e][tok[0]] = tok[1]
+
+    def order(e, r, w, b):
+        own = semof.get(e)
+        best = {}
+        toks = [wr.get(k) for k in r]
+        for k in w:
+            toks += [t for t in [wr.get(k)] + rd.get(k, []) if t is not None and (e != "P" or t[0] != own)]
+        toks += [bank[k] for k in b if k in bank and bank[k][0] != own]
+        for t in toks:
+            if t is not None:
+                best[t[0]] = max(best.get(t[0], 0), t[1])
+        for s in best:
+            need(e, (s, best[s]))
+
+    def note(tok, r, w, b):
+        for k in r:
+            rd.setdefault(k, []).append(tok)
+        for k in w:
+            wr[k] = tok
+            rd[k] = []
+        for k in b:
+            bank[k] = tok
+
+    def op(e, fn, r=(), w=(), b=()):
+        order(e, r, w, b)
+        s = semof[e]
+        cnt[s] = cnt.get(s, 0) + 1
+        fn().then_inc(T.sem[s], 1)
+        note((s, cnt[s]), r, w, b)
+
+    def dma(e, out, in_, sem, r=(), w=()):
+        order(e, r, w, ())
+        cnt[sem] = cnt.get(sem, 0) + 16
+        qu[e].dma_start(out, in_).then_inc(T.sem[sem], 16)
+        note((sem, cnt[sem]), r, w, ())
+
+    def send(to, out, in_, sem, r, local="sent"):
+        order("G", r, (), ())
+        dst = T.cores[to]
+        rid, pid = topo.addr(dst)[:2]
+        mask = sum(1 << e for e in topo.engines(core, dst)[:NE])
+        g.remote_dma(out, in_, T.sem[sem], T.sem[local], pid, rid, mask)
+        cnt[local] = cnt.get(local, 0) + NE
+
+    def lands(key, sem):
+        wr[key] = (sem, NE)
+        rd[key] = []
+        cnt[sem] = NE
+
+    v, a, pe = g.vector, g.scalar, g.tensor
+    C = lambda i: T.C[:, i:i + 1]
+    KF, G16, SC, NB, NK, KB, Z15, PF, KP1, DMK, DUM, BC, NKP, KT, KR, K2 = range(16)
+
+    def verifier(r, t):
+        return (r + 1 + t % (n_ranks - 1)) % n_ranks
+
+    def drafter(q, t):
+        return (q - 1 - t % (n_ranks - 1)) % n_ranks
+
+    op("V", lambda: v.memset(T.AW[:, RL:RL + 8], 0), w=["Rl"])
+    op("V", lambda: v.memset(T.AW[:, RL + 8:RL + 264], 0), w=["Rl2"])
+    op("V", lambda: v.memset(T.AW[:, V:RL], 0), w=["spare"])
+    dma("A", T.xs[:], T.x0[:], "dx", w=["xs"])
+    dma("S", T.AW[:, 0:QCUT], T.qt[:, 0:QCUT], "dq0", w=["A0"])
+    dma("A", T.AW[0:128:16, RL:RL + 8], T.tok[:], "dtok", w=["Rl"])
+    dma("A", T.kp[:, 0:1], T.kap[:], "dkap", w=["kp"])
+    dma("S", T.AW[:, QCUT:V], T.qt[:, QCUT:V], "dq1", w=["A"])
+    dma("S", T.K[:], T.kt[:], "dk", r=["A0"], w=["K"])
+
+    op("G", lambda: g.iota(T.pi[:, 0:1], [[0, 1]], 0, 1), w=["pi"])
+    op("G", lambda: g.iota(T.IO[:, 0:256], [[1, 256]], 0, 0, allow_small_or_imprecise_dtypes=True), w=["IO0"])
+    op("G", lambda: g.iota(T.pi[:, 16:32], [[-1, 16]], 16, 1), w=["pi2"])
+    op("G", lambda: g.iota(T.IK[:], [[0, 16], [1, 16]], 0, 0, allow_small_or_imprecise_dtypes=True), w=["IK"])
+    op("G", lambda: g.iota(T.IG[:], [[16, 8], [0, 16]], 0, 0, allow_small_or_imprecise_dtypes=True), w=["IG"])
+    op("V", lambda: v.memset(T.M[:], 0.0), w=["M"])
+    for col, m in ((0, 15), (1, 112), (2, 7), (3, 8)):
+        op("V", lambda: v.tensor_scalar(T.pj[:, col:col + 1], T.pi[:, 0:1], m, None, Op.bitwise_and), r=["pi"], w=[("pj", col)])
+    op("V", lambda: v.tensor_copy(C(PF), T.pi[:, 0:1]), r=["pi"], w=["C1"])
+    op("V", lambda: v.tensor_copy(T.C[:, 0:4], T.pj[:, 0:4]), r=[("pj", i) for i in range(4)], w=["C0"])
+    for col, src, s1, s2, f0, f1 in ((Z15, G16, 15.0, 0.0, Op.add, Op.add), (NK, KF, -4096.0, 0.0, Op.mult, Op.add),
+                                     (KB, KF, -1.0, -121.0, Op.mult, Op.add), (KP1, KF, 1.0, 0.0, Op.add, Op.add),
+                                     (DMK, KF, 15.0, 4096.0, Op.is_lt, Op.mult), (DUM, KF, float(V), 0.0, Op.add, Op.add),
+                                     (BC, NB, 0.0, 1.0, Op.is_equal, Op.mult), (KT, KF, 4096.0, -2048.0, Op.mult, Op.add),
+                                     (KR, KF, -4096.0, 32768.0, Op.mult, Op.add), (K2, SC, float(RL + 28672), 0.0, Op.add, Op.add)):
+        op("V", lambda: v.tensor_scalar(C(col), C(src), s1, s2, f0, f1), r=["C0"], w=[("C", col)])
+    CK = ["C0", "C1"] + [("C", c) for c in (NK, KB, Z15, KP1, DMK, DUM, BC, KT, KR, K2)]
+    op("V", lambda: v.tensor_copy(T.IOb[:], T.IO[:, 0:144]), r=["IO0"], w=["IOb"])
+    op("V", lambda: v.tensor_scalar(T.Zb[:], T.IOb[:], C(Z15), None, Op.is_equal), r=["IOb"] + CK, w=["Zb"])
+    op("V", lambda: v.tensor_scalar(T.Zh[:], T.IOb[:], C(Z15), None, Op.is_equal), r=["IOb"] + CK, w=["Zh"])
+    op("V", lambda: v.tensor_scalar(T.Ih[:], T.IOb[:, 0:128], C(PF), None, Op.is_equal), r=["IOb"] + CK, w=["Ih"])
+    op("V", lambda: v.tensor_scalar(T.Ib[:], T.IOb[:, 0:128], C(PF), None, Op.is_equal), r=["IOb"] + CK, w=["Ib"])
+    op("V", lambda: v.tensor_tensor(T.Z2[:], T.Zh[:, 0:136], T.Zh[:, 8:144], Op.add), r=["Zh"], w=["Z2"])
+    op("V", lambda: v.tensor_scalar(T.D1[:], T.IK[:], C(KF), 65536.0, Op.is_equal, Op.mult), r=["IK"] + CK, w=["D1"])
+    op("V", lambda: v.tensor_scalar(T.RZ[:], T.IK[:, 0:160], 0.0, None, Op.not_equal), r=["IK"], w=["RZ"])
+    op("V", lambda: v.tensor_scalar(T.BO[:], T.IG[:], C(G16), None, Op.is_equal), r=["IG"] + CK, w=["BO"])
+    op("V", lambda: v.tensor_scalar(T.BO16[:], T.IG[:], C(G16), 16.0, Op.is_equal, Op.mult), r=["IG"] + CK, w=["BO16"])
+    op("V", lambda: v.tensor_scalar(T.RS0[:], T.IK[:, 0:112], C(KP1), None, Op.not_equal), r=["IK"] + CK, w=["RS0"])
+    op("V", lambda: v.tensor_copy(T.CX[:], T.IO[:, 0:8]), r=["IO0"], w=["CX"])
+    op("V", lambda: v.tensor_scalar(T.RM[:], T.IO[:, 0:32], 0.0, None, Op.not_equal), r=["IO0"], w=["RM"])
+    op("V", lambda: v.tensor_scalar(T.RS0[:, 0:112:16], T.IO[:, 0:7], 0.0, C(DMK), Op.mult, Op.add), r=["RS0", "IO0"] + CK, w=["RS0"])
+    rows = [ROW[n] for lv in LEVELS for n in lv]
+    op("G", lambda: g.iota(T.F[:, 8:80], [[4096, 9], [0, 8]], 2048, 0, allow_small_or_imprecise_dtypes=True), w=[("F", 0)])
+    FK = [("F", 0)]
+    take = TAKE[0] + TAKE[1]
+    for lo, hi, d in runs([b - i for i, b in enumerate(take)]):
+        k = ("F", len(FK))
+        op("G", lambda: g.iota(T.F[:, 1120 + lo:1120 + hi], [[16, hi - lo]], 16 * take[lo] + 15, 0, allow_small_or_imprecise_dtypes=True), w=[k])
+        FK.append(k)
+    todo = [(0, 8, 2048)] + [(8 * (10 + lo), 8 * (10 + hi), 4096 * r + 2048) for lo, hi, r in runs(rows[10:])]
+    todo += [(544 + 8 * lo, 544 + 8 * hi, 8 * p) for lo, hi, p in runs(PAR)]
+    todo += [(832 + lo, 832 + hi, p) for lo, hi, p in runs([PAR[p] for p in PAR])]
+    todo += [(864 + 8 * lo, 864 + 8 * hi, 16 * d) for lo, hi, d in runs(DEP)]
+    for i, (lo, hi, val) in enumerate(todo):
+        k = ("F", len(FK))
+        if i % 4 == 0:
+            op("V", lambda: v.memset(T.F[:, lo:hi], float(val)), w=[k])
+        else:
+            op("A", lambda: a.activation(T.F[:, lo:hi], T.IO[:, 0:hi - lo], Fn.Identity, bias=float(val), scale=0.0), r=["IO0"], w=[k])
+        FK.append(k)
+    send(verifier(rank, 0), T.Y[:, 0:8], T.xs[:], "x0", ["xs"])
+    lands(("Yr", 0), "x0")
+
+    def select():
+        ins = None
+        for i in range(16):
+            ins = pe.matmul(T.ps1[:, 0:38], T.Zb[:, 15 - i:143 - i], T.F[:, 544 + i:1152:16], i == 0, i == 15)
+        return ins
+    op("V", lambda: v.tensor_scalar(T.pj[:, 16:32], T.pi[:, 16:32], 15, None, Op.bitwise_and), r=["pi2"], w=["pj2"])
+    op("V", lambda: v.tensor_scalar(T.CJ[:], T.pj[:, 16:32], C(G16), None, Op.add), r=["pj2", "C0"], w=["CJ"])
+
+    def shifts(j0, j1):
+        for j in range(j0, j1):
+            op("V", lambda: v.tensor_scalar(T.DM[:, 128 * j:128 * j + 128], T.IOb[:, 0:128], T.CJ[:, j:j + 1],
+                                            2048.0 if j <= 8 else -2048.0, Op.is_equal, Op.mult), r=["IOb", "CJ"], w=[("DM", j)])
+    shifts(1, 9)
+    op("G", lambda: g.affine_select(T.DM[:, 128:1152], T.DM[:, 128:1152], [[0, 8], [-1, 128]], Op.not_equal, -2048.0, 0, 1),
+       r=[("DM", x) for x in range(1, 9)], w=["DMa"])
+    op("V", lambda: v.tensor_scalar(T.F[:, 800:832], T.F[:, 544:800:8], 0.125, None, Op.mult), r=FK, w=["Fp"])
+    op("P", select, r=FK + ["Fp", "Zb"], w=["tab"], b=["ps1"])
+    op("V", lambda: v.tensor_scalar(T.F2[:], T.F[:, 0:416], C(NK), None, Op.add), r=FK + CK, w=["F2"])
+    for lo, hi in ((0, 256), (256, 416)):
+        op("V", lambda: v.tensor_tensor(T.CKa[:, lo:hi], T.F[:, lo:hi], T.D1[:, 0:hi - lo], Op.min), r=FK + ["D1"], w=[("CKa", lo)])
+    CKK = [("CKa", lo) for lo in (0, 256)]
+    shifts(9, 16)
+    op("G", lambda: g.affine_select(T.DM[:, 1152:2048], T.DM[:, 1152:2048], [[0, 7], [-1, 128]], Op.not_equal, 2048.0, 0, 1),
+       r=[("DM", x) for x in range(9, 16)], w=["DMb"])
+    shifts(0, 1)
+    for dst, lo, hi, s2, key in ((T.GL[:, 0:4:2], 36, 38, 0.0, "GL"), (T.PL[:], 0, 16, C(SC), "PL"), (T.PL2[:, 0:11], 5, 16, C(SC), "PL2"), (T.PP[:, 2:6], 16, 20, 0.0, "PP"),
+                                 (T.PP[:, 0:2], 16, 18, 0.0, "PP0"), (T.DL[:], 20, 36, C(SC), "DL"), (T.DL2[:, 0:5], 31, 36, C(SC), "DL2")):
+        op("V", lambda: v.tensor_scalar(dst, T.ps1[:, lo:hi], 0.0625, s2, Op.mult, Op.add), r=["tab"] + CK, w=[key], b=["ps1"])
+    op("V", lambda: v.tensor_scalar(T.JD[:], T.F[:, 864:1120:8], 0.0625, None, Op.mult), r=FK, w=["JD"])
+    wr["best"] = wr["Rl2"]
+    RK = ["Rl", "Rl2"]
+    for i, n in enumerate((256, 512, 1024, 2048)):
+        m = min(2 * n, V)
+        op("A", lambda: a.activation(T.IO[:, n:m], T.IO[:, 0:m - n], Fn.Identity, bias=float(n)),
+           r=["IO%d" % j for j in range(i + 1)], w=["IO%d" % (i + 1)])
+    IOK = ["IO%d" % j for j in range(5)]
+    for lo, hi, d in runs(DEP):
+        op("A", lambda: a.activation(T.SCL[:, 8 * lo:8 * hi], T.IO[:, 8 * lo:8 * hi], Fn.Identity, bias=float(2 ** d if d else 0), scale=0.0), r=["IO0"], w=[("SCL", d)])
+        op("A", lambda: a.activation(T.ISC[:, 8 * lo:8 * hi], T.IO[:, 8 * lo:8 * hi], Fn.Identity, bias=0.5 ** d, scale=0.0), r=["IO0"], w=[("ISC", d)])
+    SK, IK = [("SCL", d) for d in range(5)], [("ISC", d) for d in range(5)]
+    op("A", lambda: a.activation(T.JT[:], T.IO[:, 0:32], Fn.Identity, scale=8.0), r=["IO0"], w=["JT"])
+    DK = [("DM", 0), "DMa", "DMb"]
+
+
+    def late(i):
+        if i == 0:
+            op("V", lambda: v.tensor_scalar(T.TM[:, 0:128], T.IG[:], 0.0625, C(SC), Op.mult, Op.not_equal), r=["IG"] + CK, w=["TM0"])
+            op("A", lambda: a.activation(C(NKP), T.kp[:, 0:1], Fn.Copy, scale=-1.0), r=["kp"], w=["NKP"])
+            op("A", lambda: a.activation(T.TM[:, 128:256], T.IK[:, 0:128], Fn.Identity, bias=15.0, scale=-1.0), r=["IK"], w=["TM1"])
+        if i == 1:
+            op("A", lambda: a.activation(T.TM[:, 0:128], T.TM[:, 0:128], Fn.Copy, scale=-512.0), r=["TM0"], w=["TM0"])
+            op("V", lambda: v.tensor_tensor(T.TIE[:], T.TM[:, 0:128], T.TM[:, 128:256], Op.add), r=["TM0", "TM1"], w=["TIE"])
+
+    def top_of(win, keys, lst, lkey):
+        op("V", lambda: v.tensor_scalar(T.w1[:], win.indirect(lst), C(KT), 2048.0, Op.add, Op.min), r=keys + [lkey] + CK, w=["w1"])
+
+        def mm():
+            ins = None
+            for s in range(8):
+                ins = pe.matmul(T.psl[:, 0:1], T.Z2[:, 7 - s:135 - s], T.w1[:, s:s + 1], s == 0, s == 7)
+            return ins
+        op("P", mm, r=["w1", "Z2"], w=["sel"], b=["psl"])
+
+    def scatter(c0, c1, key):
+        for c in range(c0, c1):
+            op("V", lambda: v.tensor_copy(T.AW[:, 0:RL].indirect(T.OF[:, 2 * c:2 * c + 1]), T.AW[:, RL + 16 * c:RL + 16 * c + 16]),
+               r=[key, ("OF", 0 if c < 5 else 1 if c < 11 else 2), "spare"], w=["A"])
+
+    for t in range(S):
+        q, rr = verifier(rank, t), drafter(rank, t)
+        last = t == S - 1
+        o0, o1, o2 = T.O0, T.O1, T.O2
+        outs = [o0[:, 16 * t:16 * t + 16], o1[:, 16 * t:16 * t + 16], o2[:, 8 * t:8 * t + 5], o2[:, 8 * t + 5:8 * t + 7]]
+        lists = [T.l0[:, 0:10], o0[:, 16 * t:16 * t + 9], o1[:, 16 * t + 6:16 * t + 11], o2[:, 8 * t:8 * t + 2]]
+        mine = [o0[:, 16 * t + 10:16 * t + 15], o1[:, 16 * t:16 * t + 6], o2[:, 8 * t + 2:8 * t + 7]]
+        mineK = [[("L", 1)], [("L", 2)], [("L", 3), ("L", 4)]]
+        lm = lambda c0, c1: T.LM[:, 24 * t + c0 + (c0 > 0):24 * t + c1 + (c0 > 0)]
+        mk = lambda c: ("LM", t, 0 if c < 5 else 1 if c < 11 else 2)
+        for i in range(3):
+            lands(("LM", t, i), "m%d%d" % (t, i))
+
+        def repeat(p, i):
+            if last:
+                return
+            nc = PC[p][1] - PC[p][0]
+            lf, d0 = T.lf[:, 8 * p:8 * p + nc], 112 * p
+            if i == 0:
+                lst, x = mine[p], nc
+                for lo, hi, c0 in (((0, 80, 0),), ((160, 256, 0),), ((336, 384, 0), (384, 416, 3)))[p]:
+                    op("A", lambda: a.activation(T.lf[:, 8 * p + c0:8 * p + c0 + (hi - lo) // 16], T.sc[:, lo + 15:hi:16], Fn.Identity, bias=-float(PICK)),
+                       r=mineK[p], w=[("lf", p)])
+                op("A", lambda: a.activation(T.Bo[:, 96 * p:96 * p + 16 * x], T.IO[:].indirect(lst), Fn.Copy), r=mineK[p] + IOK, w=[("Bo", p)])
+            if i == 1:
+                bo = 96 * p
+                op("V", lambda: v.tensor_tensor(T.de[:, d0:d0 + 16 * nc], lf.indirect(T.CX[:, 0:nc]), T.Bo[:, bo:bo + 16 * nc], Op.is_equal),
+                   r=[("lf", p), ("Bo", p), "CX", "RS0"], w=[("de", p)])
+            if i == 2:
+                op("A", lambda: a.activation(T.de[:, d0 + 16:d0 + 16 * nc + 1:16], lf, Fn.Copy), r=[("lf", p), ("de", p)], w=[("de", p)])
+            if i == 3:
+                op("V", lambda: v.tensor_tensor_scan(T.ds[:, d0 + 1:d0 + 16 * nc + 1], T.RS0[:, 1:16 * nc + 1], T.de[:, d0 + 1:d0 + 16 * nc + 1],
+                                                     0.0, Op.mult, Op.add), r=[("de", p), "RS0"], w=[("ds", p)])
+            if i == 4:
+                op("V", lambda: v.tensor_scalar(T.OF[:, 2 * PC[p][0]:2 * PC[p][1]:2], T.ds[:, d0 + 16:d0 + 16 * nc + 1:16], C(DUM), None, Op.min),
+                   r=[("ds", p)] + CK, w=[("OF", p)])
+        def root():
+            bcol = T.AW[:, RL + 256:RL + 257]
+            op("V", lambda: v.tensor_scalar(T.bu[:, 0:1], bcol, C(SC), None, Op.add), r=["best"] + CK, w=["bu"])
+            if t > 0:
+                scatter(13, 14, RK[2])
+            top_of(T.AW[:, RL:RL + 256], RK, T.bu[:, 0:1], "bu")
+            op("V", lambda: v.tensor_scalar(T.M[:, 0:1], bcol, C(K2), C(BC), Op.add, Op.mult), r=["best", "M"] + CK, w=["M0"])
+            if t > 0:
+                scatter(14, 16, RK[2])
+            op("V", lambda: v.tensor_scalar(T.l0[:], T.M[:], T.psl[:, 0:1], 28672.0, Op.max, Op.subtract), r=["M0", "sel"], w=[("L", 0)], b=["psl"])
+            if t > 0:
+                op("A", lambda: a.activation(T.yb[:, 16 * t - 16:16 * t], T.IO[:].indirect(T.l0[:, 2:3]), Fn.Copy), r=[("L", 0)] + IOK, w=[("yb", t)])
+                dma("S", T.yt[:, 8 * t - 8:8 * t], T.yb[0:128:16, 16 * t - 16:16 * t - 8], "dout", r=[("yb", t)])
+
+        def pick(lv):
+            n = 8 * len(LEVELS[lv])
+            lo = LOFF[lv]
+            win = T.AW[:, 0:RL + 256] if lv == 0 else T.AW[:, 0:V]
+
+            def mm():
+                pe.matmul(T.psl[:, 0:n], T.Ib[:], T.CKa[:, lo:lo + n], True, False)
+                return pe.matmul(T.psl[:, 0:n], T.Ib[:], T.D1[:, 0:n], False, False)
+            op("P", mm, r=["Ib", "D1"] + CKK, w=["sel"], b=["psl"])
+            op("V", lambda: v.tensor_tensor(T.wf[:, 0:n], win.indirect(lists[lv]), T.F2[:, lo:lo + n], Op.subtract),
+               r=["A", "A0", ("L", lv), "spare", "F2"] + (RK if lv == 0 else []), w=["wf"])
+            op("V", lambda: v.tensor_scalar(T.wh[:, 0:n], T.wf[:, 0:n], -2048.0, 2048.0, Op.max, Op.min), r=["wf"], w=["wh"])
+            op("P", lambda: pe.matmul(T.psl[:, 0:n], T.BO[:], T.wh[:, 0:n], False, True), r=["wh", "BO"], w=["sel"], b=["psl"])
+
+        def listed(lv):
+            n, lo = 8 * len(LEVELS[lv]), LOFF[lv]
+            op("V", lambda: v.tensor_tensor_scan(T.sc[:, lo:lo + n], T.RZ[:, 0:n], T.psl[:, 0:n], 0.0, Op.mult, Op.max),
+               r=["sel", "RZ"], w=[("sc", lv)], b=["psl"])
+            src = T.sc[:, lo:lo + n].indirect(T.GL[:, 2 * lv:2 * lv + 1]) if lv < 2 else T.sc[:, lo + 15:lo + n:16]
+            op("V", lambda: v.tensor_scalar(outs[lv], src, -float(PICK), None, Op.add), r=[("sc", lv), "GL"], w=[("L", lv + 1)])
+            if lv != 2:
+                p = min(lv, 2)
+                send(q, lm(PC[p][0], PC[p][1]), mine[p], "m%d%d" % (t, p), mineK[p], "sent0" if (t, lv) == (0, 3) else "sent")
+
+        qwin, QK = (T.AW[:, 0:V], ["A"]) if t == 0 else (T.Q[:], ["Q"])
+        y0, r0 = 272 * t + 16, 264 * t
+        Y = lambda j0, j1: T.Y[:, y0 + j0:y0 + j1]
+        R = lambda j0, j1: T.R[:, r0 + j0:r0 + j1]
+        CUK = [("cu", 0), ("cu", 5), ("cu", 11)]
+
+        def cand(c0, c1):
+            op("V", lambda: v.tensor_copy(T.cu[:, 16 * c0:16 * c1], qwin.indirect(lm(c0, c1))), r=QK + [mk(c0)], w=[("cu", c0)])
+
+        def gather(j0, j1, e, ck):
+            src = T.K[:].indirect(T.cu[:, j0:j1])
+            if e == "A":
+                op("A", lambda: a.activation(T.kc[:, 16 * j0:16 * j1], src, Fn.Copy), r=["K", ("cu", ck)], w=[("kc", j0)])
+            else:
+                op("V", lambda: v.tensor_copy(T.kc[:, 16 * j0:16 * j1], src), r=["K", ("cu", ck)], w=[("kc", j0)])
+        KCK = [[0], [80, 160, 176], [208]]
+
+        root()
+        if not last:
+            pick(0)
+            if t > 0:
+                late(t - 1)
+            listed(0)
+            repeat(0, 0)
+            pick(1)
+            repeat(0, 1)
+            repeat(0, 2)
+            listed(1)
+            repeat(1, 0)
+            pick(2)
+            repeat(0, 3)
+            listed(2)
+            pick(3)
+            cand(0, 5)
+            gather(0, 80, "A", 0)
+            listed(3)
+        if t == 0:
+            need("S", ("sent0", NE))
+            dma("S", T.Q[:], T.qt[:], "dq2", w=["Q"])
+
+        def numbers(c0, c1):
+            op("V", lambda: v.tensor_tensor(T.kn[:, 16 * c0:16 * c1], T.K[:].indirect(lm(c0, c1)), T.SCL[:, 16 * c0:16 * c1], Op.mult),
+               r=["K", mk(c0)] + SK, w=[("kn", c0)])
+
+        def state(i):
+            j0, j1, win, lst, kk = ((0, 80, T.XC[:, 0:8] if last else T.Y[:, y0 - 16:y0 - 8], T.PL[:, 0:5], 0), (80, 176, Y(0, 80), T.PL2[:, 0:6], 5),
+                                    (176, 224, Y(0, 176), T.PL2[:, 6:9], 11), (224, 256, Y(0, 224), T.PL[:, 14:16], 11))[i]
+            op("V", lambda: v.tensor_tensor(Y(j0, j1), win.indirect(lst), T.kn[:, j0:j1], Op.add),
+               r=["PL", "PL2", ("kn", kk), ("Y", i - 1) if i else ("Yr", t)], w=[("Y", i)])
+
+        def thresh(i):
+            for j0, j1 in (((0, 8), (8, 80)), ((80, 88), (88, 176)), ((176, 224),), ((224, 256),))[i]:
+                op("V", lambda: v.tensor_scalar(T.pth[:, j0:j1], Y(j0, j1), 0.5 ** DEP[j0 // 8], T.kp[:, 0:1], Op.mult, Op.subtract),
+                   r=[("Y", i), "kp"], w=[("th", j0)])
+        THK = [[0, 8], [80, 88, 176], [176, 224]]
+
+        def compare(m, k0, k1):
+            j0, j1 = 16 * CH[m][0], 16 * CH[m][1]
+            n = j1 - j0
+            ps = T["ps%d" % (m % 2)]
+            for k in range(k0, k1):
+                bo = 16 * j0 + n * k
+                op("V", lambda: v.tensor_tensor(T.bits[:, bo:bo + n], T.kc[:, 16 * j0 + k:16 * j1:16], T.pth[:, j0:j1], Op.is_ge),
+                   r=[("kc", x) for x in KCK[m]] + [("th", x) for x in THK[m]], w=[("bits", m, k)])
+                op("P", lambda: pe.matmul(ps[:, 0:n], T.Zh[:, 15 - k:143 - k], T.bits[:, bo:bo + n], k == 0, k == 15),
+                   r=[("bits", m, k), "Zh"], w=[("S", m % 2)], b=[ps.name] if k in (0, 15) else [])
+
+        def keys(m, e):
+            j0, j1 = 16 * CH[m][0], 16 * CH[m][1]
+            n = j1 - j0
+            ps = T["ps%d" % (m % 2)]
+            if e == "A":
+                op("A", lambda: a.activation(T.key[:, j0:j1], ps[:, 0:n], Fn.Identity, bias=C(KB), scale=16.0), r=[("S", m % 2)] + CK, w=[("key", m)], b=[ps.name])
+            else:
+                op("V", lambda: v.tensor_scalar(T.key[:, j0:j1], ps[:, 0:n], 16.0, C(KB), Op.mult, Op.add), r=[("S", m % 2)] + CK, w=[("key", m)], b=[ps.name])
+
+        def diffs(m):
+            j0, j1 = 16 * CH[m][0], 16 * CH[m][1]
+            n = j1 - j0
+            for h in range(2):
+                pd = T["p%s%d" % ("ab"[h], m % 2)]
+
+                def mm():
+                    ins = None
+                    for jj in range(4):
+                        j = 1 + 4 * h + jj
+                        ins = pe.matmul(pd[:, n * jj:n * jj + n], T.DM[:, 128 * j:128 * j + 128], T.key[:, j0:j1], True, True)
+                    return ins
+                op("P", mm, r=[("key", m)] + DK, w=[("D", m % 2, h)], b=[pd.name])
+
+        def signs(m, h, e):
+            n = 16 * (CH[m][1] - CH[m][0])
+            pd = T["p%s%d" % ("ab"[h], m % 2)]
+            so = 128 * CH[m][0] + 4 * n * h
+            if e == "A":
+                op("A", lambda: a.activation(T.sg[:, so:so + 4 * n], pd[:, 0:4 * n], Fn.Sign), r=[("D", m % 2, h)], w=[("sg", m, h)], b=[pd.name])
+            else:
+                op("V", lambda: v.tensor_scalar(T.sg[:, so:so + 4 * n], pd[:, 0:4 * n], -1.0, 1.0, Op.max, Op.min), r=[("D", m % 2, h)], w=[("sg", m, h)], b=[pd.name])
+
+        def places(m, h):
+            n = 16 * (CH[m][1] - CH[m][0])
+            so = 128 * CH[m][0] + 4 * n * h
+            ps = T["ps%d" % (m % 2)]
+
+            def mm():
+                ins = None
+                if h == 0:
+                    pe.matmul(ps[:, 128:128 + n], T.Ih[:], T.ch[:, 16 * CH[m][0]:16 * CH[m][1]], True, False)
+                for jj in range(4):
+                    j = 1 + 4 * h + jj
+                    dj = 16 - j if j < 8 else 0
+                    ins = pe.matmul(ps[:, 128:128 + n], T.DM[:, 128 * dj:128 * dj + 128], T.sg[:, so + n * jj:so + n * jj + n], False, j == 8)
+                return ins
+            op("P", mm, r=[("sg", m, h), "ch", "Ih"] + DK, w=[("Rp", m % 2)], b=[ps.name])
+
+        def ranked(m):
+            j0, j1 = 16 * CH[m][0], 16 * CH[m][1]
+            ps = T["ps%d" % (m % 2)]
+            op("V", lambda: v.tensor_scalar(R(j0, j1), ps[:, 128:128 + j1 - j0], C(KR), None, Op.add), r=[("Rp", m % 2)] + CK, w=[("R", m)], b=[ps.name])
+            if m < 2:
+                send(rr, T.AW[:, RL + j0:RL + j1], R(j0, j1), "r%d%d" % (t, m), [("R", m)])
+
+        def tokens(c0, c1):
+            op("A", lambda: a.activation(T.B[:, 16 * c0:16 * c1], T.IO[:].indirect(lm(c0, c1)), Fn.Identity, bias=0.0 if last else C(NK)),
+               r=IOK + CK + [mk(c0), mk(c1 - 1)], w=[("B", c0)])
+
+        def commit(i):
+            if i == -1:
+                src = T.CB[:, 0:48].indirect(T.DL[:, 0:11]) if last else R(0, 80).indirect(T.PL[:, 0:11])
+                op("V", lambda: v.tensor_tensor(T.eq[:, 0:176], src, T.B[:, 0:176], Op.is_equal),
+                   r=[("B", 0), ("B", 5), "PL", "DL"] + ([("CB", d) for d in range(3)] if last else [("R", 0)]), w=["eqa"])
+            if i == 0:
+                src = T.CB[:, 0:80].indirect(T.DL2[:, 0:5]) if last else R(0, 208).indirect(T.PL2[:, 6:11])
+                op("V", lambda: v.tensor_tensor(T.eq[:, 176:256], src, T.B[:, 176:256], Op.is_equal),
+                   r=[("B", 11), "PL2", "DL2"] + ([("CB", d) for d in range(5)] if last else [("R", 0), ("R", 1)]), w=["eq"])
+
+                def mm():
+                    ins = None
+                    for s in range(8):
+                        ins = pe.matmul(T.psl[:, 0:32], T.Z2[:, 7 - s:135 - s], T.eq[:, s:256:8], s == 0, s == 7)
+                    return ins
+                op("P", mm, r=["eq", "eqa", "Z2"], w=["sel"], b=["psl"])
+            if i == 1:
+                jt = T.JD if last else T.JT
+                op("V", lambda: v.tensor_tensor(T.E[:, 0:32], T.psl[:, 0:32], T.RM[:], Op.is_ge), r=["sel", "RM"], w=["E"], b=["psl"])
+                op("V", lambda: v.tensor_tensor(T.E[:, 32:64], T.psl[:, 0:32], jt[:], Op.mult), r=["sel", "JT", "JD"], w=["Ej"], b=["psl"])
+                op("V", lambda: v.tensor_tensor(T.E[:, 64:96], T.psl[:, 0:32], T.RM[:], Op.is_ge), r=["sel", "RM"], w=["E2"], b=["psl"])
+            if i == 2:
+                op("V", lambda: v.tensor_tensor(T.t1[:], T.E[:, 0:32].indirect(T.PP[:, 0:4]), T.E[:, 32:96], Op.mult), r=["E", "Ej", "E2", "PP", "PP0"], w=["t1"])
+            if i == 3:
+                op("V", lambda: v.tensor_tensor(T.t2[:], T.t1[:, 32:64].indirect(T.PP[:, 4:6]), T.t1[:, 0:32], Op.mult), r=["t1", "PP"], w=["t2"])
+            if i == 4:
+                op("V", lambda: v.tensor_reduce(T.bf[:, 0:1], T.t2[:], Ax.X, Op.max), r=["t2"], w=["bf"])
+                if not last:
+                    ranked(2)
+                    op("V", lambda: v.tensor_copy(R(256, 257), T.bf[:, 0:1]), r=["bf"], w=["bs"])
+            if i == 5:
+                op("V", lambda: v.tensor_scalar(T.bq[:, 0:1], T.bf[:, 0:1], C(SC), None, Op.add), r=["bf"] + CK, w=["bq"])
+            if i == 6:
+                op("V", lambda: v.tensor_copy(T.ig[:], T.ISC[:].indirect(T.bq[:, 0:1])), r=["bq"] + IK, w=["ig"])
+            if i == 7:
+                op("V", lambda: v.tensor_tensor(T.X[:, 32 * t:32 * t + 16], Y(0, 256).indirect(T.bq[:, 0:1]), T.ig[:], Op.mult),
+                   r=["bq", "ig", ("Y", 3)], w=["X"])
+
+        def chain(i, st):
+            c, xk = T.cc[:, 2 * i:2 * i + 1], ("XC", i)
+            if st == 0:
+                if i == 0:
+                    op("V", lambda: v.tensor_copy(c, T.XC[:, 8:9]), r=[xk], w=[("cc", 0)])
+                    op("A", lambda: a.activation(T.CB[:, 0:16], T.IO[:].indirect(c), Fn.Copy), r=[("cc", 0)] + IOK, w=[("CB", 0)])
+                else:
+                    op("V", lambda: v.tensor_tensor(T.XC[:, 16 * i:16 * i + 16], T.K[:].indirect(c), T.hx[:], Op.add), r=["K", ("cc", i), "hx"], w=[xk])
+                op("A", lambda: a.activation(T.thx[:], T.XC[:, 16 * i:16 * i + 8].indirect(T.CX[:]), Fn.Identity, bias=C(NKP)),
+                   r=[xk, "CX", "NKP"], w=["thx"])
+                op("V", lambda: v.tensor_copy(T.ccu[:], T.Q[:].indirect(c)), r=QK + [("cc", i)], w=["ccu"])
+                op("P", lambda: pe.matmul(T.ps0[:, 0:128], T.Ib[:], T.TIE[:], True, False), r=["TIE", "Ib"], w=["cA"], b=["ps0"])
+                op("A", lambda: a.activation(T.tkT[:], T.IO[:].indirect(T.ccu[:, 0:8]), Fn.Copy, scale=0.5 ** 12), r=["ccu"] + IOK, w=["tkT"])
+                if i < 4:
+                    op("A", lambda: a.activation(T.hx[:], T.XC[:, 16 * i:16 * i + 16], Fn.Copy, scale=0.5), r=[xk], w=["hx"])
+                if i > 0:
+                    op("A", lambda: a.activation(T.CB[:, 16 * i:16 * i + 16], T.IO[:].indirect(c), Fn.Copy), r=[("cc", i)] + IOK, w=[("CB", i)])
+            if st == 1:
+                op("V", lambda: v.tensor_tensor(T.cb[:], T.K[:].indirect(T.ccu[:, 0:8]), T.thx[:], Op.is_ge), r=["K", "ccu", "thx"], w=["cb"])
+                op("P", lambda: pe.matmul(T.ps0[:, 0:128], T.BO16[:], T.cb[:], False, True), r=["cb", "BO16"], w=["cA"], b=["ps0"])
+            if st == 2:
+                op("V", lambda: v.tensor_tensor(T.cv[:], T.ps0[:, 0:128], T.tkT[:], Op.add), r=["cA", "tkT"], w=["cv"], b=["ps0"])
+                op("V", lambda: v.tensor_reduce(T.cm[:, 0:1], T.ps0[:, 0:128], Ax.X, Op.max), r=["cA"], w=["m2"], b=["ps0"])
+                op("V", lambda: v.tensor_reduce(T.cm[:, 1:2], T.cv[:], Ax.X, Op.max), r=["cv"], w=["m1"])
+            if st == 3:
+                c1 = T.cc[:, 2 * i + 2:2 * i + 3]
+                op("V", lambda: v.tensor_scalar(c1, T.cm[:, 1:2], T.cm[:, 0:1], 4096.0, Op.subtract, Op.mult), r=["m1", "m2"], w=[("cc", i + 1)])
+                if i == 4:
+                    op("A", lambda: a.activation(T.CB[:, 80:96], T.IO[:].indirect(c1), Fn.Copy), r=[("cc", 5)] + IOK, w=[("CB", 5)])
+
+        def unscale(d0, d1):
+            for lo, hi, d in runs(DEP)[d0:d1]:
+                op("A", lambda: a.activation(T.YN[:, 8 * lo:8 * hi], Y(8 * lo, 8 * hi), Fn.Copy, scale=0.5 ** d),
+                   r=[("Y", 1 if d < 3 else d - 1)], w=[("YN", d)])
+
+        if last:
+            wr[("XC", 0)] = wr[("Yr", t)]
+            pick(0)
+            chain(0, 0)
+            chain(0, 1)
+            listed(0)
+            pick(1)
+            chain(0, 2)
+            chain(0, 3)
+            chain(1, 0)
+            listed(1)
+            chain(1, 1)
+            pick(2)
+            chain(1, 2)
+            chain(1, 3)
+            listed(2)
+            chain(2, 0)
+            chain(2, 1)
+            pick(3)
+            tokens(0, 5)
+            tokens(5, 11)
+            chain(2, 2)
+            chain(2, 3)
+            listed(3)
+            chain(3, 0)
+            chain(3, 1)
+            commit(-1)
+            chain(3, 2)
+            chain(3, 3)
+            chain(4, 0)
+            chain(4, 1)
+            numbers(0, 5)
+            numbers(5, 11)
+            tokens(11, 16)
+            chain(4, 2)
+            commit(0)
+            chain(4, 3)
+            state(0)
+            numbers(11, 16)
+            commit(1)
+            state(1)
+            unscale(0, 3)
+            send(rr, T.YL[:, 0:176], T.YN[:, 0:176], "yn0", [("YN", d) for d in range(3)])
+            commit(2)
+            state(2)
+            commit(3)
+            state(3)
+            unscale(3, 5)
+            commit(4)
+            commit(5)
+            op("V", lambda: v.tensor_copy(T.YN[:, 256:272], T.XC[:].indirect(T.bq[:, 0:1])), r=["bq"] + [("XC", d) for d in range(5)], w=["X"])
+            op("V", lambda: v.tensor_copy(T.YN[:, 272:288], T.CB[:, 16:96].indirect(T.bq[:, 0:1])),
+               r=["bq"] + [("CB", d) for d in range(6)], w=["X2"])
+            send(rr, T.YL[:, 176:280], T.YN[:, 176:280], "fin", ["X", "X2", ("YN", 3), ("YN", 4)])
+            break
+
+        numbers(0, 5)
+        repeat(0, 4)
+        state(0)
+        repeat(1, 1)
+        thresh(0)
+        cand(5, 11)
+        repeat(1, 2)
+        gather(80, 160, "A", 5)
+        numbers(5, 11)
+        gather(160, 176, "V", 5)
+        state(1)
+        compare(0, 0, 1)
+        thresh(1)
+        compare(0, 1, 11)
+        cand(11, 16)
+        gather(176, 208, "A", 11)
+        gather(208, 256, "A", 11)
+        numbers(11, 16)
+        compare(0, 11, 12)
+        state(2)
+        compare(0, 12, 13)
+        state(3)
+        thresh(2)
+        compare(0, 13, 14)
+        thresh(3)
+        compare(0, 14, 16)
+        op("V", lambda: v.tensor_scalar(T.ch[:], T.cu[:], -2048.0, None, Op.add), r=CUK, w=["ch"])
+        keys(0, "A")
+        tokens(0, 5)
+        compare(1, 0, 8)
+        diffs(0)
+        signs(0, 0, "A")
+        signs(0, 1, "A")
+        compare(1, 8, 12)
+        places(0, 0)
+        compare(1, 12, 14)
+        places(0, 1)
+        tokens(5, 11)
+        compare(1, 14, 16)
+        keys(1, "A")
+        diffs(1)
+        signs(1, 0, "A")
+        tokens(11, 16)
+        repeat(1, 3)
+        ranked(0)
+        compare(2, 0, 4)
+        commit(-1)
+        signs(1, 1, "V")
+        places(1, 0)
+        places(1, 1)
+        compare(2, 4, 9)
+        ranked(1)
+        compare(2, 9, 10)
+        commit(0)
+        compare(2, 10, 16)
+        keys(2, "A")
+        diffs(2)
+        signs(2, 0, "A")
+        commit(1)
+        commit(2)
+        signs(2, 1, "V")
+        places(2, 0)
+        places(2, 1)
+        RK = [("Rl", m) for m in range(3)]
+        for m in range(3):
+            lands(RK[m], "r%d%d" % (t, m))
+        wr["best"] = wr[RK[2]]
+        commit(3)
+        repeat(1, 4)
+        commit(4)
+        send(rr, T.AW[:, RL + 208:RL + 257], R(208, 257), "r%d2" % t, [("R", 2), "bs"])
+        repeat(2, 0)
+        scatter(0, 1, RK[0])
+        commit(5)
+        scatter(1, 2, RK[0])
+        if t == S - 2:
+            top_of(R(0, 256), [("R", m) for m in range(3)], T.bq[:, 0:1], "bq")
+        commit(6)
+        scatter(2, 3, RK[0])
+        commit(7)
+        if t == S - 2:
+            op("V", lambda: v.tensor_scalar(T.X[:, 32 * t + 8:32 * t + 9], T.psl[:, 0:1], -28672.0, None, Op.add), r=["sel"], w=["X"], b=["psl"])
+            send(verifier(rr, t + 1), T.XC[:, 0:16], T.X[:, 32 * t:32 * t + 16], "x%d" % (t + 1), ["X"])
+        else:
+            send(verifier(rr, t + 1), T.Y[:, 272 * (t + 1):272 * (t + 1) + 8], T.X[:, 32 * t:32 * t + 8], "x%d" % (t + 1), ["X"])
+        lands(("Yr", t + 1), "x%d" % (t + 1))
+        scatter(3, 4, RK[0])
+        repeat(2, 1)
+        scatter(4, 5, RK[0])
+        repeat(2, 2)
+        scatter(5, 7, RK[1])
+        repeat(2, 3)
+        scatter(7, 8, RK[1])
+        repeat(2, 4)
+        scatter(8, 13, RK[1])
+
+    lands("YL0", "yn0")
+    lands("XL", "fin")
+    dma("S", T.yn[:, 0:176], T.YL[:, 0:176], "dout", r=["YL0"])
+    dma("S", T.yn[:, 176:256], T.YL[:, 176:256], "dout", r=["XL"])
+    dma("A", T.yx[:], T.YL[:, 256:264], "dout", r=["XL"])
+    dma("A", T.yt[:, 24:32], T.YL[0:128:16, 272:280], "dout", r=["XL"])
+    for s in sorted(cnt):
+        if max(waited[e].get(s, 0) for e in qu) < cnt[s]:
+            need("S" if s == "dout" else "G", (s, cnt[s]))

@@ -22,7 +22,8 @@ TAKE = [_blocks(LV0, LV1) + [0] + list(range(5)) + [0], list(range(6)) + _blocks
 LOFF = [0, 160, 304, 384]
 CH = [(0, 5), (5, 13), (13, 16)]
 PC = [(0, 5), (5, 11), (11, 16)]
-RL = V + 16
+SG = [(0, 5, 0), (5, 11, 405), (11, 13, 987), (13, 16, 1053)]
+RL = V + 96
 PICK = 30720 + 65536
 QCUT = 2560
 NE = 8
@@ -42,13 +43,13 @@ SCRATCH = {
     "ccu": ("sbuf", [128, 16], "uint16"), "thx": ("sbuf", [128, 128], "float32"),
     "cb": ("sbuf", [128, 128], "float16"), "hx": ("sbuf", [128, 16], "float32"),
     "tkT": ("sbuf", [128, 128], "float32"), "cv": ("sbuf", [128, 128], "float32"), "cm": ("sbuf", [128, 2], "float32"),
-    "TIE": ("sbuf", [128, 128], "bfloat16"),
+    "TIE": ("sbuf", [128, 256], "bfloat16"),
     "DL": ("sbuf", [128, 16], "uint16"), "DL2": ("sbuf", [128, 6], "uint16"), "JD": ("sbuf", [128, 32], "float32"),
     "ch": ("sbuf", [128, 256], "float16"),
     "F": ("sbuf", [128, 1152], "bfloat16"),
     "PL": ("sbuf", [128, 16], "uint16"), "PL2": ("sbuf", [128, 12], "uint16"), "PP": ("sbuf", [128, 6], "uint16"),
     "CX": ("sbuf", [128, 8], "uint16"), "SCL": ("sbuf", [128, 256], "float32"), "ISC": ("sbuf", [128, 256], "float32"),
-    "JT": ("sbuf", [128, 32], "float32"), "RM": ("sbuf", [128, 32], "float32"), "RS0": ("sbuf", [128, 112], "float32"),
+    "DT": ("sbuf", [128, 8], "float32"), "d1": ("sbuf", [128, 18], "float32"), "RS0": ("sbuf", [128, 1200], "float32"),
     "bf": ("sbuf", [128, 4], "float32"), "M": ("sbuf", [128, 16], "float32"),
     "bu": ("sbuf", [128, 2], "uint16"), "w1": ("sbuf", [128, 16], "float16"), "l0": ("sbuf", [128, 16], "uint16"),
     "wf": ("sbuf", [128, 256], "float32"), "wh": ("sbuf", [128, 256], "float16"),
@@ -57,11 +58,12 @@ SCRATCH = {
     "cu": ("sbuf", [128, 256], "uint16"), "kn": ("sbuf", [128, 256], "float32"),
     "kc": ("sbuf", [128, 4096], "bfloat16"), "bits": ("sbuf", [128, 4096], "float16"),
     "key": ("sbuf", [128, 256], "bfloat16"), "sg": ("sbuf", [128, 2048], "bfloat16"),
-    "R": ("sbuf", [128, 3 * 264], "int32"), "B": ("sbuf", [128, 256], "float32"), "eq": ("sbuf", [128, 256], "float16"),
-    "E": ("sbuf", [128, 96], "float32"), "t1": ("sbuf", [128, 64], "float32"), "t2": ("sbuf", [128, 32], "float32"),
+    "R": ("sbuf", [128, 3 * 264], "int32"), "B": ("sbuf", [128, 256], "float32"), "eq": ("sbuf", [128, 256], "bfloat16"),
+    "ok2": ("sbuf", [128, 96], "bfloat16"), "BOb": ("sbuf", [128, 256], "bfloat16"),
+    "CT": ("sbuf", [128, 512], "bfloat16"), "CU": ("sbuf", [128, 1536], "bfloat16"), "tkh": ("sbuf", [128, 128], "float16"),
     "bq": ("sbuf", [128, 4], "uint16"), "ig": ("sbuf", [128, 16], "float32"), "X": ("sbuf", [128, 4 * 32], "float32"),
     "lf": ("sbuf", [128, 24], "float32"), "Bo": ("sbuf", [128, 3 * 96], "float32"),
-    "de": ("sbuf", [128, 3 * 112], "float32"), "ds": ("sbuf", [128, 3 * 112], "float32"),
+    "de": ("sbuf", [128, 1200], "float32"), "ds": ("sbuf", [128, 1200], "float32"),
     "OF": ("sbuf", [128, 32], "uint16"), "yb": ("sbuf", [128, 48], "float32"),
     "YN": ("sbuf", [128, 288], "float32"), "YL": ("sbuf", [128, 288], "float32"),
     "pth": ("psum", [128, 512], "float32"), "psl": ("psum", [128, 512], "float32"),
@@ -194,10 +196,9 @@ def rank_program(g, core, T, topo):
     op("V", lambda: v.tensor_scalar(T.RZ[:], T.IK[:, 0:160], 0.0, None, Op.not_equal), r=["IK"], w=["RZ"])
     op("V", lambda: v.tensor_scalar(T.BO[:], T.IG[:], C(G16), None, Op.is_equal), r=["IG"] + CK, w=["BO"])
     op("V", lambda: v.tensor_scalar(T.BO16[:], T.IG[:], C(G16), 16.0, Op.is_equal, Op.mult), r=["IG"] + CK, w=["BO16"])
-    op("V", lambda: v.tensor_scalar(T.RS0[:], T.IK[:, 0:112], C(KP1), None, Op.not_equal), r=["IK"] + CK, w=["RS0"])
+    op("V", lambda: v.tensor_scalar(T.BOb[:, 0:128], T.IG[:], C(G16), None, Op.is_equal), r=["IG"] + CK, w=["BOb0"])
+    op("V", lambda: v.tensor_scalar(T.BOb[:, 128:256], T.IG[:], C(G16), 16.0, Op.is_equal, Op.mult), r=["IG"] + CK, w=["BOb"])
     op("V", lambda: v.tensor_copy(T.CX[:], T.IO[:, 0:8]), r=["IO0"], w=["CX"])
-    op("V", lambda: v.tensor_scalar(T.RM[:], T.IO[:, 0:32], 0.0, None, Op.not_equal), r=["IO0"], w=["RM"])
-    op("V", lambda: v.tensor_scalar(T.RS0[:, 0:112:16], T.IO[:, 0:7], 0.0, C(DMK), Op.mult, Op.add), r=["RS0", "IO0"] + CK, w=["RS0"])
     rows = [ROW[n] for lv in LEVELS for n in lv]
     op("G", lambda: g.iota(T.F[:, 8:80], [[4096, 9], [0, 8]], 2048, 0, allow_small_or_imprecise_dtypes=True), w=[("F", 0)])
     FK = [("F", 0)]
@@ -219,6 +220,8 @@ def rank_program(g, core, T, topo):
         FK.append(k)
     send(verifier(rank, 0), T.Y[:, 0:8], T.xs[:], "x0", ["xs"])
     lands(("Yr", 0), "x0")
+    op("G", lambda: g.iota(T.CU[:, 0:256], [[0, 32], [1, 8]], 0, 0, allow_small_or_imprecise_dtypes=True), w=["CU0"])
+    op("G", lambda: g.iota(T.CU[:, 256:512], [[1, 32], [0, 8]], 0, 0, allow_small_or_imprecise_dtypes=True), w=["CU1"])
 
     def select():
         ins = None
@@ -245,10 +248,33 @@ def rank_program(g, core, T, topo):
     op("G", lambda: g.affine_select(T.DM[:, 1152:2048], T.DM[:, 1152:2048], [[0, 7], [-1, 128]], Op.not_equal, 2048.0, 0, 1),
        r=[("DM", x) for x in range(9, 16)], w=["DMb"])
     shifts(0, 1)
-    for dst, lo, hi, s2, key in ((T.GL[:, 0:4:2], 36, 38, 0.0, "GL"), (T.PL[:], 0, 16, C(SC), "PL"), (T.PL2[:, 0:11], 5, 16, C(SC), "PL2"), (T.PP[:, 2:6], 16, 20, 0.0, "PP"),
-                                 (T.PP[:, 0:2], 16, 18, 0.0, "PP0"), (T.DL[:], 20, 36, C(SC), "DL"), (T.DL2[:, 0:5], 31, 36, C(SC), "DL2")):
+    for dst, lo, hi, s2, key in ((T.GL[:, 0:4:2], 36, 38, 0.0, "GL"), (T.PL[:], 0, 16, C(SC), "PL"), (T.PL2[:, 0:11], 5, 16, C(SC), "PL2"),
+                                 (T.DL[:], 20, 36, C(SC), "DL"), (T.DL2[:, 0:5], 31, 36, C(SC), "DL2")):
         op("V", lambda: v.tensor_scalar(dst, T.ps1[:, lo:hi], 0.0625, s2, Op.mult, Op.add), r=["tab"] + CK, w=[key], b=["ps1"])
-    op("V", lambda: v.tensor_scalar(T.JD[:], T.F[:, 864:1120:8], 0.0625, None, Op.mult), r=FK, w=["JD"])
+    def table(i):
+        c = lambda x: T.CU[:, 256 * x:256 * x + 256]
+        if i == 0:
+            op("V", lambda: v.tensor_scalar(c(2), c(0), C(SC), -128.0, Op.not_equal, Op.mult), r=["CU0"] + CK, w=["CU2"])
+            op("V", lambda: v.tensor_scalar(c(3), T.F[:, 864:1120], 0.0625, None, Op.mult), r=FK, w=["CU3"])
+            op("V", lambda: v.tensor_scalar(c(4), c(1), 0.5, None, Op.mult), r=["CU1"], w=["CU4"])
+            for lo, hi, d in runs(DEP)[1:]:
+                op("V", lambda: v.tensor_scalar(T.CU[:, 512 + 8 * lo:512 + 8 * hi], T.CU[:, 512 + 8 * lo:512 + 8 * hi], -16.0 * d, None, Op.add), r=["CU2"], w=[("CU2", d)])
+        if i == 1:
+            op("V", lambda: v.tensor_tensor(T.CT[:, 256:512], c(3), c(2), Op.add), r=["CU3"] + [("CU2", d) for d in (1, 2, 3, 4)], w=["CT2"])
+        if i == 2:
+            op("V", lambda: v.tensor_tensor(T.CT[:, 0:256], c(4), c(2), Op.add), r=["CU4", "CT2"], w=["CT"])
+    RSK = []
+    for c0, c1, d0 in SG:
+        w = 16 * (c1 - c0) + 1
+        for x in range(c1 - c0):
+            op("V", lambda: v.tensor_scalar(T.RS0[:, d0 + x * w:d0 + x * w + w - 1], T.IO[:, 0:w - 1], -16.0 * x, C(KP1), Op.add, Op.not_equal),
+               r=["IO0"] + CK, w=[("RS", c0 + x)])
+        op("V", lambda: v.memset(T.RS0[:, d0 + w - 1:d0 + (c1 - c0 - 1) * w:w], 4096.0), w=[("RS1", c0)])
+        op("V", lambda: v.tensor_copy(T.RS0[:, d0 + (c1 - c0) * w - 1:d0 + (c1 - c0) * w], C(DMK)), r=CK, w=[("RS2", c0)])
+        RSK += [("RS", c) for c in range(c0, c1)] + [("RS1", c0), ("RS2", c0)]
+    op("V", lambda: v.tensor_scalar(T.DT[:], T.IO[:, 0:8], 16.0, C(DUM), Op.mult, Op.add), r=["IO0"] + CK, w=["DT"])
+    op("A", lambda: a.activation(T.de[:, 0:256], T.IO[:, 0:256], Fn.Copy, scale=0.0), r=["IO0"], w=["de0a"])
+    op("V", lambda: v.memset(T.de[:, 256:1200], 0.0), r=["de0a"], w=["de0"])
     wr["best"] = wr["Rl2"]
     RK = ["Rl", "Rl2"]
     for i, n in enumerate((256, 512, 1024, 2048)):
@@ -260,7 +286,6 @@ def rank_program(g, core, T, topo):
         op("A", lambda: a.activation(T.SCL[:, 8 * lo:8 * hi], T.IO[:, 8 * lo:8 * hi], Fn.Identity, bias=float(2 ** d if d else 0), scale=0.0), r=["IO0"], w=[("SCL", d)])
         op("A", lambda: a.activation(T.ISC[:, 8 * lo:8 * hi], T.IO[:, 8 * lo:8 * hi], Fn.Identity, bias=0.5 ** d, scale=0.0), r=["IO0"], w=[("ISC", d)])
     SK, IK = [("SCL", d) for d in range(5)], [("ISC", d) for d in range(5)]
-    op("A", lambda: a.activation(T.JT[:], T.IO[:, 0:32], Fn.Identity, scale=8.0), r=["IO0"], w=["JT"])
     DK = [("DM", 0), "DMa", "DMb"]
 
 
@@ -271,7 +296,8 @@ def rank_program(g, core, T, topo):
             op("A", lambda: a.activation(T.TM[:, 128:256], T.IK[:, 0:128], Fn.Identity, bias=15.0, scale=-1.0), r=["IK"], w=["TM1"])
         if i == 1:
             op("A", lambda: a.activation(T.TM[:, 0:128], T.TM[:, 0:128], Fn.Copy, scale=-512.0), r=["TM0"], w=["TM0"])
-            op("V", lambda: v.tensor_tensor(T.TIE[:], T.TM[:, 0:128], T.TM[:, 128:256], Op.add), r=["TM0", "TM1"], w=["TIE"])
+            op("V", lambda: v.tensor_tensor(T.TIE[:, 0:128], T.TM[:, 0:128], T.TM[:, 128:256], Op.add), r=["TM0", "TM1"], w=["TIE0"])
+            op("A", lambda: a.activation(T.TIE[:, 128:256], T.TIE[:, 0:128], Fn.Identity, bias=0.5), r=["TIE0"], w=["TIE"])
 
     def top_of(win, keys, lst, lkey):
         op("V", lambda: v.tensor_scalar(T.w1[:], win.indirect(lst), C(KT), 2048.0, Op.add, Op.min), r=keys + [lkey] + CK, w=["w1"])
@@ -284,9 +310,8 @@ def rank_program(g, core, T, topo):
         op("P", mm, r=["w1", "Z2"], w=["sel"], b=["psl"])
 
     def scatter(c0, c1, key):
-        for c in range(c0, c1):
-            op("V", lambda: v.tensor_copy(T.AW[:, 0:RL].indirect(T.OF[:, 2 * c:2 * c + 1]), T.AW[:, RL + 16 * c:RL + 16 * c + 16]),
-               r=[key, ("OF", 0 if c < 5 else 1 if c < 11 else 2), "spare"], w=["A"])
+        op("V", lambda: v.tensor_copy(T.AW[:, 0:RL].indirect(T.OF[:, c0 + (c0 > 0):c1 + (c0 > 0)]), T.AW[:, RL + 16 * c0:RL + 16 * c1]),
+           r=[key, ("OF", 0 if c0 < 5 else 1 if c0 < 11 else 2), "spare"], w=["A"])
 
     for t in range(S):
         q, rr = verifier(rank, t), drafter(rank, t)
@@ -305,34 +330,45 @@ def rank_program(g, core, T, topo):
             if last:
                 return
             nc = PC[p][1] - PC[p][0]
-            lf, d0 = T.lf[:, 8 * p:8 * p + nc], 112 * p
+            grp = [x for x in SG if PC[p][0] <= x[0] < PC[p][1]]
+            rel = lambda c: c - PC[p][0]
             if i == 0:
                 lst, x = mine[p], nc
                 for lo, hi, c0 in (((0, 80, 0),), ((160, 256, 0),), ((336, 384, 0), (384, 416, 3)))[p]:
                     op("A", lambda: a.activation(T.lf[:, 8 * p + c0:8 * p + c0 + (hi - lo) // 16], T.sc[:, lo + 15:hi:16], Fn.Identity, bias=-float(PICK)),
                        r=mineK[p], w=[("lf", p)])
                 op("A", lambda: a.activation(T.Bo[:, 96 * p:96 * p + 16 * x], T.IO[:].indirect(lst), Fn.Copy), r=mineK[p] + IOK, w=[("Bo", p)])
+                for c0, c1, d0 in grp:
+                    w = 16 * (c1 - c0) + 1
+                    op("A", lambda: a.activation(T.de[:, d0 + w - 1:d0 + (c1 - c0) * w:w], T.lf[:, 8 * p + rel(c0):8 * p + rel(c1)], Fn.Copy),
+                       r=[("lf", p), "de0"], w=[("dz", c0)])
             if i == 1:
-                bo = 96 * p
-                op("V", lambda: v.tensor_tensor(T.de[:, d0:d0 + 16 * nc], lf.indirect(T.CX[:, 0:nc]), T.Bo[:, bo:bo + 16 * nc], Op.is_equal),
-                   r=[("lf", p), ("Bo", p), "CX", "RS0"], w=[("de", p)])
+                for c0, c1, d0 in grp:
+                    w = 16 * (c1 - c0) + 1
+                    for c in range(c0, c1):
+                        lo = d0 + (c - c0) * w
+                        op("V", lambda: v.tensor_scalar(T.de[:, lo + 16 * (c - c0):lo + w - 1], T.Bo[:, 96 * p + 16 * rel(c):96 * p + 16 * rel(c1)],
+                                                        T.lf[:, 8 * p + rel(c):8 * p + rel(c) + 1], None, Op.is_equal),
+                           r=[("lf", p), ("Bo", p), "de0"], w=[("de", c)])
             if i == 2:
-                op("A", lambda: a.activation(T.de[:, d0 + 16:d0 + 16 * nc + 1:16], lf, Fn.Copy), r=[("lf", p), ("de", p)], w=[("de", p)])
+                lo, hi = grp[0][2], grp[-1][2] + (grp[-1][1] - grp[-1][0]) * (16 * (grp[-1][1] - grp[-1][0]) + 1)
+                op("V", lambda: v.tensor_tensor_scan(T.ds[:, lo:hi], T.RS0[:, lo:hi], T.de[:, lo:hi], 0.0, Op.mult, Op.add),
+                   r=[("de", c) for c in range(*PC[p])] + [("dz", x[0]) for x in grp] + RSK, w=[("ds", p)])
             if i == 3:
-                op("V", lambda: v.tensor_tensor_scan(T.ds[:, d0 + 1:d0 + 16 * nc + 1], T.RS0[:, 1:16 * nc + 1], T.de[:, d0 + 1:d0 + 16 * nc + 1],
-                                                     0.0, Op.mult, Op.add), r=[("de", p), "RS0"], w=[("ds", p)])
+                for c0, c1, d0 in grp:
+                    w = 16 * (c1 - c0) + 1
+                    op("V", lambda: v.tensor_tensor(T.d1[:, c0 + (c0 > 0):c1 + (c0 > 0)], T.ds[:, d0 + w - 1:d0 + (c1 - c0) * w:w], T.DT[:, 0:c1 - c0], Op.min),
+                       r=[("ds", p), "DT"], w=[("d1", c0)])
             if i == 4:
-                op("V", lambda: v.tensor_scalar(T.OF[:, 2 * PC[p][0]:2 * PC[p][1]:2], T.ds[:, d0 + 16:d0 + 16 * nc + 1:16], C(DUM), None, Op.min),
-                   r=[("ds", p)] + CK, w=[("OF", p)])
+                lo, hi = PC[p][0] + (p > 0), PC[p][1] + (p > 0)
+                op("V", lambda: v.tensor_copy(T.OF[:, lo:hi], T.d1[:, lo:hi]), r=[("d1", x[0]) for x in grp], w=[("OF", p)])
         def root():
             bcol = T.AW[:, RL + 256:RL + 257]
             op("V", lambda: v.tensor_scalar(T.bu[:, 0:1], bcol, C(SC), None, Op.add), r=["best"] + CK, w=["bu"])
             if t > 0:
-                scatter(13, 14, RK[2])
+                scatter(13, 16, RK[2])
             top_of(T.AW[:, RL:RL + 256], RK, T.bu[:, 0:1], "bu")
             op("V", lambda: v.tensor_scalar(T.M[:, 0:1], bcol, C(K2), C(BC), Op.add, Op.mult), r=["best", "M"] + CK, w=["M0"])
-            if t > 0:
-                scatter(14, 16, RK[2])
             op("V", lambda: v.tensor_scalar(T.l0[:], T.M[:], T.psl[:, 0:1], 28672.0, Op.max, Op.subtract), r=["M0", "sel"], w=[("L", 0)], b=["psl"])
             if t > 0:
                 op("A", lambda: a.activation(T.yb[:, 16 * t - 16:16 * t], T.IO[:].indirect(T.l0[:, 2:3]), Fn.Copy), r=[("L", 0)] + IOK, w=[("yb", t)])
@@ -384,15 +420,20 @@ def rank_program(g, core, T, topo):
             pick(0)
             if t > 0:
                 late(t - 1)
+            else:
+                table(0)
             listed(0)
             repeat(0, 0)
             pick(1)
             repeat(0, 1)
-            repeat(0, 2)
+            if t == 0:
+                table(1)
             listed(1)
             repeat(1, 0)
             pick(2)
-            repeat(0, 3)
+            repeat(0, 2)
+            if t == 0:
+                table(2)
             listed(2)
             pick(3)
             cand(0, 5)
@@ -488,38 +529,42 @@ def rank_program(g, core, T, topo):
             op("A", lambda: a.activation(T.B[:, 16 * c0:16 * c1], T.IO[:].indirect(lm(c0, c1)), Fn.Identity, bias=0.0 if last else C(NK)),
                r=IOK + CK + [mk(c0), mk(c1 - 1)], w=[("B", c0)])
 
+        def paths(early):
+            bo = T.BOb[:, 0:128] if last else T.BOb[:, 128:256]
+            ins = None
+            if early:
+                pe.matmul(T.psl[:, 0:256], T.Ib[:], T.CT[:, 256:512] if last else T.CT[:, 0:256], True, False)
+                pe.matmul(T.psl[:, 8:88], bo, T.eq[:, 8:88], False, False)
+                pe.matmul(T.psl[:, 88:176], bo, T.ok2[:, 8:96], False, False)
+                for n in range(22, 32):
+                    anc = (PAR[n] if DEP[n] == 3 else PAR[PAR[n]]) - 10
+                    ins = pe.matmul(T.psl[:, 8 * n:8 * n + 8], bo, T.ok2[:, 8 * anc:8 * anc + 8], False, False)
+            else:
+                pe.matmul(T.psl[:, 176:256], bo, T.eq[:, 176:256], False, False)
+                for n in range(28, 32):
+                    ins = pe.matmul(T.psl[:, 8 * n:8 * n + 8], bo, T.eq[:, 8 * PAR[n]:8 * PAR[n] + 8], False, n == 31)
+            return ins
+
         def commit(i):
             if i == -1:
                 src = T.CB[:, 0:48].indirect(T.DL[:, 0:11]) if last else R(0, 80).indirect(T.PL[:, 0:11])
                 op("V", lambda: v.tensor_tensor(T.eq[:, 0:176], src, T.B[:, 0:176], Op.is_equal),
                    r=[("B", 0), ("B", 5), "PL", "DL"] + ([("CB", d) for d in range(3)] if last else [("R", 0)]), w=["eqa"])
+            if i == -2:
+                op("V", lambda: v.tensor_tensor(T.ok2[:], T.eq[:, 0:80].indirect(T.PL2[:, 0:6]), T.eq[:, 80:176], Op.add), r=["eqa", "PL2"], w=["ok2"])
+            if i == -3:
+                op("P", lambda: paths(True), r=["eqa", "ok2", "BOb", "Ib", "CT"], w=["sel"], b=["psl"])
             if i == 0:
                 src = T.CB[:, 0:80].indirect(T.DL2[:, 0:5]) if last else R(0, 208).indirect(T.PL2[:, 6:11])
                 op("V", lambda: v.tensor_tensor(T.eq[:, 176:256], src, T.B[:, 176:256], Op.is_equal),
                    r=[("B", 11), "PL2", "DL2"] + ([("CB", d) for d in range(5)] if last else [("R", 0), ("R", 1)]), w=["eq"])
-
-                def mm():
-                    ins = None
-                    for s in range(8):
-                        ins = pe.matmul(T.psl[:, 0:32], T.Z2[:, 7 - s:135 - s], T.eq[:, s:256:8], s == 0, s == 7)
-                    return ins
-                op("P", mm, r=["eq", "eqa", "Z2"], w=["sel"], b=["psl"])
-            if i == 1:
-                jt = T.JD if last else T.JT
-                op("V", lambda: v.tensor_tensor(T.E[:, 0:32], T.psl[:, 0:32], T.RM[:], Op.is_ge), r=["sel", "RM"], w=["E"], b=["psl"])
-                op("V", lambda: v.tensor_tensor(T.E[:, 32:64], T.psl[:, 0:32], jt[:], Op.mult), r=["sel", "JT", "JD"], w=["Ej"], b=["psl"])
-                op("V", lambda: v.tensor_tensor(T.E[:, 64:96], T.psl[:, 0:32], T.RM[:], Op.is_ge), r=["sel", "RM"], w=["E2"], b=["psl"])
-            if i == 2:
-                op("V", lambda: v.tensor_tensor(T.t1[:], T.E[:, 0:32].indirect(T.PP[:, 0:4]), T.E[:, 32:96], Op.mult), r=["E", "Ej", "E2", "PP", "PP0"], w=["t1"])
-            if i == 3:
-                op("V", lambda: v.tensor_tensor(T.t2[:], T.t1[:, 32:64].indirect(T.PP[:, 4:6]), T.t1[:, 0:32], Op.mult), r=["t1", "PP"], w=["t2"])
+                op("P", lambda: paths(False), r=["eq"], w=["sel"], b=["psl"])
             if i == 4:
-                op("V", lambda: v.tensor_reduce(T.bf[:, 0:1], T.t2[:], Ax.X, Op.max), r=["t2"], w=["bf"])
-                if not last:
-                    ranked(2)
-                    op("V", lambda: v.tensor_copy(R(256, 257), T.bf[:, 0:1]), r=["bf"], w=["bs"])
+                op("V", lambda: v.tensor_reduce(T.bf[:, 0:1], T.psl[:, 0:256], Ax.X, Op.max), r=["sel"], w=["bf"], b=["psl"])
+            if i == 41:
+                op("V", lambda: v.tensor_scalar(R(256, 257), T.bf[:, 0:1], 16.0, None, Op.mult), r=["bf"], w=["bs"])
             if i == 5:
-                op("V", lambda: v.tensor_scalar(T.bq[:, 0:1], T.bf[:, 0:1], C(SC), None, Op.add), r=["bf"] + CK, w=["bq"])
+                op("V", lambda: v.tensor_scalar(T.bq[:, 0:1], T.bf[:, 0:1], 16.0, C(SC), Op.mult, Op.add), r=["bf"] + CK, w=["bq"])
             if i == 6:
                 op("V", lambda: v.tensor_copy(T.ig[:], T.ISC[:].indirect(T.bq[:, 0:1])), r=["bq"] + IK, w=["ig"])
             if i == 7:
@@ -537,8 +582,10 @@ def rank_program(g, core, T, topo):
                 op("A", lambda: a.activation(T.thx[:], T.XC[:, 16 * i:16 * i + 8].indirect(T.CX[:]), Fn.Identity, bias=C(NKP)),
                    r=[xk, "CX", "NKP"], w=["thx"])
                 op("V", lambda: v.tensor_copy(T.ccu[:], T.Q[:].indirect(c)), r=QK + [("cc", i)], w=["ccu"])
-                op("P", lambda: pe.matmul(T.ps0[:, 0:128], T.Ib[:], T.TIE[:], True, False), r=["TIE", "Ib"], w=["cA"], b=["ps0"])
-                op("A", lambda: a.activation(T.tkT[:], T.IO[:].indirect(T.ccu[:, 0:8]), Fn.Copy, scale=0.5 ** 12), r=["ccu"] + IOK, w=["tkT"])
+                op("P", lambda: pe.matmul(T.ps0[:, 0:128], T.Ib[:], T.TIE[:, 0:128], True, False), r=["TIE", "Ib"], w=["cA"], b=["ps0"])
+                op("P", lambda: pe.matmul(T.ps1[:, 0:128], T.Ib[:], T.TIE[:, 128:256], True, False), r=["TIE", "Ib"], w=["cB"], b=["ps1"])
+                op("V", lambda: v.tensor_scalar(T.tkh[:], T.IO[:].indirect(T.ccu[:, 0:8]), -2048.0, 0.5 ** 12, Op.add, Op.mult), r=["ccu"] + IOK, w=["tkh"])
+                op("P", lambda: pe.matmul(T.ps1[:, 0:128], T.Ih[:], T.tkh[:], False, False), r=["tkh", "Ih"], w=["cB"], b=["ps1"])
                 if i < 4:
                     op("A", lambda: a.activation(T.hx[:], T.XC[:, 16 * i:16 * i + 16], Fn.Copy, scale=0.5), r=[xk], w=["hx"])
                 if i > 0:
@@ -546,10 +593,10 @@ def rank_program(g, core, T, topo):
             if st == 1:
                 op("V", lambda: v.tensor_tensor(T.cb[:], T.K[:].indirect(T.ccu[:, 0:8]), T.thx[:], Op.is_ge), r=["K", "ccu", "thx"], w=["cb"])
                 op("P", lambda: pe.matmul(T.ps0[:, 0:128], T.BO16[:], T.cb[:], False, True), r=["cb", "BO16"], w=["cA"], b=["ps0"])
+                op("P", lambda: pe.matmul(T.ps1[:, 0:128], T.BO16[:], T.cb[:], False, True), r=["cb", "BO16"], w=["cB"], b=["ps1"])
             if st == 2:
-                op("V", lambda: v.tensor_tensor(T.cv[:], T.ps0[:, 0:128], T.tkT[:], Op.add), r=["cA", "tkT"], w=["cv"], b=["ps0"])
                 op("V", lambda: v.tensor_reduce(T.cm[:, 0:1], T.ps0[:, 0:128], Ax.X, Op.max), r=["cA"], w=["m2"], b=["ps0"])
-                op("V", lambda: v.tensor_reduce(T.cm[:, 1:2], T.cv[:], Ax.X, Op.max), r=["cv"], w=["m1"])
+                op("V", lambda: v.tensor_reduce(T.cm[:, 1:2], T.ps1[:, 0:128], Ax.X, Op.max), r=["cB"], w=["m1"], b=["ps1"])
             if st == 3:
                 c1 = T.cc[:, 2 * i + 2:2 * i + 3]
                 op("V", lambda: v.tensor_scalar(c1, T.cm[:, 1:2], T.cm[:, 0:1], 4096.0, Op.subtract, Op.mult), r=["m1", "m2"], w=[("cc", i + 1)])
@@ -586,30 +633,29 @@ def rank_program(g, core, T, topo):
             chain(2, 3)
             listed(3)
             chain(3, 0)
+            numbers(0, 5)
             chain(3, 1)
             commit(-1)
-            chain(3, 2)
-            chain(3, 3)
-            chain(4, 0)
-            chain(4, 1)
-            numbers(0, 5)
-            numbers(5, 11)
-            tokens(11, 16)
-            chain(4, 2)
-            commit(0)
-            chain(4, 3)
             state(0)
-            numbers(11, 16)
-            commit(1)
+            commit(-2)
+            commit(-3)
+            chain(3, 2)
+            numbers(5, 11)
+            chain(3, 3)
             state(1)
+            chain(4, 0)
+            tokens(11, 16)
             unscale(0, 3)
             send(rr, T.YL[:, 0:176], T.YN[:, 0:176], "yn0", [("YN", d) for d in range(3)])
-            commit(2)
+            numbers(11, 16)
+            chain(4, 1)
+            commit(0)
             state(2)
-            commit(3)
+            chain(4, 2)
             state(3)
             unscale(3, 5)
             commit(4)
+            chain(4, 3)
             commit(5)
             op("V", lambda: v.tensor_copy(T.YN[:, 256:272], T.XC[:].indirect(T.bq[:, 0:1])), r=["bq"] + [("XC", d) for d in range(5)], w=["X"])
             op("V", lambda: v.tensor_copy(T.YN[:, 272:288], T.CB[:, 16:96].indirect(T.bq[:, 0:1])),
@@ -618,12 +664,11 @@ def rank_program(g, core, T, topo):
             break
 
         numbers(0, 5)
-        repeat(0, 4)
+        repeat(0, 3)
         state(0)
-        repeat(1, 1)
+        repeat(0, 4)
         thresh(0)
         cand(5, 11)
-        repeat(1, 2)
         gather(80, 160, "A", 5)
         numbers(5, 11)
         gather(160, 176, "V", 5)
@@ -644,58 +689,55 @@ def rank_program(g, core, T, topo):
         thresh(3)
         compare(0, 14, 16)
         op("V", lambda: v.tensor_scalar(T.ch[:], T.cu[:], -2048.0, None, Op.add), r=CUK, w=["ch"])
-        keys(0, "A")
-        tokens(0, 5)
-        compare(1, 0, 8)
+        keys(0, "V")
         diffs(0)
-        signs(0, 0, "A")
-        signs(0, 1, "A")
-        compare(1, 8, 12)
-        places(0, 0)
-        compare(1, 12, 14)
-        places(0, 1)
+        tokens(0, 5)
         tokens(5, 11)
-        compare(1, 14, 16)
+        compare(1, 0, 3)
+        signs(0, 0, "V")
+        signs(0, 1, "A")
+        compare(1, 3, 5)
+        places(0, 0)
+        places(0, 1)
+        repeat(2, 0)
+        tokens(11, 16)
+        compare(1, 5, 10)
+        ranked(0)
+        compare(1, 10, 16)
         keys(1, "A")
         diffs(1)
         signs(1, 0, "A")
-        tokens(11, 16)
-        repeat(1, 3)
-        ranked(0)
-        compare(2, 0, 4)
-        commit(-1)
-        signs(1, 1, "V")
-        places(1, 0)
-        places(1, 1)
-        compare(2, 4, 9)
-        ranked(1)
-        compare(2, 9, 10)
-        commit(0)
-        compare(2, 10, 16)
-        keys(2, "A")
-        diffs(2)
-        signs(2, 0, "A")
-        commit(1)
-        commit(2)
-        signs(2, 1, "V")
-        places(2, 0)
-        places(2, 1)
         RK = [("Rl", m) for m in range(3)]
         for m in range(3):
             lands(RK[m], "r%d%d" % (t, m))
         wr["best"] = wr[RK[2]]
-        commit(3)
-        repeat(1, 4)
+        compare(2, 0, 16)
+        commit(-1)
+        keys(2, "A")
+        signs(1, 1, "V")
+        places(1, 0)
+        places(1, 1)
+        diffs(2)
+        signs(2, 0, "A")
+        signs(2, 1, "A")
+        commit(-2)
+        commit(-3)
+        repeat(1, 1)
+        ranked(1)
+        places(2, 0)
+        places(2, 1)
+        commit(0)
+        repeat(2, 1)
+        ranked(2)
         commit(4)
+        commit(41)
         send(rr, T.AW[:, RL + 208:RL + 257], R(208, 257), "r%d2" % t, [("R", 2), "bs"])
-        repeat(2, 0)
-        scatter(0, 1, RK[0])
         commit(5)
-        scatter(1, 2, RK[0])
+        repeat(2, 2)
         if t == S - 2:
             top_of(R(0, 256), [("R", m) for m in range(3)], T.bq[:, 0:1], "bq")
         commit(6)
-        scatter(2, 3, RK[0])
+        scatter(0, 5, RK[0])
         commit(7)
         if t == S - 2:
             op("V", lambda: v.tensor_scalar(T.X[:, 32 * t + 8:32 * t + 9], T.psl[:, 0:1], -28672.0, None, Op.add), r=["sel"], w=["X"], b=["psl"])
@@ -703,15 +745,13 @@ def rank_program(g, core, T, topo):
         else:
             send(verifier(rr, t + 1), T.Y[:, 272 * (t + 1):272 * (t + 1) + 8], T.X[:, 32 * t:32 * t + 8], "x%d" % (t + 1), ["X"])
         lands(("Yr", t + 1), "x%d" % (t + 1))
-        scatter(3, 4, RK[0])
-        repeat(2, 1)
-        scatter(4, 5, RK[0])
-        repeat(2, 2)
-        scatter(5, 7, RK[1])
+        repeat(1, 2)
         repeat(2, 3)
-        scatter(7, 8, RK[1])
+        repeat(1, 3)
         repeat(2, 4)
-        scatter(8, 13, RK[1])
+        repeat(1, 4)
+        scatter(5, 11, RK[1])
+        scatter(11, 13, RK[1])
 
     lands("YL0", "yn0")
     lands("XL", "fin")

@@ -3,13 +3,17 @@ from concourse.mybir import AluOpType as Op, AxisListType as Ax, ActivationFunct
 V, S = 3840, 4
 PAR = [0, 0, 0, 0, 0, 0, 0, 0, 0, 0, 0, 1, 1, 1, 1, 2, 2, 2, 3, 3, 4, 4, 11, 11, 11, 15, 15, 18, 22, 22, 23, 25]
 ROW = [0, 0, 1, 2, 3, 4, 5, 6, 7, 8, 9, 0, 10, 11, 1, 0, 12, 13, 0, 14, 0, 15, 0, 1, 2, 0, 3, 0, 0, 5, 0, 0]
+SWAP = (14, 24, 30)
+NODE = [n ^ 1 if n - n % 2 in SWAP else n for n in range(32)]
+PAR, ROW = [NODE.index(PAR[n]) for n in NODE], [ROW[n] for n in NODE]
 DEP = [0]
 for _n in range(1, 32):
     DEP.append(DEP[PAR[_n]] + 1)
+ANC = [(PAR[n] if DEP[n] == 3 else PAR[PAR[n]]) - 10 for n in range(22, 32)]
 LV3 = [28, 29, 30, 31]
 LV2 = [PAR[n] for n in LV3] + list(range(22, 28))
-LV1 = list(range(10, 22)) + [11, 11, 11, 15, 15, 18]
-LV0 = list(range(0, 10)) + [1, 1, 1, 2, 2, 2, 3, 3, 4, 4]
+LV1 = list(range(10, 22)) + [PAR[n] for n in range(22, 28)]
+LV0 = list(range(0, 10)) + [1, 1, 2, 1, 2, 2, 3, 3, 4, 4]
 LEVELS = [LV0, LV1, LV2, LV3]
 
 
@@ -19,52 +23,54 @@ def _blocks(lv, nxt):
 
 
 TAKE = [_blocks(LV0, LV1) + [0] + list(range(5)) + [0], list(range(6)) + _blocks(LV1, LV2) + [0] * 5]
-LOFF = [0, 160, 304, 384]
-CH = [(0, 5), (5, 13), (13, 16)]
+LOFF = [0, 160, 304, 384, 416]
+FP, FD, FA, FT, FE = 416, 672, 928, 1008, 1040
 PC = [(0, 5), (5, 11), (11, 16)]
-SG = [(0, 5, 0), (5, 11, 405), (11, 13, 987), (13, 16, 1053)]
-RL = V + 96
-PICK = 30720 + 65536
+OWN = [(0, 5, 0), (5, 11, 160), (11, 14, 336), (14, 16, 384)]
+POS = [(0, 96), (96, 200), (200, 256)]
+DD = [(0, 4, 160), (4, 10, 304), (10, 16, 416)]
+RL = V + 32
+TOP = 28672
 QCUT = 2560
 NE = 8
 
 SCRATCH = {
-    "Q": ("sbuf", [128, V], "int32"), "K": ("sbuf", [128, V], "bfloat16"), "AW": ("sbuf", [128, RL + 264], "int32"),
+    "Q": ("sbuf", [128, V], "int32"), "K": ("sbuf", [128, V], "bfloat16"), "AW": ("sbuf", [128, RL + 256], "int32"),
     "IO": ("sbuf", [128, V], "float32"), "IOb": ("sbuf", [128, 144], "bfloat16"),
     "xs": ("sbuf", [128, 8], "float32"), "IK": ("sbuf", [128, 256], "bfloat16"), "IG": ("sbuf", [128, 128], "bfloat16"),
+    "IJ": ("sbuf", [128, 256], "bfloat16"), "IS": ("sbuf", [128, 256], "bfloat16"),
     "BO": ("sbuf", [128, 128], "float16"), "BO16": ("sbuf", [128, 128], "float16"), "Ib": ("sbuf", [128, 128], "bfloat16"),
-    "D1": ("sbuf", [128, 256], "bfloat16"), "CKa": ("sbuf", [128, 416], "bfloat16"), "F2": ("sbuf", [128, 416], "bfloat16"),
-    "RZ": ("sbuf", [128, 160], "bfloat16"), "sc": ("sbuf", [128, 416], "float32"), "GL": ("sbuf", [128, 4], "uint16"), "TM": ("sbuf", [128, 256], "bfloat16"),
+    "I16": ("sbuf", [128, 256], "bfloat16"), "GT": ("sbuf", [128, 256], "bfloat16"), "one": ("sbuf", [128, 2], "float16"),
+    "D1": ("sbuf", [128, 176], "bfloat16"), "F2": ("sbuf", [128, FP], "bfloat16"), "GM": ("sbuf", [128, 8], "float32"),
+    "RZ": ("sbuf", [128, 256], "bfloat16"), "sc": ("sbuf", [128, FP], "float32"), "GL": ("sbuf", [128, 4], "uint16"),
+    "AL": ("sbuf", [128, 6], "uint16"), "ok3": ("sbuf", [128, 80], "bfloat16"),
+    "TM": ("sbuf", [128, 256], "bfloat16"), "LX": ("sbuf", [128, 16], "uint16"),
     "kp": ("sbuf", [128, 4], "float32"), "pi": ("sbuf", [128, 32], "int32"), "pj": ("sbuf", [128, 32], "int32"),
-    "C": ("sbuf", [128, 16], "float32"), "CJ": ("sbuf", [128, 16], "float32"),
-    "Zb": ("sbuf", [128, 144], "bfloat16"), "Zh": ("sbuf", [128, 144], "float16"), "Z2": ("sbuf", [128, 136], "float16"),
+    "C": ("sbuf", [128, 20], "float32"), "CJ": ("sbuf", [128, 16], "float32"),
+    "Zb": ("sbuf", [128, 144], "bfloat16"), "Zh": ("sbuf", [128, 144], "float16"),
     "Ih": ("sbuf", [128, 128], "float16"), "DM": ("sbuf", [128, 2048], "bfloat16"),
     "XC": ("sbuf", [128, 80], "float32"), "CB": ("sbuf", [128, 96], "float32"), "cc": ("sbuf", [128, 12], "uint16"),
     "ccu": ("sbuf", [128, 16], "uint16"), "thx": ("sbuf", [128, 128], "float32"),
-    "cb": ("sbuf", [128, 128], "float16"), "hx": ("sbuf", [128, 16], "float32"),
-    "tkT": ("sbuf", [128, 128], "float32"), "cv": ("sbuf", [128, 128], "float32"), "cm": ("sbuf", [128, 2], "float32"),
+    "cb": ("sbuf", [128, 128], "float16"), "hx": ("sbuf", [128, 16], "float32"), "cm": ("sbuf", [128, 2], "float32"),
     "TIE": ("sbuf", [128, 256], "bfloat16"),
-    "DL": ("sbuf", [128, 16], "uint16"), "DL2": ("sbuf", [128, 6], "uint16"), "JD": ("sbuf", [128, 32], "float32"),
-    "ch": ("sbuf", [128, 256], "float16"),
-    "F": ("sbuf", [128, 1152], "bfloat16"),
-    "PL": ("sbuf", [128, 16], "uint16"), "PL2": ("sbuf", [128, 12], "uint16"), "PP": ("sbuf", [128, 6], "uint16"),
-    "CX": ("sbuf", [128, 8], "uint16"), "SCL": ("sbuf", [128, 256], "float32"), "ISC": ("sbuf", [128, 256], "float32"),
-    "DT": ("sbuf", [128, 8], "float32"), "d1": ("sbuf", [128, 18], "float32"), "RS0": ("sbuf", [128, 1200], "float32"),
-    "bf": ("sbuf", [128, 4], "float32"), "M": ("sbuf", [128, 16], "float32"),
-    "bu": ("sbuf", [128, 2], "uint16"), "w1": ("sbuf", [128, 16], "float16"), "l0": ("sbuf", [128, 16], "uint16"),
-    "wf": ("sbuf", [128, 256], "float32"), "wh": ("sbuf", [128, 256], "float16"),
+    "DL": ("sbuf", [128, 16], "uint16"), "DL2": ("sbuf", [128, 6], "uint16"),
+    "ch": ("sbuf", [128, 256], "float16"), "F": ("sbuf", [128, FE], "bfloat16"),
+    "PL": ("sbuf", [128, 16], "uint16"), "PL2": ("sbuf", [128, 12], "uint16"),
+    "CX": ("sbuf", [128, 8], "uint16"), "SCL": ("sbuf", [128, 256], "float32"), "ISC": ("sbuf", [128, 264], "float32"),
+    "bf": ("sbuf", [128, 4], "float32"), "M": ("sbuf", [128, 16], "float32"), "bl": ("sbuf", [128, 8], "uint16"),
+    "w1": ("sbuf", [128, 128], "float16"), "l0": ("sbuf", [128, 64], "uint16"), "ls": ("sbuf", [128, 48], "uint16"),
+    "wf": ("sbuf", [128, 176], "float32"), "wh": ("sbuf", [128, 176], "float16"),
     "O0": ("sbuf", [128, 64], "uint16"), "O1": ("sbuf", [128, 64], "uint16"), "O2": ("sbuf", [128, 32], "uint16"),
-    "LM": ("sbuf", [128, 96], "uint16"), "Y": ("sbuf", [128, 4 * 272], "float32"),
+    "LM": ("sbuf", [128, 96], "uint16"), "Y": ("sbuf", [128, 4 * 264], "float32"),
     "cu": ("sbuf", [128, 256], "uint16"), "kn": ("sbuf", [128, 256], "float32"),
     "kc": ("sbuf", [128, 4096], "bfloat16"), "bits": ("sbuf", [128, 4096], "float16"),
     "key": ("sbuf", [128, 256], "bfloat16"), "sg": ("sbuf", [128, 2048], "bfloat16"),
     "R": ("sbuf", [128, 3 * 264], "int32"), "B": ("sbuf", [128, 256], "float32"), "eq": ("sbuf", [128, 256], "bfloat16"),
     "ok2": ("sbuf", [128, 96], "bfloat16"), "BOb": ("sbuf", [128, 256], "bfloat16"),
-    "CT": ("sbuf", [128, 512], "bfloat16"), "CU": ("sbuf", [128, 1536], "bfloat16"), "tkh": ("sbuf", [128, 128], "float16"),
-    "bq": ("sbuf", [128, 4], "uint16"), "ig": ("sbuf", [128, 16], "float32"), "X": ("sbuf", [128, 4 * 32], "float32"),
-    "lf": ("sbuf", [128, 24], "float32"), "Bo": ("sbuf", [128, 3 * 96], "float32"),
-    "de": ("sbuf", [128, 1200], "float32"), "ds": ("sbuf", [128, 1200], "float32"),
-    "OF": ("sbuf", [128, 32], "uint16"), "yb": ("sbuf", [128, 48], "float32"),
+    "CT": ("sbuf", [128, 768], "bfloat16"), "tkh": ("sbuf", [128, 128], "float16"),
+    "bq": ("sbuf", [128, 4], "uint16"), "ig": ("sbuf", [128, 16], "float32"), "X": ("sbuf", [128, 3 * 16], "float32"),
+    "Bo": ("sbuf", [128, 256], "float16"), "ed": ("sbuf", [128, 512], "bfloat16"), "ds": ("sbuf", [128, 256], "float32"),
+    "OF": ("sbuf", [128, 16], "uint16"), "yb": ("sbuf", [128, 48], "float32"),
     "YN": ("sbuf", [128, 288], "float32"), "YL": ("sbuf", [128, 288], "float32"),
     "pth": ("psum", [128, 512], "float32"), "psl": ("psum", [128, 512], "float32"),
     "ps0": ("psum", [128, 512], "float32"), "ps1": ("psum", [128, 512], "float32"),
@@ -73,7 +79,7 @@ SCRATCH = {
 }
 SEMAPHORES = (["sv", "sa", "sp", "sq", "sent", "dtok", "dx", "dkap", "dk", "dout", "yn0", "fin", "dq0", "dq1", "dq2", "sent0"]
               + ["m%d%d" % (t, i) for t in range(S) for i in range(3)] + ["r%d%d" % (t, i) for t in range(3) for i in range(3)]
-              + ["x%d" % t for t in range(S)])
+              + ["x%d" % t for t in range(S)] + ["l%d" % t for t in range(1, S)])
 
 
 def runs(vals):
@@ -83,6 +89,111 @@ def runs(vals):
             out.append((a, i, vals[a]))
             a = i
     return out
+
+
+def ramps(vals):
+    out, a = [], 0
+    while a < len(vals):
+        b, d = a + 1, (vals[a + 1] - vals[a] if a + 1 < len(vals) else 0)
+        while b < len(vals) and vals[b] - vals[b - 1] == d:
+            b += 1
+        out.append((a, b, vals[a], d))
+        a = b
+    return out
+
+
+CYCLE, WAKE, ISSUE, FLIGHT, PER_BYTE = 0.00091, 0.1, 0.35, 1.35, 0.0013
+TURNS = 2
+ITEM = {"float32": 4, "int32": 4, "bfloat16": 2, "float16": 2, "uint16": 2}
+
+
+def size(ap):
+    return ap.shape[-1]
+
+
+def cost(name, fn, args, kw):
+    if name == "matmul":
+        return max(64, size(args[2])) * CYCLE
+    if name == "iota":
+        return 0.15 + 2 * size(args[0]) * CYCLE
+    if isinstance(args[0], tuple):
+        return 0.05 + 3.8 * size(args[1]) * CYCLE
+    if isinstance(args[1], tuple):
+        return (0.065 if name == "act" else 0.05) + 1.56 * size(args[0]) * CYCLE
+    sides = [SCRATCH[x.name] for x in args[:3 if name in ("pair", "scan") else 2] if not isinstance(x, (int, float))]
+    rate = 1.0
+    if name == "pair" and all(x[0] == "sbuf" for x in sides[1:]):
+        rate = 2.0
+    if name in ("copy", "scan") and all(ITEM[x[2]] == 2 for x in sides):
+        rate = 0.5
+    return (0.06 if name == "act" else 0.03) + max(64, rate * size(args[1 if name == "reduce" else 0])) * CYCLE
+
+
+def arrange(nodes):
+    wr, rd, bank, far = {}, {}, {}, {nd["far"]: i for i, nd in enumerate(nodes) if "far" in nd}
+    deps, kids, turns = [], [[] for nd in nodes], []
+    for i, nd in enumerate(nodes):
+        d = {wr[k] for k in nd["r"]} | {bank[k] for k in nd["b"] if k in bank}
+        for k in nd["w"]:
+            d |= set(rd.get(k, [])) | ({wr[k]} if k in wr else set())
+        if nd["e"] == "L":
+            d.add(far[nd["sem"]])
+        if nd.get("turn"):
+            d |= set(turns[-1:])
+            turns.append(i)
+        d.discard(i)
+        deps.append(d)
+        for j in d:
+            kids[j].append(i)
+        for k in nd["r"]:
+            rd.setdefault(k, []).append(i)
+        for k in nd["w"]:
+            wr[k], rd[k] = i, []
+        for k in nd["b"]:
+            bank[k] = i
+
+    def gap(j, i):
+        if j in turns and i in turns:
+            return 0.0
+        return nodes[j]["lag"] + (0.0 if nodes[i]["e"] == "L" or nodes[i]["e"] == nodes[j]["e"] == "P" else WAKE)
+    chain, depth, left, todo = {}, {}, [len(k) for k in kids], [i for i, k in enumerate(kids) if not k]
+    while todo:
+        i = todo.pop()
+        depth[i] = -len(depth)
+        chain[i] = nodes[i]["busy"] + max([gap(i, k) + chain[k] for k in kids[i]] + [nodes[i]["lag"]])
+        for j in deps[i]:
+            left[j] -= 1
+            if not left[j]:
+                todo.append(j)
+
+    def place(before, after, wait, first, rank):
+        end, taken, left = {}, {}, [len(d) for d in before]
+        ready = [i for i, d in enumerate(before) if not d]
+        while ready:
+            c = max(ready, key=lambda i: (rank[i], -i))
+            ready.remove(c)
+            t, need = max([end[j] + wait(j, c) for j in before[c]] + [first(c)]), nodes[c]["busy"]
+            line = taken.setdefault(nodes[c]["e"], [])
+            at = 0
+            for at, (lo, hi) in enumerate(line + [(1e9, 1e9)]):
+                if t + need <= lo + 1e-9:
+                    break
+                t = max(t, hi)
+            line.insert(at, (t, t + need))
+            end[c] = t + need
+            for k in after[c]:
+                left[k] -= 1
+                if not left[k]:
+                    ready.append(k)
+        return end
+    best, chain = None, {i: -i for i in chain}
+    for turn in range(TURNS):
+        end = place(deps, kids, gap, lambda i: 0.0, chain)
+        total = max(end[i] + nodes[i]["lag"] for i in end)
+        if best is None or total < best[0]:
+            best = (total, end)
+        chain = place(kids, deps, lambda j, i: gap(i, j), lambda i: nodes[i]["lag"], end)
+    return [nodes[i] for i in sorted(best[1], key=lambda i: (round(best[1][i] - nodes[i]["busy"], 6), depth[i]))]
 
 
 def rank_program(g, core, T, topo):
@@ -104,7 +215,7 @@ def rank_program(g, core, T, topo):
     def order(e, r, w, b):
         own = semof.get(e)
         best = {}
-        toks = [wr.get(k) for k in r]
+        toks = [wr[k] for k in r]
         for k in w:
             toks += [t for t in [wr.get(k)] + rd.get(k, []) if t is not None and (e != "P" or t[0] != own)]
         toks += [bank[k] for k in b if k in bank and bank[k][0] != own]
@@ -123,35 +234,78 @@ def rank_program(g, core, T, topo):
         for k in b:
             bank[k] = tok
 
-    def op(e, fn, r=(), w=(), b=()):
+    def emit(nd):
+        e, r, w, b, sem = nd["e"], nd["r"], nd["w"], nd["b"], nd["sem"]
+        if e == "L":
+            note((sem, NE), (), w, ())
+            cnt[sem] = NE
+            return
         order(e, r, w, b)
-        s = semof[e]
-        cnt[s] = cnt.get(s, 0) + 1
-        fn().then_inc(T.sem[s], 1)
-        note((s, cnt[s]), r, w, b)
+        ins = None
+        for name, fn, args, kw in nd["calls"]:
+            ins = fn(*[x[0] if isinstance(x, tuple) else x for x in args], **kw)
+        step = NE if name == "remote_dma" else 16 if name == "dma_start" else 1
+        cnt[sem] = cnt.get(sem, 0) + step
+        if name == "remote_dma":
+            note((sem, cnt[sem]), (), w, ())
+        else:
+            ins.then_inc(T.sem[sem], step)
+            note((sem, cnt[sem]), r, w, b)
 
-    def dma(e, out, in_, sem, r=(), w=()):
-        order(e, r, w, ())
-        cnt[sem] = cnt.get(sem, 0) + 16
-        qu[e].dma_start(out, in_).then_inc(T.sem[sem], 16)
-        note((sem, cnt[sem]), r, w, ())
+    nodes, said = [], []
 
-    def send(to, out, in_, sem, r, local="sent"):
-        order("G", r, (), ())
+    def noted(name, fn):
+        return lambda *args, **kw: said.append((name, fn, args, kw))
+
+    class v:
+        memset, tensor_copy = noted("copy", g.vector.memset), noted("copy", g.vector.tensor_copy)
+        tensor_scalar, tensor_tensor = noted("copy", g.vector.tensor_scalar), noted("pair", g.vector.tensor_tensor)
+        tensor_reduce, tensor_tensor_scan = noted("reduce", g.vector.tensor_reduce), noted("scan", g.vector.tensor_tensor_scan)
+
+    class a:
+        activation = noted("act", g.scalar.activation)
+
+    class pe:
+        matmul = noted("matmul", g.tensor.matmul)
+
+    class gp:
+        iota, affine_select = noted("iota", g.iota), noted("iota", g.affine_select)
+
+    def ind(win, lst):
+        return (win.indirect(lst),)
+
+    def op(e, fn, r=(), w=(), b=()):
+        fn()
+        nodes.append(dict(e=e, calls=said[:], r=r, w=w, b=b, sem=semof[e], busy=sum(cost(*c) for c in said), lag=0.0))
+        del said[:]
+
+    def dma(e, out, in_, sem, r=(), w=(), lag=1.4, turn=0):
+        nodes.append(dict(e=e, turn=turn, calls=[("dma_start", qu[e].dma_start, (out, in_), {})], r=r, w=w, b=(), sem=sem, busy=0.05, lag=lag))
+
+    def send(to, out, in_, sem, r, local="sent", w=()):
         dst = T.cores[to]
         rid, pid = topo.addr(dst)[:2]
         mask = sum(1 << e for e in topo.engines(core, dst)[:NE])
-        g.remote_dma(out, in_, T.sem[sem], T.sem[local], pid, rid, mask)
-        cnt[local] = cnt.get(local, 0) + NE
+        nodes.append(dict(e="G", calls=[("remote_dma", g.remote_dma, (out, in_, T.sem[sem], T.sem[local], pid, rid, mask), {})],
+                          r=r, w=w, b=(), sem=local, far=sem, busy=ISSUE, lag=FLIGHT + size(in_) * ITEM[SCRATCH[in_.name][2]] * PER_BYTE))
 
     def lands(key, sem):
-        wr[key] = (sem, NE)
-        rd[key] = []
-        cnt[sem] = NE
+        nodes.append(dict(e="L", calls=[], r=(), w=[key], b=(), sem=sem, busy=0.0, lag=0.0))
 
-    v, a, pe = g.vector, g.scalar, g.tensor
     C = lambda i: T.C[:, i:i + 1]
-    KF, G16, SC, NB, NK, KB, Z15, PF, KP1, DMK, DUM, BC, NKP, KT, KR, K2 = range(16)
+    KF, G16, SC, NB, NK, KB, Z15, PF, GI, ZC, SP0, BC, NKP, KT, KR, SP1, KX = range(17)
+
+    def lin(e, out, in_, mul, add, r, w, b=()):
+        if e == "A":
+            op("A", lambda: a.activation(out, in_, Fn.Identity, bias=add, scale=mul), r=r, w=w, b=b)
+        else:
+            op("V", lambda: v.tensor_scalar(out, in_, mul, add, Op.mult, Op.add), r=r, w=w, b=b)
+
+    def cmp(out, in_, col, mul, how, r, w):
+        op("V", lambda: v.tensor_scalar(out, in_, col, mul, how, Op.mult), r=r, w=w)
+
+    def iota(out, pattern, key):
+        op("G", lambda: gp.iota(out, pattern, 0, 0, allow_small_or_imprecise_dtypes=True), w=[key])
 
     def verifier(r, t):
         return (r + 1 + t % (n_ranks - 1)) % n_ranks
@@ -160,165 +314,159 @@ def rank_program(g, core, T, topo):
         return (q - 1 - t % (n_ranks - 1)) % n_ranks
 
     op("V", lambda: v.memset(T.AW[:, RL:RL + 8], 0), w=["Rl"])
-    op("V", lambda: v.memset(T.AW[:, RL + 8:RL + 264], 0), w=["Rl2"])
-    op("V", lambda: v.memset(T.AW[:, V:RL], 0), w=["spare"])
     dma("A", T.xs[:], T.x0[:], "dx", w=["xs"])
-    dma("S", T.AW[:, 0:QCUT], T.qt[:, 0:QCUT], "dq0", w=["A0"])
-    dma("A", T.AW[0:128:16, RL:RL + 8], T.tok[:], "dtok", w=["Rl"])
+    dma("S", T.AW[0:128:16, RL:RL + 8], T.tok[:], "dtok", w=["Rl"], turn=1)
+    dma("S", T.AW[:, 0:QCUT], T.qt[:, 0:QCUT], "dq0", w=["A0"], lag=5.2, turn=1)
     dma("A", T.kp[:, 0:1], T.kap[:], "dkap", w=["kp"])
-    dma("S", T.AW[:, QCUT:V], T.qt[:, QCUT:V], "dq1", w=["A"])
-    dma("S", T.K[:], T.kt[:], "dk", r=["A0"], w=["K"])
+    dma("S", T.AW[:, QCUT:V], T.qt[:, QCUT:V], "dq1", w=["A"], lag=7.1, turn=1)
+    dma("S", T.K[:], T.kt[:], "dk", r=["A0"], w=["K"], lag=4.6)
 
-    op("G", lambda: g.iota(T.pi[:, 0:1], [[0, 1]], 0, 1), w=["pi"])
-    op("G", lambda: g.iota(T.IO[:, 0:256], [[1, 256]], 0, 0, allow_small_or_imprecise_dtypes=True), w=["IO0"])
-    op("G", lambda: g.iota(T.pi[:, 16:32], [[-1, 16]], 16, 1), w=["pi2"])
-    op("G", lambda: g.iota(T.IK[:], [[0, 16], [1, 16]], 0, 0, allow_small_or_imprecise_dtypes=True), w=["IK"])
-    op("G", lambda: g.iota(T.IG[:], [[16, 8], [0, 16]], 0, 0, allow_small_or_imprecise_dtypes=True), w=["IG"])
+    op("G", lambda: gp.iota(T.pi[:, 0:1], [[0, 1]], 0, 1), w=["pi"])
+    iota(T.IO[:, 0:256], [[1, 256]], "IO0")
+    op("G", lambda: gp.iota(T.pi[:, 16:32], [[-1, 16]], 16, 1), w=["pi2"])
+    iota(T.IJ[:], [[1, 32], [0, 8]], "IJ")
+    iota(T.IK[:], [[0, 16], [1, 16]], "IK")
+    iota(T.IG[:], [[16, 8], [0, 16]], "IG")
     op("V", lambda: v.memset(T.M[:], 0.0), w=["M"])
+    op("V", lambda: v.memset(T.bf[:], 0.5), w=["bf"])
     for col, m in ((0, 15), (1, 112), (2, 7), (3, 8)):
         op("V", lambda: v.tensor_scalar(T.pj[:, col:col + 1], T.pi[:, 0:1], m, None, Op.bitwise_and), r=["pi"], w=[("pj", col)])
     op("V", lambda: v.tensor_copy(C(PF), T.pi[:, 0:1]), r=["pi"], w=["C1"])
     op("V", lambda: v.tensor_copy(T.C[:, 0:4], T.pj[:, 0:4]), r=[("pj", i) for i in range(4)], w=["C0"])
-    for col, src, s1, s2, f0, f1 in ((Z15, G16, 15.0, 0.0, Op.add, Op.add), (NK, KF, -4096.0, 0.0, Op.mult, Op.add),
-                                     (KB, KF, -1.0, -121.0, Op.mult, Op.add), (KP1, KF, 1.0, 0.0, Op.add, Op.add),
-                                     (DMK, KF, 15.0, 4096.0, Op.is_lt, Op.mult), (DUM, KF, float(V), 0.0, Op.add, Op.add),
-                                     (BC, NB, 0.0, 1.0, Op.is_equal, Op.mult), (KT, KF, 4096.0, -2048.0, Op.mult, Op.add),
-                                     (KR, KF, -4096.0, 32768.0, Op.mult, Op.add), (K2, SC, float(RL + 28672), 0.0, Op.add, Op.add)):
-        op("V", lambda: v.tensor_scalar(C(col), C(src), s1, s2, f0, f1), r=["C0"], w=[("C", col)])
-    CK = ["C0", "C1"] + [("C", c) for c in (NK, KB, Z15, KP1, DMK, DUM, BC, KT, KR, K2)]
+    op("V", lambda: v.tensor_scalar(T.pj[:, 16:32], T.pi[:, 16:32], 15, None, Op.bitwise_and), r=["pi2"], w=["pj2"])
     op("V", lambda: v.tensor_copy(T.IOb[:], T.IO[:, 0:144]), r=["IO0"], w=["IOb"])
-    op("V", lambda: v.tensor_scalar(T.Zb[:], T.IOb[:], C(Z15), None, Op.is_equal), r=["IOb"] + CK, w=["Zb"])
-    op("V", lambda: v.tensor_scalar(T.Zh[:], T.IOb[:], C(Z15), None, Op.is_equal), r=["IOb"] + CK, w=["Zh"])
-    op("V", lambda: v.tensor_scalar(T.Ih[:], T.IOb[:, 0:128], C(PF), None, Op.is_equal), r=["IOb"] + CK, w=["Ih"])
-    op("V", lambda: v.tensor_scalar(T.Ib[:], T.IOb[:, 0:128], C(PF), None, Op.is_equal), r=["IOb"] + CK, w=["Ib"])
-    op("V", lambda: v.tensor_tensor(T.Z2[:], T.Zh[:, 0:136], T.Zh[:, 8:144], Op.add), r=["Zh"], w=["Z2"])
-    op("V", lambda: v.tensor_scalar(T.D1[:], T.IK[:], C(KF), 65536.0, Op.is_equal, Op.mult), r=["IK"] + CK, w=["D1"])
-    op("V", lambda: v.tensor_scalar(T.RZ[:], T.IK[:, 0:160], 0.0, None, Op.not_equal), r=["IK"], w=["RZ"])
-    op("V", lambda: v.tensor_scalar(T.BO[:], T.IG[:], C(G16), None, Op.is_equal), r=["IG"] + CK, w=["BO"])
-    op("V", lambda: v.tensor_scalar(T.BO16[:], T.IG[:], C(G16), 16.0, Op.is_equal, Op.mult), r=["IG"] + CK, w=["BO16"])
-    op("V", lambda: v.tensor_scalar(T.BOb[:, 0:128], T.IG[:], C(G16), None, Op.is_equal), r=["IG"] + CK, w=["BOb0"])
-    op("V", lambda: v.tensor_scalar(T.BOb[:, 128:256], T.IG[:], C(G16), 16.0, Op.is_equal, Op.mult), r=["IG"] + CK, w=["BOb"])
-    op("V", lambda: v.tensor_copy(T.CX[:], T.IO[:, 0:8]), r=["IO0"], w=["CX"])
-    rows = [ROW[n] for lv in LEVELS for n in lv]
-    op("G", lambda: g.iota(T.F[:, 8:80], [[4096, 9], [0, 8]], 2048, 0, allow_small_or_imprecise_dtypes=True), w=[("F", 0)])
-    FK = [("F", 0)]
-    take = TAKE[0] + TAKE[1]
-    for lo, hi, d in runs([b - i for i, b in enumerate(take)]):
-        k = ("F", len(FK))
-        op("G", lambda: g.iota(T.F[:, 1120 + lo:1120 + hi], [[16, hi - lo]], 16 * take[lo] + 15, 0, allow_small_or_imprecise_dtypes=True), w=[k])
-        FK.append(k)
-    todo = [(0, 8, 2048)] + [(8 * (10 + lo), 8 * (10 + hi), 4096 * r + 2048) for lo, hi, r in runs(rows[10:])]
-    todo += [(544 + 8 * lo, 544 + 8 * hi, 8 * p) for lo, hi, p in runs(PAR)]
-    todo += [(832 + lo, 832 + hi, p) for lo, hi, p in runs([PAR[p] for p in PAR])]
-    todo += [(864 + 8 * lo, 864 + 8 * hi, 16 * d) for lo, hi, d in runs(DEP)]
-    for i, (lo, hi, val) in enumerate(todo):
-        k = ("F", len(FK))
-        if i % 4 == 0:
-            op("V", lambda: v.memset(T.F[:, lo:hi], float(val)), w=[k])
-        else:
-            op("A", lambda: a.activation(T.F[:, lo:hi], T.IO[:, 0:hi - lo], Fn.Identity, bias=float(val), scale=0.0), r=["IO0"], w=[k])
-        FK.append(k)
+    op("V", lambda: v.tensor_scalar(T.CJ[:], T.pj[:, 16:32], C(G16), None, Op.add), r=["pj2", "C0"], w=["CJ"])
+    for col, src, mul, add in ((Z15, G16, 1.0, 15.0), (KT, KF, 4096.0, -2048.0), (ZC, KF, -4096.0, 2048.0), (GI, G16, 0.0625, 0.0),
+                               (BC, NB, -0.125, 1.0), (KR, KF, -4096.0, 32768.0), (NK, KF, -4096.0, 0.0), (KB, KF, -1.0, -121.0),
+                               (SP0, KF, 1.0, float(V)), (SP1, KF, 1.0, float(V + 16))):
+        lin("A", C(col), C(src), mul, add, ["C0"], [("C", col)])
+    CK = ["C0", "C1"] + [("C", c) for c in (Z15, KT, ZC, GI, BC, KR, NK, KB, SP0, SP1)]
+
+    def shifts(j0, j1):
+        for j in range(j0, j1):
+            cmp(T.DM[:, 128 * j:128 * j + 128], T.IOb[:, 0:128], T.CJ[:, j:j + 1], 2048.0 if j <= 8 else -2048.0, Op.is_equal, ["IOb", "CJ"], [("DM", j)])
+    shifts(1, 9)
     send(verifier(rank, 0), T.Y[:, 0:8], T.xs[:], "x0", ["xs"])
     lands(("Yr", 0), "x0")
-    op("G", lambda: g.iota(T.CU[:, 0:256], [[0, 32], [1, 8]], 0, 0, allow_small_or_imprecise_dtypes=True), w=["CU0"])
-    op("G", lambda: g.iota(T.CU[:, 256:512], [[1, 32], [0, 8]], 0, 0, allow_small_or_imprecise_dtypes=True), w=["CU1"])
+    op("G", lambda: gp.affine_select(T.DM[:, 128:1152], T.DM[:, 128:1152], [[0, 8], [-1, 128]], Op.not_equal, -2048.0, 0, 1),
+       r=[("DM", x) for x in range(1, 9)], w=["DMa"])
+    shifts(9, 16)
+    op("G", lambda: gp.affine_select(T.DM[:, 1152:2048], T.DM[:, 1152:2048], [[0, 7], [-1, 128]], Op.not_equal, 2048.0, 0, 1),
+       r=[("DM", x) for x in range(9, 16)], w=["DMb"])
+    shifts(0, 1)
+    DK = [("DM", 0), "DMa", "DMb"]
+    rows = [ROW[n] for lv in LEVELS for n in lv]
+    todo = [(FP + 8 * lo, FP + 8 * hi, T.IJ, 8 * p, 8 * d) for lo, hi, p, d in ramps(PAR)]
+    todo += [(FD + 8 * lo, FD + 8 * hi, T.IJ, 16 * p, 0) for lo, hi, p in runs(DEP)]
+    todo += [(FA + 8 * lo, FA + 8 * hi, T.IJ, 8 * p, 8 * d) for lo, hi, p, d in ramps(ANC)]
+    todo += [(FT + lo, FT + hi, T.IOb, 16 * p + 15, 16 * d) for lo, hi, p, d in ramps(TAKE[0] + TAKE[1])]
+    nsel = len(todo)
+    todo += [(8 * lo, 8 * hi, T.IJ, 4096 * p - 30720, 4096 * d) for lo, hi, p, d in ramps(rows)]
+    FK = []
+    for i, (lo, hi, src, val, d) in enumerate(todo):
+        FK.append(("F", i))
+        lin("V" if i % 3 == 2 else "A", T.F[:, lo:hi], src[:, 0:hi - lo], float(d), float(val), ["IJ", "IOb"], [FK[-1]])
+    cmp(T.Zb[:], T.IOb[:], C(Z15), 1.0, Op.is_equal, ["IOb"] + CK, ["Zb"])
 
     def select():
         ins = None
         for i in range(16):
-            ins = pe.matmul(T.ps1[:, 0:38], T.Zb[:, 15 - i:143 - i], T.F[:, 544 + i:1152:16], i == 0, i == 15)
+            ins = pe.matmul(T.ps1[:, 0:39], T.Zb[:, 15 - i:143 - i], T.F[:, FP + i:FE:16], i == 0, i == 15)
         return ins
-    op("V", lambda: v.tensor_scalar(T.pj[:, 16:32], T.pi[:, 16:32], 15, None, Op.bitwise_and), r=["pi2"], w=["pj2"])
-    op("V", lambda: v.tensor_scalar(T.CJ[:], T.pj[:, 16:32], C(G16), None, Op.add), r=["pj2", "C0"], w=["CJ"])
+    op("P", select, r=FK[:nsel] + ["Zb"], w=["tab"], b=["ps1"])
+    cmp(T.GM[:], T.IO[:, 0:8], C(GI), 16.0, Op.is_equal, ["IO0"] + CK, ["GM"])
+    lin("V", T.one[:], T.IO[:, 0:2], 0.0, 1.0, ["IO0"], ["one"])
+    lin("V", T.AW[:, V:RL], T.IO[:, 0:32], 0.0, C(ZC), ["IO0"] + CK, ["spare"])
+    cmp(T.Ib[:], T.IOb[:, 0:128], C(PF), 1.0, Op.is_equal, ["IOb"] + CK, ["Ib"])
+    cmp(T.D1[:], T.IK[:, 0:176], C(KF), -65536.0, Op.not_equal, ["IK"] + CK, ["D1"])
+    cmp(T.RZ[:], T.IK[:], 0.0, -1048576.0, Op.is_equal, ["IK"], ["RZ"])
+    cmp(T.BO[:], T.IG[:], C(G16), 1.0, Op.is_equal, ["IG"] + CK, ["BO"])
+    lin("A", T.F2[:], T.F[:, 0:FP], 1.0, C(KR), FK + CK, ["F2"])
+    PB = [T.pa1, T.pb1, T.pa0, T.pb0]
 
-    def shifts(j0, j1):
-        for j in range(j0, j1):
-            op("V", lambda: v.tensor_scalar(T.DM[:, 128 * j:128 * j + 128], T.IOb[:, 0:128], T.CJ[:, j:j + 1],
-                                            2048.0 if j <= 8 else -2048.0, Op.is_equal, Op.mult), r=["IOb", "CJ"], w=[("DM", j)])
-    shifts(1, 9)
-    op("G", lambda: g.affine_select(T.DM[:, 128:1152], T.DM[:, 128:1152], [[0, 8], [-1, 128]], Op.not_equal, -2048.0, 0, 1),
-       r=[("DM", x) for x in range(1, 9)], w=["DMa"])
-    op("V", lambda: v.tensor_scalar(T.F[:, 800:832], T.F[:, 544:800:8], 0.125, None, Op.mult), r=FK, w=["Fp"])
-    op("P", select, r=FK + ["Fp", "Zb"], w=["tab"], b=["ps1"])
-    op("V", lambda: v.tensor_scalar(T.F2[:], T.F[:, 0:416], C(NK), None, Op.add), r=FK + CK, w=["F2"])
-    for lo, hi in ((0, 256), (256, 416)):
-        op("V", lambda: v.tensor_tensor(T.CKa[:, lo:hi], T.F[:, lo:hi], T.D1[:, 0:hi - lo], Op.min), r=FK + ["D1"], w=[("CKa", lo)])
-    CKK = [("CKa", lo) for lo in (0, 256)]
-    shifts(9, 16)
-    op("G", lambda: g.affine_select(T.DM[:, 1152:2048], T.DM[:, 1152:2048], [[0, 7], [-1, 128]], Op.not_equal, 2048.0, 0, 1),
-       r=[("DM", x) for x in range(9, 16)], w=["DMb"])
-    shifts(0, 1)
-    for dst, lo, hi, s2, key in ((T.GL[:, 0:4:2], 36, 38, 0.0, "GL"), (T.PL[:], 0, 16, C(SC), "PL"), (T.PL2[:, 0:11], 5, 16, C(SC), "PL2"),
-                                 (T.DL[:], 20, 36, C(SC), "DL"), (T.DL2[:, 0:5], 31, 36, C(SC), "DL2")):
-        op("V", lambda: v.tensor_scalar(dst, T.ps1[:, lo:hi], 0.0625, s2, Op.mult, Op.add), r=["tab"] + CK, w=[key], b=["ps1"])
-    def table(i):
-        c = lambda x: T.CU[:, 256 * x:256 * x + 256]
+    def prepare(lv):
+        n, lo = 8 * len(LEVELS[lv]), LOFF[lv]
+
+        def mm():
+            pe.matmul(PB[lv][:, 0:n], T.Ib[:], T.F[:, lo:lo + n], True, False)
+            return pe.matmul(PB[lv][:, 0:n], T.Ib[:], T.D1[:, 0:n], False, False)
+        op("P", mm, r=["Ib", "D1"] + FK, w=[PB[lv].name], b=[PB[lv].name])
+
+    def best_lists():
+        lin("V", T.bl[:], T.GM[:], T.bf[:, 0:1], C(SC), ["bf", "GM"] + CK, ["bl"])
+        lin("V", T.bq[:, 0:1], T.bf[:, 0:1], 16.0, C(SC), ["bf"] + CK, ["bq"])
+
+    def root_mark():
+        op("V", lambda: v.tensor_scalar(T.M[:, 0:1], T.bq[:, 0:1], float(RL - 8 + TOP), C(BC), Op.add, Op.mult), r=["bq", "M"] + CK, w=["M0"])
+
+    def root(i, win, keys, out, okey):
         if i == 0:
-            op("V", lambda: v.tensor_scalar(c(2), c(0), C(SC), -128.0, Op.not_equal, Op.mult), r=["CU0"] + CK, w=["CU2"])
-            op("V", lambda: v.tensor_scalar(c(3), T.F[:, 864:1120], 0.0625, None, Op.mult), r=FK, w=["CU3"])
-            op("V", lambda: v.tensor_scalar(c(4), c(1), 0.5, None, Op.mult), r=["CU1"], w=["CU4"])
-            for lo, hi, d in runs(DEP)[1:]:
-                op("V", lambda: v.tensor_scalar(T.CU[:, 512 + 8 * lo:512 + 8 * hi], T.CU[:, 512 + 8 * lo:512 + 8 * hi], -16.0 * d, None, Op.add), r=["CU2"], w=[("CU2", d)])
-        if i == 1:
-            op("V", lambda: v.tensor_tensor(T.CT[:, 256:512], c(3), c(2), Op.add), r=["CU3"] + [("CU2", d) for d in (1, 2, 3, 4)], w=["CT2"])
-        if i == 2:
-            op("V", lambda: v.tensor_tensor(T.CT[:, 0:256], c(4), c(2), Op.add), r=["CU4", "CT2"], w=["CT"])
-    RSK = []
-    for c0, c1, d0 in SG:
-        w = 16 * (c1 - c0) + 1
-        for x in range(c1 - c0):
-            op("V", lambda: v.tensor_scalar(T.RS0[:, d0 + x * w:d0 + x * w + w - 1], T.IO[:, 0:w - 1], -16.0 * x, C(KP1), Op.add, Op.not_equal),
-               r=["IO0"] + CK, w=[("RS", c0 + x)])
-        op("V", lambda: v.memset(T.RS0[:, d0 + w - 1:d0 + (c1 - c0 - 1) * w:w], 4096.0), w=[("RS1", c0)])
-        op("V", lambda: v.tensor_copy(T.RS0[:, d0 + (c1 - c0) * w - 1:d0 + (c1 - c0) * w], C(DMK)), r=CK, w=[("RS2", c0)])
-        RSK += [("RS", c) for c in range(c0, c1)] + [("RS1", c0), ("RS2", c0)]
-    op("V", lambda: v.tensor_scalar(T.DT[:], T.IO[:, 0:8], 16.0, C(DUM), Op.mult, Op.add), r=["IO0"] + CK, w=["DT"])
-    op("A", lambda: a.activation(T.de[:, 0:256], T.IO[:, 0:256], Fn.Copy, scale=0.0), r=["IO0"], w=["de0a"])
-    op("V", lambda: v.memset(T.de[:, 256:1200], 0.0), r=["de0a"], w=["de0"])
-    wr["best"] = wr["Rl2"]
-    RK = ["Rl", "Rl2"]
+            op("V", lambda: v.tensor_scalar(T.w1[:], ind(win, T.bl[:]), C(KT), 2048.0, Op.add, Op.min), r=keys + ["bl"] + CK, w=["w1"])
+            op("P", lambda: pe.matmul(T.psl[:, 0:1], T.w1[:], T.one[:, 0:1], True, True), r=["w1", "one"], w=["sel"], b=["psl"])
+        else:
+            op("V", lambda: v.tensor_scalar(out, T.M[:], T.psl[:, 0:1], float(TOP), Op.max, Op.subtract), r=["M0", "sel"], w=[okey], b=["psl"])
+    best_lists()
+    root_mark()
+    root(0, T.AW[:, RL - 8:RL + 8], ["Rl", "spare"], None, None)
+    for lv in range(4):
+        prepare(lv)
+    for dst, lo, hi, s2, key in ((T.GL[:, 0:4:2], 37, 39, 0.0, "GL"), (T.PL[:], 0, 16, C(SC), "PL"), (T.PL2[:, 0:11], 5, 16, C(SC), "PL2"),
+                                 (T.DL[:], 16, 32, C(SC), "DL"), (T.DL2[:, 0:5], 27, 32, C(SC), "DL2"), (T.AL[:, 0:5], 32, 37, C(SC), "AL")):
+        lin("V", dst, T.ps1[:, lo:hi], 0.0625, s2, ["tab"] + CK, [key], ["ps1"])
+    root(1, None, None, T.l0[:, 0:16], ("l0", 0))
+    RK = ["Rl"]
+    cmp(T.Zh[:], T.IOb[:], C(Z15), 1.0, Op.is_equal, ["IOb"] + CK, ["Zh"])
+    cmp(T.Ih[:], T.IOb[:, 0:128], C(PF), 1.0, Op.is_equal, ["IOb"] + CK, ["Ih"])
+    cmp(T.I16[:, 0:128], T.IOb[:, 0:128], C(PF), 16384.0, Op.is_equal, ["IOb"] + CK, ["I16"])
+    cmp(T.I16[:, 128:256], T.IOb[:, 0:128], C(PF), 32768.0, Op.is_equal, ["IOb"] + CK, ["I32"])
+    cmp(T.GT[:], T.IK[:], C(KF), 0.5, Op.is_gt, ["IK"] + CK, ["GT"])
+    lin("A", C(KX), C(BC), 8.0, C(SC), CK, ["KX"])
+    for n in SWAP:
+        cmp(T.GT[:, 8 * n:8 * n + 16], T.IK[:, 8:24], C(KX), 0.5, Op.is_gt, ["IK", "KX", "GT"], [("GT", n)])
+    for c0, c1, p in OWN:
+        lin("V", T.LX[:, c0:c1], T.IO[:, 0:c1 - c0], 16.0, float(p + 15), ["IO0"], [("LX", c0)])
+    LXK = [("LX", x[0]) for x in OWN]
+    cmp(T.BOb[:, 0:128], T.IG[:], C(G16), 1.0, Op.is_equal, ["IG"] + CK, ["BOb0"])
+    cmp(T.BOb[:, 128:256], T.IG[:], C(G16), 16.0, Op.is_equal, ["IG"] + CK, ["BOb"])
     for i, n in enumerate((256, 512, 1024, 2048)):
         m = min(2 * n, V)
-        op("A", lambda: a.activation(T.IO[:, n:m], T.IO[:, 0:m - n], Fn.Identity, bias=float(n)),
-           r=["IO%d" % j for j in range(i + 1)], w=["IO%d" % (i + 1)])
+        lin("A", T.IO[:, n:m], T.IO[:, 0:m - n], 1.0, float(n), ["IO%d" % j for j in range(i + 1)], ["IO%d" % (i + 1)])
     IOK = ["IO%d" % j for j in range(5)]
-    for lo, hi, d in runs(DEP):
-        op("A", lambda: a.activation(T.SCL[:, 8 * lo:8 * hi], T.IO[:, 8 * lo:8 * hi], Fn.Identity, bias=float(2 ** d if d else 0), scale=0.0), r=["IO0"], w=[("SCL", d)])
-        op("A", lambda: a.activation(T.ISC[:, 8 * lo:8 * hi], T.IO[:, 8 * lo:8 * hi], Fn.Identity, bias=0.5 ** d, scale=0.0), r=["IO0"], w=[("ISC", d)])
+    lin("V", T.SCL[:, 0:8], T.IO[:, 0:8], 0.0, 0.0, ["IO0"], [("SCL", 0)])
+    for lo, hi, d in runs(DEP)[1:]:
+        lin("V", T.SCL[:, 8 * lo:8 * hi], T.IJ[:, 8 * lo:8 * hi], 0.0, 2.0 ** d, ["IJ"], [("SCL", d)])
     SK, IK = [("SCL", d) for d in range(5)], [("ISC", d) for d in range(5)]
-    DK = [("DM", 0), "DMa", "DMb"]
-
 
     def late(i):
         if i == 0:
-            op("V", lambda: v.tensor_scalar(T.TM[:, 0:128], T.IG[:], 0.0625, C(SC), Op.mult, Op.not_equal), r=["IG"] + CK, w=["TM0"])
-            op("A", lambda: a.activation(C(NKP), T.kp[:, 0:1], Fn.Copy, scale=-1.0), r=["kp"], w=["NKP"])
-            op("A", lambda: a.activation(T.TM[:, 128:256], T.IK[:, 0:128], Fn.Identity, bias=15.0, scale=-1.0), r=["IK"], w=["TM1"])
+            iota(T.IS[:], [[0, 32], [1, 8]], "IS")
         if i == 1:
-            op("A", lambda: a.activation(T.TM[:, 0:128], T.TM[:, 0:128], Fn.Copy, scale=-512.0), r=["TM0"], w=["TM0"])
+            for lo, hi, d in runs(DEP):
+                lin("A", T.CT[:, 8 * lo:8 * hi], T.IJ[:, 8 * lo:8 * hi], 0.5, 0.5 - 16 * d, ["IJ"], [("CT", d)])
+                lin("A", T.ISC[:, 8 * lo + (8 if d else 0):8 * hi + 8], T.IO[:, 0:8 * (hi - lo) + (0 if d else 8)], 0.0, 0.5 ** d, ["IO0"], [("ISC", d)])
+            cmp(T.CT[:, 512:768], T.IS[:], C(SC), -128.0, Op.not_equal, ["IS"] + CK, ["CTm"])
+            for x in range(3):
+                lin("A", T.R[:, 264 * x:264 * x + 8], T.IO[:, 0:8], 0.0, C(ZC), ["IO0"] + CK, [("Rz", x)])
+        if i == 2:
+            op("V", lambda: v.tensor_scalar(T.TM[:, 0:128], T.IG[:], 0.0625, C(SC), Op.mult, Op.not_equal), r=["IG"] + CK, w=["TM0"])
+            lin("A", C(NKP), T.kp[:, 0:1], -1.0, 0.0, ["kp"], ["NKP"])
+            lin("A", T.TM[:, 128:256], T.IK[:, 0:128], -1.0, 15.0, ["IK"], ["TM1"])
+            lin("A", T.TM[:, 0:128], T.TM[:, 0:128], -512.0, 0.0, ["TM0"], ["TM0"])
+            lin("A", T.CT[:, 256:512], T.F[:, FD:FA], -0.9375, 0.0, FK, ["CTl"])
+            lin("A", T.CX[:], T.IO[:, 0:8], 1.0, 0.0, ["IO0"], ["CX"])
+        if i == 3:
             op("V", lambda: v.tensor_tensor(T.TIE[:, 0:128], T.TM[:, 0:128], T.TM[:, 128:256], Op.add), r=["TM0", "TM1"], w=["TIE0"])
-            op("A", lambda: a.activation(T.TIE[:, 128:256], T.TIE[:, 0:128], Fn.Identity, bias=0.5), r=["TIE0"], w=["TIE"])
-
-    def top_of(win, keys, lst, lkey):
-        op("V", lambda: v.tensor_scalar(T.w1[:], win.indirect(lst), C(KT), 2048.0, Op.add, Op.min), r=keys + [lkey] + CK, w=["w1"])
-
-        def mm():
-            ins = None
-            for s in range(8):
-                ins = pe.matmul(T.psl[:, 0:1], T.Z2[:, 7 - s:135 - s], T.w1[:, s:s + 1], s == 0, s == 7)
-            return ins
-        op("P", mm, r=["w1", "Z2"], w=["sel"], b=["psl"])
-
-    def scatter(c0, c1, key):
-        op("V", lambda: v.tensor_copy(T.AW[:, 0:RL].indirect(T.OF[:, c0 + (c0 > 0):c1 + (c0 > 0)]), T.AW[:, RL + 16 * c0:RL + 16 * c1]),
-           r=[key, ("OF", 0 if c0 < 5 else 1 if c0 < 11 else 2), "spare"], w=["A"])
+            lin("A", T.TIE[:, 128:256], T.TIE[:, 0:128], 1.0, 0.5, ["TIE0"], ["TIE"])
+            lin("A", T.BO16[:], T.BOb[:, 128:256], 1.0, 0.0, ["BOb"], ["BO16"])
+    CTK = [("CT", d) for d in range(5)] + ["CTm"]
 
     for t in range(S):
         q, rr = verifier(rank, t), drafter(rank, t)
         last = t == S - 1
         o0, o1, o2 = T.O0, T.O1, T.O2
+        l0 = T.l0[:, 16 * t:16 * t + 16]
         outs = [o0[:, 16 * t:16 * t + 16], o1[:, 16 * t:16 * t + 16], o2[:, 8 * t:8 * t + 5], o2[:, 8 * t + 5:8 * t + 7]]
-        lists = [T.l0[:, 0:10], o0[:, 16 * t:16 * t + 9], o1[:, 16 * t + 6:16 * t + 11], o2[:, 8 * t:8 * t + 2]]
+        lists = [l0[:, 0:10], o0[:, 16 * t:16 * t + 9], o1[:, 16 * t + 6:16 * t + 11], o2[:, 8 * t:8 * t + 2]]
         mine = [o0[:, 16 * t + 10:16 * t + 15], o1[:, 16 * t:16 * t + 6], o2[:, 8 * t + 2:8 * t + 7]]
         mineK = [[("L", 1)], [("L", 2)], [("L", 3), ("L", 4)]]
         lm = lambda c0, c1: T.LM[:, 24 * t + c0 + (c0 > 0):24 * t + c1 + (c0 > 0)]
@@ -326,219 +474,177 @@ def rank_program(g, core, T, topo):
         for i in range(3):
             lands(("LM", t, i), "m%d%d" % (t, i))
 
-        def repeat(p, i):
-            if last:
-                return
-            nc = PC[p][1] - PC[p][0]
-            grp = [x for x in SG if PC[p][0] <= x[0] < PC[p][1]]
-            rel = lambda c: c - PC[p][0]
-            if i == 0:
-                lst, x = mine[p], nc
-                for lo, hi, c0 in (((0, 80, 0),), ((160, 256, 0),), ((336, 384, 0), (384, 416, 3)))[p]:
-                    op("A", lambda: a.activation(T.lf[:, 8 * p + c0:8 * p + c0 + (hi - lo) // 16], T.sc[:, lo + 15:hi:16], Fn.Identity, bias=-float(PICK)),
-                       r=mineK[p], w=[("lf", p)])
-                op("A", lambda: a.activation(T.Bo[:, 96 * p:96 * p + 16 * x], T.IO[:].indirect(lst), Fn.Copy), r=mineK[p] + IOK, w=[("Bo", p)])
-                for c0, c1, d0 in grp:
-                    w = 16 * (c1 - c0) + 1
-                    op("A", lambda: a.activation(T.de[:, d0 + w - 1:d0 + (c1 - c0) * w:w], T.lf[:, 8 * p + rel(c0):8 * p + rel(c1)], Fn.Copy),
-                       r=[("lf", p), "de0"], w=[("dz", c0)])
-            if i == 1:
-                for c0, c1, d0 in grp:
-                    w = 16 * (c1 - c0) + 1
-                    for c in range(c0, c1):
-                        lo = d0 + (c - c0) * w
-                        op("V", lambda: v.tensor_scalar(T.de[:, lo + 16 * (c - c0):lo + w - 1], T.Bo[:, 96 * p + 16 * rel(c):96 * p + 16 * rel(c1)],
-                                                        T.lf[:, 8 * p + rel(c):8 * p + rel(c) + 1], None, Op.is_equal),
-                           r=[("lf", p), ("Bo", p), "de0"], w=[("de", c)])
-            if i == 2:
-                lo, hi = grp[0][2], grp[-1][2] + (grp[-1][1] - grp[-1][0]) * (16 * (grp[-1][1] - grp[-1][0]) + 1)
-                op("V", lambda: v.tensor_tensor_scan(T.ds[:, lo:hi], T.RS0[:, lo:hi], T.de[:, lo:hi], 0.0, Op.mult, Op.add),
-                   r=[("de", c) for c in range(*PC[p])] + [("dz", x[0]) for x in grp] + RSK, w=[("ds", p)])
-            if i == 3:
-                for c0, c1, d0 in grp:
-                    w = 16 * (c1 - c0) + 1
-                    op("V", lambda: v.tensor_tensor(T.d1[:, c0 + (c0 > 0):c1 + (c0 > 0)], T.ds[:, d0 + w - 1:d0 + (c1 - c0) * w:w], T.DT[:, 0:c1 - c0], Op.min),
-                       r=[("ds", p), "DT"], w=[("d1", c0)])
-            if i == 4:
-                lo, hi = PC[p][0] + (p > 0), PC[p][1] + (p > 0)
-                op("V", lambda: v.tensor_copy(T.OF[:, lo:hi], T.d1[:, lo:hi]), r=[("d1", x[0]) for x in grp], w=[("OF", p)])
-        def root():
-            bcol = T.AW[:, RL + 256:RL + 257]
-            op("V", lambda: v.tensor_scalar(T.bu[:, 0:1], bcol, C(SC), None, Op.add), r=["best"] + CK, w=["bu"])
-            if t > 0:
-                scatter(13, 16, RK[2])
-            top_of(T.AW[:, RL:RL + 256], RK, T.bu[:, 0:1], "bu")
-            op("V", lambda: v.tensor_scalar(T.M[:, 0:1], bcol, C(K2), C(BC), Op.add, Op.mult), r=["best", "M"] + CK, w=["M0"])
-            op("V", lambda: v.tensor_scalar(T.l0[:], T.M[:], T.psl[:, 0:1], 28672.0, Op.max, Op.subtract), r=["M0", "sel"], w=[("L", 0)], b=["psl"])
-            if t > 0:
-                op("A", lambda: a.activation(T.yb[:, 16 * t - 16:16 * t], T.IO[:].indirect(T.l0[:, 2:3]), Fn.Copy), r=[("L", 0)] + IOK, w=[("yb", t)])
-                dma("S", T.yt[:, 8 * t - 8:8 * t], T.yb[0:128:16, 16 * t - 16:16 * t - 8], "dout", r=[("yb", t)])
-
         def pick(lv):
-            n = 8 * len(LEVELS[lv])
-            lo = LOFF[lv]
-            win = T.AW[:, 0:RL + 256] if lv == 0 else T.AW[:, 0:V]
-
-            def mm():
-                pe.matmul(T.psl[:, 0:n], T.Ib[:], T.CKa[:, lo:lo + n], True, False)
-                return pe.matmul(T.psl[:, 0:n], T.Ib[:], T.D1[:, 0:n], False, False)
-            op("P", mm, r=["Ib", "D1"] + CKK, w=["sel"], b=["psl"])
-            op("V", lambda: v.tensor_tensor(T.wf[:, 0:n], win.indirect(lists[lv]), T.F2[:, lo:lo + n], Op.subtract),
-               r=["A", "A0", ("L", lv), "spare", "F2"] + (RK if lv == 0 else []), w=["wf"])
+            n, lo = 8 * len(LEVELS[lv]), LOFF[lv]
+            win = T.AW[:, 0:RL + (256 if t else 8)] if lv == 0 else T.AW[:, 0:V]
+            op("V", lambda: v.tensor_tensor(T.wf[:, 0:n], ind(win, lists[lv]), T.F2[:, lo:lo + n], Op.subtract),
+               r=["A", "A0", "spare", "F2"] + (RK + [("l0", t)] if lv == 0 else [("L", lv)]), w=["wf"])
             op("V", lambda: v.tensor_scalar(T.wh[:, 0:n], T.wf[:, 0:n], -2048.0, 2048.0, Op.max, Op.min), r=["wf"], w=["wh"])
-            op("P", lambda: pe.matmul(T.psl[:, 0:n], T.BO[:], T.wh[:, 0:n], False, True), r=["wh", "BO"], w=["sel"], b=["psl"])
+            op("P", lambda: pe.matmul(PB[lv][:, 0:n], T.BO[:], T.wh[:, 0:n], False, True), r=["wh", "BO"], w=[PB[lv].name], b=[PB[lv].name])
 
         def listed(lv):
             n, lo = 8 * len(LEVELS[lv]), LOFF[lv]
-            op("V", lambda: v.tensor_tensor_scan(T.sc[:, lo:lo + n], T.RZ[:, 0:n], T.psl[:, 0:n], 0.0, Op.mult, Op.max),
-               r=["sel", "RZ"], w=[("sc", lv)], b=["psl"])
-            src = T.sc[:, lo:lo + n].indirect(T.GL[:, 2 * lv:2 * lv + 1]) if lv < 2 else T.sc[:, lo + 15:lo + n:16]
-            op("V", lambda: v.tensor_scalar(outs[lv], src, -float(PICK), None, Op.add), r=[("sc", lv), "GL"], w=[("L", lv + 1)])
+            op("V", lambda: v.tensor_tensor_scan(T.sc[:, lo:lo + n], T.RZ[:, 0:n], PB[lv][:, 0:n], 0.0, Op.add, Op.max),
+               r=[PB[lv].name, "RZ"], w=[("sc", lv)], b=[PB[lv].name])
+            src = ind(T.sc[:, lo:lo + n], T.GL[:, 2 * lv:2 * lv + 1]) if lv < 2 else T.sc[:, lo + 15:lo + n:16]
+            op("V", lambda: v.tensor_scalar(outs[lv], src, 2048.0, None, Op.add), r=[("sc", lv), "GL"], w=[("L", lv + 1)])
             if lv != 2:
                 p = min(lv, 2)
-                send(q, lm(PC[p][0], PC[p][1]), mine[p], "m%d%d" % (t, p), mineK[p], "sent0" if (t, lv) == (0, 3) else "sent")
+                send(q, lm(PC[p][0], PC[p][1]), mine[p], "m%d%d" % (t, p), mineK[p], *(("sent0", ["left"]) if (t, lv) == (0, 3) else ()))
 
-        qwin, QK = (T.AW[:, 0:V], ["A"]) if t == 0 else (T.Q[:], ["Q"])
-        y0, r0 = 272 * t + 16, 264 * t
-        Y = lambda j0, j1: T.Y[:, y0 + j0:y0 + j1]
-        R = lambda j0, j1: T.R[:, r0 + j0:r0 + j1]
-        CUK = [("cu", 0), ("cu", 5), ("cu", 11)]
-
-        def cand(c0, c1):
-            op("V", lambda: v.tensor_copy(T.cu[:, 16 * c0:16 * c1], qwin.indirect(lm(c0, c1))), r=QK + [mk(c0)], w=[("cu", c0)])
-
-        def gather(j0, j1, e, ck):
-            src = T.K[:].indirect(T.cu[:, j0:j1])
-            if e == "A":
-                op("A", lambda: a.activation(T.kc[:, 16 * j0:16 * j1], src, Fn.Copy), r=["K", ("cu", ck)], w=[("kc", j0)])
-            else:
-                op("V", lambda: v.tensor_copy(T.kc[:, 16 * j0:16 * j1], src), r=["K", ("cu", ck)], w=[("kc", j0)])
-        KCK = [[0], [80, 160, 176], [208]]
-
-        root()
-        if not last:
-            pick(0)
+        def emitted():
             if t > 0:
-                late(t - 1)
-            else:
-                table(0)
-            listed(0)
-            repeat(0, 0)
-            pick(1)
-            repeat(0, 1)
-            if t == 0:
-                table(1)
-            listed(1)
-            repeat(1, 0)
-            pick(2)
-            repeat(0, 2)
-            if t == 0:
-                table(2)
-            listed(2)
-            pick(3)
-            cand(0, 5)
-            gather(0, 80, "A", 0)
-            listed(3)
-        if t == 0:
-            need("S", ("sent0", NE))
-            dma("S", T.Q[:], T.qt[:], "dq2", w=["Q"])
+                op("A", lambda: a.activation(T.yb[:, 16 * t - 16:16 * t], ind(T.IO[:], l0[:, 2:3]), Fn.Copy), r=[("l0", t)] + IOK, w=[("yb", t)])
+                dma("S", T.yt[:, 8 * t - 8:8 * t], T.yb[0:128:16, 16 * t - 16:16 * t - 8], "dout", r=[("yb", t)])
 
-        def numbers(c0, c1):
-            op("V", lambda: v.tensor_tensor(T.kn[:, 16 * c0:16 * c1], T.K[:].indirect(lm(c0, c1)), T.SCL[:, 16 * c0:16 * c1], Op.mult),
-               r=["K", mk(c0)] + SK, w=[("kn", c0)])
+        def repeat(i, p=0):
+            c0, c1, end = DD[min(p, 2)]
+            c2 = min(c1, 15)
+            sk = [("sc", lv) for lv in range(4) if LOFF[lv] < end]
+            if i == 0:
+                lo, hi = 16 * PC[p][0], 16 * PC[p][1]
+                op("A", lambda: a.activation(T.Bo[:, lo:hi], ind(T.IO[:], mine[p]), Fn.Identity, bias=-2048.0), r=mineK[p] + IOK, w=[("Bo", p)])
+            bk = [("Bo", x) for x in range(p + 1)]
+            if i == 1:
+                op("V", lambda: v.tensor_tensor(T.ed[:, 16 * c0:16 * c1], ind(T.sc[:, 0:end], T.LX[:, c0:c1]), T.Bo[:, 16 * c0:16 * c1], Op.is_equal),
+                   r=sk + bk + LXK, w=[("ed", 0, p)])
+            if i == 2:
+                op("V", lambda: v.tensor_tensor(T.ed[:, 256 + 16 * c0:256 + 16 * c2], ind(T.sc[:, 0:end], T.LX[:, c0:c2]),
+                                                T.Bo[:, 16 * c0 + 16:16 * c2 + 16], Op.is_equal), r=sk + bk + LXK, w=[("ed", 1, p)])
+            if i == 3:
+                lo, hi, lhs, rhs, key = ((0, 256, T.I16[:, 0:128], T.GT[:], [("GT", n) for n in SWAP]),
+                                         (0, 160, T.I16[:, 0:128], T.ed[:, 0:160], [("ed", 0, 0), ("ed", 0, 1)]),
+                                         (0, 160, T.I16[:, 128:256], T.ed[:, 256:416], [("ed", 1, 0), ("ed", 1, 1)]),
+                                         (0, 256, T.Ih[:], T.Bo[:], [("Bo", x) for x in range(3)]),
+                                         (160, 256, T.I16[:, 0:128], T.ed[:, 160:256], [("ed", 0, 2)]),
+                                         (160, 240, T.I16[:, 128:256], T.ed[:, 416:496], [("ed", 1, 2)]))[p]
+                op("P", lambda: pe.matmul(T.pb0[:, lo:hi], lhs, rhs, p == 0, p == 5), r=key + ["I16", "I32", "Ih"], w=["pb0"], b=["pb0"])
+            if i == 4:
+                op("V", lambda: v.tensor_tensor_scan(T.ds[:], T.RZ[:], T.pb0[:, 0:256], 0.0, Op.add, Op.max), r=["pb0", "RZ"], w=["ds"], b=["pb0"])
+            if i == 5:
+                for h in range(2):
+                    op("V", lambda: v.tensor_scalar(T.OF[:, h:16:2], T.ds[:, 16 * h + 15:256:32], 2048.0 - 16384.0, C(SP1 if h else SP0), Op.add, Op.min),
+                       r=["ds"] + CK, w=[("OF", h)])
+
+        def scatter(c):
+            keys = [("Rl", t, m) for m in range(3) if POS[m][0] < 16 * c + 32 and 16 * c < POS[m][1]]
+            op("V", lambda: v.tensor_copy(ind(T.AW[:, 0:RL], T.OF[:, c:c + 2]), T.AW[:, RL + 16 * c:RL + 16 * c + 32]),
+               r=keys + [("OF", 0), ("OF", 1)], w=["A", "A0", "spare"])
+
+        qwin, QK = (T.AW[:, 0:V], ["A", "A0"]) if t == 0 else (T.Q[:], ["Q"])
+        y0 = 264 * t + 8
+        Y = lambda j0, j1: T.Y[:, y0 + j0:y0 + j1]
+        R = lambda j0, j1: T.R[:, y0 + j0:y0 + j1]
+        piece = lambda j: 0 if j < 80 else 1 if j < 176 else 2
+        KCK = [[], [], []]
+        DB = [(T.pa0, T.pb0), (T.pa1, T.pb1), (T.pa0, T.pb1)]
+
+        def cand(p, e="A"):
+            c0, c1 = PC[p]
+            lin(e, T.cu[:, 16 * c0:16 * c1], ind(qwin, lm(c0, c1)), 1.0, 0.0, QK + [mk(c0)], [("cu", p)])
+
+        def half(m, e="A"):
+            lo, hi = (0, POS[0][1]) if m == 0 else (POS[0][1], 256)
+            lin(e, T.ch[:, lo:hi], T.cu[:, lo:hi], 1.0, -2048.0, [("cu", p) for p in range(piece(hi - 1) + 1)], [("ch", m)])
+
+        def gather(j0, j1, e="A"):
+            lin(e, T.kc[:, 16 * j0:16 * j1], ind(T.K[:], T.cu[:, j0:j1]), 1.0, 0.0, ["K", ("cu", piece(j0))], [("kc", j0)])
+            KCK[[lo <= j0 < hi for lo, hi in POS].index(True)].append(("kc", j0))
+
+        def numbers(p):
+            c0, c1 = PC[p]
+            op("V", lambda: v.tensor_tensor(T.kn[:, 16 * c0:16 * c1], ind(T.K[:], lm(c0, c1)), T.SCL[:, 16 * c0:16 * c1], Op.mult),
+               r=["K", mk(c0)] + SK, w=[("kn", p)])
 
         def state(i):
-            j0, j1, win, lst, kk = ((0, 80, T.XC[:, 0:8] if last else T.Y[:, y0 - 16:y0 - 8], T.PL[:, 0:5], 0), (80, 176, Y(0, 80), T.PL2[:, 0:6], 5),
-                                    (176, 224, Y(0, 176), T.PL2[:, 6:9], 11), (224, 256, Y(0, 224), T.PL[:, 14:16], 11))[i]
-            op("V", lambda: v.tensor_tensor(Y(j0, j1), win.indirect(lst), T.kn[:, j0:j1], Op.add),
+            j0, j1, win, lst, kk = ((0, 80, T.XC[:, 0:8] if last else Y(-8, 0), T.PL[:, 0:5], 0), (80, 176, Y(0, 80), T.PL2[:, 0:6], 1),
+                                    (176, 224, Y(0, 176), T.PL2[:, 6:9], 2), (224, 256, Y(0, 224), T.PL[:, 14:16], 2))[i]
+            op("V", lambda: v.tensor_tensor(Y(j0, j1), ind(win, lst), T.kn[:, j0:j1], Op.add),
                r=["PL", "PL2", ("kn", kk), ("Y", i - 1) if i else ("Yr", t)], w=[("Y", i)])
 
-        def thresh(i):
-            for j0, j1 in (((0, 8), (8, 80)), ((80, 88), (88, 176)), ((176, 224),), ((224, 256),))[i]:
+        TH = [(0, 8, 0), (8, 80, 0), (80, 88, 1), (88, 176, 1), (176, 224, 2), (224, 256, 3)]
+        THK = [[j0 for j0, j1, i in TH if j0 < hi and lo < j1] for lo, hi in POS]
+
+        def thresh(i0, i1):
+            for j0, j1, i in TH[i0:i1]:
                 op("V", lambda: v.tensor_scalar(T.pth[:, j0:j1], Y(j0, j1), 0.5 ** DEP[j0 // 8], T.kp[:, 0:1], Op.mult, Op.subtract),
                    r=[("Y", i), "kp"], w=[("th", j0)])
-        THK = [[0, 8], [80, 88, 176], [176, 224]]
 
         def compare(m, k0, k1):
-            j0, j1 = 16 * CH[m][0], 16 * CH[m][1]
+            j0, j1 = POS[m]
             n = j1 - j0
             ps = T["ps%d" % (m % 2)]
             for k in range(k0, k1):
                 bo = 16 * j0 + n * k
                 op("V", lambda: v.tensor_tensor(T.bits[:, bo:bo + n], T.kc[:, 16 * j0 + k:16 * j1:16], T.pth[:, j0:j1], Op.is_ge),
-                   r=[("kc", x) for x in KCK[m]] + [("th", x) for x in THK[m]], w=[("bits", m, k)])
+                   r=KCK[m] + [("th", x) for x in THK[m]], w=[("bits", m, k)])
                 op("P", lambda: pe.matmul(ps[:, 0:n], T.Zh[:, 15 - k:143 - k], T.bits[:, bo:bo + n], k == 0, k == 15),
                    r=[("bits", m, k), "Zh"], w=[("S", m % 2)], b=[ps.name] if k in (0, 15) else [])
 
         def keys(m, e):
-            j0, j1 = 16 * CH[m][0], 16 * CH[m][1]
-            n = j1 - j0
+            j0, j1 = POS[m]
             ps = T["ps%d" % (m % 2)]
-            if e == "A":
-                op("A", lambda: a.activation(T.key[:, j0:j1], ps[:, 0:n], Fn.Identity, bias=C(KB), scale=16.0), r=[("S", m % 2)] + CK, w=[("key", m)], b=[ps.name])
-            else:
-                op("V", lambda: v.tensor_scalar(T.key[:, j0:j1], ps[:, 0:n], 16.0, C(KB), Op.mult, Op.add), r=[("S", m % 2)] + CK, w=[("key", m)], b=[ps.name])
+            lin(e, T.key[:, j0:j1], ps[:, 0:j1 - j0], 16.0, C(KB), [("S", m % 2)] + CK, [("key", m)], [ps.name])
 
-        def diffs(m):
-            j0, j1 = 16 * CH[m][0], 16 * CH[m][1]
+        def diffs(m, h):
+            j0, j1 = POS[m]
             n = j1 - j0
-            for h in range(2):
-                pd = T["p%s%d" % ("ab"[h], m % 2)]
+            pd = DB[m][h]
 
-                def mm():
-                    ins = None
-                    for jj in range(4):
-                        j = 1 + 4 * h + jj
-                        ins = pe.matmul(pd[:, n * jj:n * jj + n], T.DM[:, 128 * j:128 * j + 128], T.key[:, j0:j1], True, True)
-                    return ins
-                op("P", mm, r=[("key", m)] + DK, w=[("D", m % 2, h)], b=[pd.name])
+            def mm():
+                ins = None
+                for jj in range(4):
+                    j = 1 + 4 * h + jj
+                    ins = pe.matmul(pd[:, n * jj:n * jj + n], T.DM[:, 128 * j:128 * j + 128], T.key[:, j0:j1], True, True)
+                return ins
+            op("P", mm, r=[("key", m)] + DK, w=[pd.name], b=[pd.name])
 
         def signs(m, h, e):
-            n = 16 * (CH[m][1] - CH[m][0])
-            pd = T["p%s%d" % ("ab"[h], m % 2)]
-            so = 128 * CH[m][0] + 4 * n * h
+            n = POS[m][1] - POS[m][0]
+            pd = DB[m][h]
+            so = 8 * POS[m][0] + 4 * n * h
             if e == "A":
-                op("A", lambda: a.activation(T.sg[:, so:so + 4 * n], pd[:, 0:4 * n], Fn.Sign), r=[("D", m % 2, h)], w=[("sg", m, h)], b=[pd.name])
+                op("A", lambda: a.activation(T.sg[:, so:so + 4 * n], pd[:, 0:4 * n], Fn.Sign), r=[pd.name], w=[("sg", m, h)], b=[pd.name])
             else:
-                op("V", lambda: v.tensor_scalar(T.sg[:, so:so + 4 * n], pd[:, 0:4 * n], -1.0, 1.0, Op.max, Op.min), r=[("D", m % 2, h)], w=[("sg", m, h)], b=[pd.name])
+                op("V", lambda: v.tensor_scalar(T.sg[:, so:so + 4 * n], pd[:, 0:4 * n], -1.0, 1.0, Op.max, Op.min), r=[pd.name], w=[("sg", m, h)], b=[pd.name])
 
         def places(m, h):
-            n = 16 * (CH[m][1] - CH[m][0])
-            so = 128 * CH[m][0] + 4 * n * h
+            n = POS[m][1] - POS[m][0]
+            so = 8 * POS[m][0] + 4 * n * h
             ps = T["ps%d" % (m % 2)]
 
             def mm():
                 ins = None
-                if h == 0:
-                    pe.matmul(ps[:, 128:128 + n], T.Ih[:], T.ch[:, 16 * CH[m][0]:16 * CH[m][1]], True, False)
+                if h < 0:
+                    return pe.matmul(ps[:, 128:128 + n], T.Ih[:], T.ch[:, POS[m][0]:POS[m][1]], True, False)
                 for jj in range(4):
                     j = 1 + 4 * h + jj
                     dj = 16 - j if j < 8 else 0
                     ins = pe.matmul(ps[:, 128:128 + n], T.DM[:, 128 * dj:128 * dj + 128], T.sg[:, so + n * jj:so + n * jj + n], False, j == 8)
                 return ins
-            op("P", mm, r=[("sg", m, h), "ch", "Ih"] + DK, w=[("Rp", m % 2)], b=[ps.name])
+            op("P", mm, r=([("ch", min(m, 1)), "Ih"] if h < 0 else [("sg", m, h)]) + DK, w=[("Rp", m % 2)], b=[ps.name])
 
-        def ranked(m):
-            j0, j1 = 16 * CH[m][0], 16 * CH[m][1]
+        def ranked(m, e):
+            lo, hi = POS[m]
             ps = T["ps%d" % (m % 2)]
-            op("V", lambda: v.tensor_scalar(R(j0, j1), ps[:, 128:128 + j1 - j0], C(KR), None, Op.add), r=[("Rp", m % 2)] + CK, w=[("R", m)], b=[ps.name])
-            if m < 2:
-                send(rr, T.AW[:, RL + j0:RL + j1], R(j0, j1), "r%d%d" % (t, m), [("R", m)])
+            lin(e, R(lo, hi), ps[:, 128:128 + hi - lo], 1.0, C(KR), [("Rp", m % 2)] + CK, [("R", m)], [ps.name])
+            send(rr, T.AW[:, RL + lo:RL + hi], R(lo, hi), "r%d%d" % (t, m), [("R", m)])
 
-        def tokens(c0, c1):
-            op("A", lambda: a.activation(T.B[:, 16 * c0:16 * c1], T.IO[:].indirect(lm(c0, c1)), Fn.Identity, bias=0.0 if last else C(NK)),
-               r=IOK + CK + [mk(c0), mk(c1 - 1)], w=[("B", c0)])
+        def tokens(p):
+            c0, c1 = PC[p]
+            op("A", lambda: a.activation(T.B[:, 16 * c0:16 * c1], ind(T.IO[:], lm(c0, c1)), Fn.Identity, bias=0.0 if last else C(NK)),
+               r=IOK + CK + [mk(c0)], w=[("B", p)])
 
         def paths(early):
             bo = T.BOb[:, 0:128] if last else T.BOb[:, 128:256]
             ins = None
-            if early:
+            if early == 0:
                 pe.matmul(T.psl[:, 0:256], T.Ib[:], T.CT[:, 256:512] if last else T.CT[:, 0:256], True, False)
+                ins = pe.matmul(T.psl[:, 0:256], T.Ib[:], T.CT[:, 512:768], False, False)
+            elif early == 1:
                 pe.matmul(T.psl[:, 8:88], bo, T.eq[:, 8:88], False, False)
                 pe.matmul(T.psl[:, 88:176], bo, T.ok2[:, 8:96], False, False)
-                for n in range(22, 32):
-                    anc = (PAR[n] if DEP[n] == 3 else PAR[PAR[n]]) - 10
-                    ins = pe.matmul(T.psl[:, 8 * n:8 * n + 8], bo, T.ok2[:, 8 * anc:8 * anc + 8], False, False)
+                ins = pe.matmul(T.psl[:, 176:256], bo, T.ok3[:], False, False)
             else:
                 pe.matmul(T.psl[:, 176:256], bo, T.eq[:, 176:256], False, False)
                 for n in range(28, 32):
@@ -546,54 +652,51 @@ def rank_program(g, core, T, topo):
             return ins
 
         def commit(i):
-            if i == -1:
-                src = T.CB[:, 0:48].indirect(T.DL[:, 0:11]) if last else R(0, 80).indirect(T.PL[:, 0:11])
-                op("V", lambda: v.tensor_tensor(T.eq[:, 0:176], src, T.B[:, 0:176], Op.is_equal),
-                   r=[("B", 0), ("B", 5), "PL", "DL"] + ([("CB", d) for d in range(3)] if last else [("R", 0)]), w=["eqa"])
-            if i == -2:
-                op("V", lambda: v.tensor_tensor(T.ok2[:], T.eq[:, 0:80].indirect(T.PL2[:, 0:6]), T.eq[:, 80:176], Op.add), r=["eqa", "PL2"], w=["ok2"])
-            if i == -3:
-                op("P", lambda: paths(True), r=["eqa", "ok2", "BOb", "Ib", "CT"], w=["sel"], b=["psl"])
             if i == 0:
-                src = T.CB[:, 0:80].indirect(T.DL2[:, 0:5]) if last else R(0, 208).indirect(T.PL2[:, 6:11])
+                src = ind(T.CB[:, 0:48], T.DL[:, 0:11]) if last else ind(R(0, 80), T.PL[:, 0:11])
+                op("V", lambda: v.tensor_tensor(T.eq[:, 0:176], src, T.B[:, 0:176], Op.is_equal),
+                   r=[("B", 0), ("B", 1), "PL", "DL"] + ([("CB", d) for d in range(3)] if last else [("R", 0)]), w=["eqa"])
+            if i == 1:
+                op("V", lambda: v.tensor_tensor(T.ok2[:], ind(T.eq[:, 0:80], T.PL2[:, 0:6]), T.eq[:, 80:176], Op.add), r=["eqa", "PL2"], w=["ok2"])
+                lin("A", T.ok3[:], ind(T.ok2[:], T.AL[:, 0:5]), 1.0, 0.0, ["ok2", "AL"], ["ok3"])
+            if i == -1:
+                op("P", lambda: paths(0), r=["Ib"] + (["CTl", "CTm"] if last else CTK), w=["sel"], b=["psl"])
+            if i == 11:
+                op("P", lambda: paths(1), r=["eqa", "ok2", "ok3", "BOb", "BOb0"], w=["sel"], b=["psl"])
+            if i == 2:
+                src = ind(T.CB[:, 0:80], T.DL2[:, 0:5]) if last else ind(R(0, 200), T.PL2[:, 6:11])
                 op("V", lambda: v.tensor_tensor(T.eq[:, 176:256], src, T.B[:, 176:256], Op.is_equal),
-                   r=[("B", 11), "PL2", "DL2"] + ([("CB", d) for d in range(5)] if last else [("R", 0), ("R", 1)]), w=["eq"])
-                op("P", lambda: paths(False), r=["eq"], w=["sel"], b=["psl"])
-            if i == 4:
+                   r=[("B", 2), "DL2", "PL2"] + ([("CB", d) for d in range(5)] if last else [("R", 0), ("R", 1)]), w=["eq"])
+                op("P", lambda: paths(2), r=["eq"], w=["sel"], b=["psl"])
+            if i == 3:
                 op("V", lambda: v.tensor_reduce(T.bf[:, 0:1], T.psl[:, 0:256], Ax.X, Op.max), r=["sel"], w=["bf"], b=["psl"])
-            if i == 41:
-                op("V", lambda: v.tensor_scalar(R(256, 257), T.bf[:, 0:1], 16.0, None, Op.mult), r=["bf"], w=["bs"])
+            if i == 4:
+                op("A", lambda: a.activation(T.ig[:], ind(T.ISC[:], T.bq[:, 0:1]), Fn.Copy), r=["bq"] + IK, w=["ig"])
             if i == 5:
-                op("V", lambda: v.tensor_scalar(T.bq[:, 0:1], T.bf[:, 0:1], 16.0, C(SC), Op.mult, Op.add), r=["bf"] + CK, w=["bq"])
-            if i == 6:
-                op("V", lambda: v.tensor_copy(T.ig[:], T.ISC[:].indirect(T.bq[:, 0:1])), r=["bq"] + IK, w=["ig"])
-            if i == 7:
-                op("V", lambda: v.tensor_tensor(T.X[:, 32 * t:32 * t + 16], Y(0, 256).indirect(T.bq[:, 0:1]), T.ig[:], Op.mult),
-                   r=["bq", "ig", ("Y", 3)], w=["X"])
+                op("V", lambda: v.tensor_tensor(T.X[:, 16 * t:16 * t + 16], ind(Y(-8, 256), T.bq[:, 0:1]), T.ig[:], Op.mult),
+                   r=["bq", "ig", ("Y", 3)], w=[("X", t)])
 
         def chain(i, st):
-            c, xk = T.cc[:, 2 * i:2 * i + 1], ("XC", i)
+            c, xk = T.cc[:, 2 * i:2 * i + 1], ("XC", i) if i else ("Yr", t)
             if st == 0:
                 if i == 0:
                     op("V", lambda: v.tensor_copy(c, T.XC[:, 8:9]), r=[xk], w=[("cc", 0)])
-                    op("A", lambda: a.activation(T.CB[:, 0:16], T.IO[:].indirect(c), Fn.Copy), r=[("cc", 0)] + IOK, w=[("CB", 0)])
                 else:
-                    op("V", lambda: v.tensor_tensor(T.XC[:, 16 * i:16 * i + 16], T.K[:].indirect(c), T.hx[:], Op.add), r=["K", ("cc", i), "hx"], w=[xk])
-                op("A", lambda: a.activation(T.thx[:], T.XC[:, 16 * i:16 * i + 8].indirect(T.CX[:]), Fn.Identity, bias=C(NKP)),
+                    op("V", lambda: v.tensor_tensor(T.XC[:, 16 * i:16 * i + 16], ind(T.K[:], c), T.hx[:], Op.add), r=["K", ("cc", i), "hx"], w=[xk])
+                op("A", lambda: a.activation(T.thx[:], ind(T.XC[:, 16 * i:16 * i + 8], T.CX[:]), Fn.Identity, bias=C(NKP)),
                    r=[xk, "CX", "NKP"], w=["thx"])
-                op("V", lambda: v.tensor_copy(T.ccu[:], T.Q[:].indirect(c)), r=QK + [("cc", i)], w=["ccu"])
+                op("V", lambda: v.tensor_copy(T.ccu[:], ind(T.Q[:], c)), r=QK + [("cc", i)], w=["ccu"])
                 op("P", lambda: pe.matmul(T.ps0[:, 0:128], T.Ib[:], T.TIE[:, 0:128], True, False), r=["TIE", "Ib"], w=["cA"], b=["ps0"])
                 op("P", lambda: pe.matmul(T.ps1[:, 0:128], T.Ib[:], T.TIE[:, 128:256], True, False), r=["TIE", "Ib"], w=["cB"], b=["ps1"])
-                op("V", lambda: v.tensor_scalar(T.tkh[:], T.IO[:].indirect(T.ccu[:, 0:8]), -2048.0, 0.5 ** 12, Op.add, Op.mult), r=["ccu"] + IOK, w=["tkh"])
-                op("P", lambda: pe.matmul(T.ps1[:, 0:128], T.Ih[:], T.tkh[:], False, False), r=["tkh", "Ih"], w=["cB"], b=["ps1"])
+                lin("A", T.tkh[:], ind(T.IO[:], T.ccu[:, 0:8]), 0.5 ** 12, -0.5, ["ccu"] + IOK, ["tkh"])
                 if i < 4:
-                    op("A", lambda: a.activation(T.hx[:], T.XC[:, 16 * i:16 * i + 16], Fn.Copy, scale=0.5), r=[xk], w=["hx"])
-                if i > 0:
-                    op("A", lambda: a.activation(T.CB[:, 16 * i:16 * i + 16], T.IO[:].indirect(c), Fn.Copy), r=[("cc", i)] + IOK, w=[("CB", i)])
+                    lin("A", T.hx[:], T.XC[:, 16 * i:16 * i + 16], 0.5, 0.0, [xk], ["hx"])
+                op("A", lambda: a.activation(T.CB[:, 16 * i:16 * i + 16], ind(T.IO[:], c), Fn.Copy), r=[("cc", i)] + IOK, w=[("CB", i)])
             if st == 1:
-                op("V", lambda: v.tensor_tensor(T.cb[:], T.K[:].indirect(T.ccu[:, 0:8]), T.thx[:], Op.is_ge), r=["K", "ccu", "thx"], w=["cb"])
+                op("V", lambda: v.tensor_tensor(T.cb[:], ind(T.K[:], T.ccu[:, 0:8]), T.thx[:], Op.is_ge), r=["K", "ccu", "thx"], w=["cb"])
                 op("P", lambda: pe.matmul(T.ps0[:, 0:128], T.BO16[:], T.cb[:], False, True), r=["cb", "BO16"], w=["cA"], b=["ps0"])
-                op("P", lambda: pe.matmul(T.ps1[:, 0:128], T.BO16[:], T.cb[:], False, True), r=["cb", "BO16"], w=["cB"], b=["ps1"])
+                op("P", lambda: pe.matmul(T.ps1[:, 0:128], T.BO16[:], T.cb[:], False, False), r=["cb", "BO16"], w=["cB"], b=["ps1"])
+                op("P", lambda: pe.matmul(T.ps1[:, 0:128], T.Ih[:], T.tkh[:], False, True), r=["tkh", "Ih"], w=["cB"], b=["ps1"])
             if st == 2:
                 op("V", lambda: v.tensor_reduce(T.cm[:, 0:1], T.ps0[:, 0:128], Ax.X, Op.max), r=["cA"], w=["m2"], b=["ps0"])
                 op("V", lambda: v.tensor_reduce(T.cm[:, 1:2], T.ps1[:, 0:128], Ax.X, Op.max), r=["cB"], w=["m1"], b=["ps1"])
@@ -601,157 +704,179 @@ def rank_program(g, core, T, topo):
                 c1 = T.cc[:, 2 * i + 2:2 * i + 3]
                 op("V", lambda: v.tensor_scalar(c1, T.cm[:, 1:2], T.cm[:, 0:1], 4096.0, Op.subtract, Op.mult), r=["m1", "m2"], w=[("cc", i + 1)])
                 if i == 4:
-                    op("A", lambda: a.activation(T.CB[:, 80:96], T.IO[:].indirect(c1), Fn.Copy), r=[("cc", 5)] + IOK, w=[("CB", 5)])
+                    op("A", lambda: a.activation(T.CB[:, 80:96], ind(T.IO[:], c1), Fn.Copy), r=[("cc", 5)] + IOK, w=[("CB", 5)])
 
         def unscale(d0, d1):
-            for lo, hi, d in runs(DEP)[d0:d1]:
-                op("A", lambda: a.activation(T.YN[:, 8 * lo:8 * hi], Y(8 * lo, 8 * hi), Fn.Copy, scale=0.5 ** d),
-                   r=[("Y", 1 if d < 3 else d - 1)], w=[("YN", d)])
+            for lo, hi, (d, x) in runs([(DEP[n], NODE[n] - n) for n in range(32)]):
+                if d0 <= d < d1:
+                    lin("A", T.YN[:, 8 * (lo + x):8 * (hi + x)], Y(8 * lo, 8 * hi), 0.5 ** d, 0.0, [("Y", 1 if d < 3 else d - 1)], [("YN", lo)])
+        YNK = lambda d0, d1: [("YN", lo) for lo, hi, (d, x) in runs([(DEP[n], NODE[n] - n) for n in range(32)]) if d0 <= d < d1]
 
         if last:
-            wr[("XC", 0)] = wr[("Yr", t)]
             pick(0)
             chain(0, 0)
-            chain(0, 1)
+            emitted()
             listed(0)
+            chain(0, 1)
             pick(1)
             chain(0, 2)
-            chain(0, 3)
-            chain(1, 0)
             listed(1)
-            chain(1, 1)
+            chain(0, 3)
             pick(2)
-            chain(1, 2)
-            chain(1, 3)
+            chain(1, 0)
             listed(2)
-            chain(2, 0)
-            chain(2, 1)
+            chain(1, 1)
             pick(3)
-            tokens(0, 5)
-            tokens(5, 11)
+            chain(1, 2)
+            listed(3)
+            chain(1, 3)
+            chain(2, 0)
+            tokens(0)
+            numbers(0)
+            chain(2, 1)
+            state(0)
+            numbers(1)
             chain(2, 2)
             chain(2, 3)
-            listed(3)
+            tokens(1)
             chain(3, 0)
-            numbers(0, 5)
-            chain(3, 1)
-            commit(-1)
-            state(0)
-            commit(-2)
-            commit(-3)
-            chain(3, 2)
-            numbers(5, 11)
-            chain(3, 3)
             state(1)
-            chain(4, 0)
-            tokens(11, 16)
-            unscale(0, 3)
-            send(rr, T.YL[:, 0:176], T.YN[:, 0:176], "yn0", [("YN", d) for d in range(3)])
-            numbers(11, 16)
-            chain(4, 1)
+            chain(3, 1)
             commit(0)
+            unscale(0, 3)
+            send(rr, T.YL[:, 0:176], T.YN[:, 0:176], "yn0", YNK(0, 3))
+            chain(3, 2)
+            commit(1)
+            commit(-1)
+            commit(11)
+            chain(3, 3)
+            tokens(2)
+            chain(4, 0)
+            numbers(2)
+            chain(4, 1)
+            commit(2)
             state(2)
             chain(4, 2)
             state(3)
             unscale(3, 5)
-            commit(4)
+            commit(3)
             chain(4, 3)
-            commit(5)
-            op("V", lambda: v.tensor_copy(T.YN[:, 256:272], T.XC[:].indirect(T.bq[:, 0:1])), r=["bq"] + [("XC", d) for d in range(5)], w=["X"])
-            op("V", lambda: v.tensor_copy(T.YN[:, 272:288], T.CB[:, 16:96].indirect(T.bq[:, 0:1])),
+            lin("V", T.bq[:, 0:1], T.bf[:, 0:1], 16.0, C(SC), ["bf"] + CK, ["bq"])
+            op("V", lambda: v.tensor_copy(T.YN[:, 256:272], ind(T.XC[:], T.bq[:, 0:1])), r=["bq", ("Yr", t)] + [("XC", d) for d in range(1, 5)], w=["X"])
+            op("V", lambda: v.tensor_copy(T.YN[:, 272:288], ind(T.CB[:, 16:96], T.bq[:, 0:1])),
                r=["bq"] + [("CB", d) for d in range(6)], w=["X2"])
-            send(rr, T.YL[:, 176:280], T.YN[:, 176:280], "fin", ["X", "X2", ("YN", 3), ("YN", 4)])
+            send(rr, T.YL[:, 176:280], T.YN[:, 176:280], "fin", ["X", "X2"] + YNK(3, 5))
             break
 
-        numbers(0, 5)
-        repeat(0, 3)
+        for m in range(3):
+            lands(("Rl", t, m), "r%d%d" % (t, m))
+        pick(0)
+        emitted()
+        listed(0)
+        repeat(0, 0)
+        for lv in (1, 2, 3):
+            pick(lv)
+            listed(lv)
+        if t == 0:
+            late(0)
+            dma("S", T.Q[:], T.qt[:], "dq2", r=["left"], w=["Q"], lag=7.0)
+        cand(0)
+        gather(0, 80)
+        numbers(0)
         state(0)
-        repeat(0, 4)
-        thresh(0)
-        cand(5, 11)
-        gather(80, 160, "A", 5)
-        numbers(5, 11)
-        gather(160, 176, "V", 5)
+        thresh(0, 2)
+        cand(1)
+        gather(80, POS[0][1])
+        gather(POS[0][1], 176)
+        numbers(1)
         state(1)
-        compare(0, 0, 1)
-        thresh(1)
-        compare(0, 1, 11)
-        cand(11, 16)
-        gather(176, 208, "A", 11)
-        gather(208, 256, "A", 11)
-        numbers(11, 16)
-        compare(0, 11, 12)
-        state(2)
-        compare(0, 12, 13)
-        state(3)
-        thresh(2)
-        compare(0, 13, 14)
-        thresh(3)
-        compare(0, 14, 16)
-        op("V", lambda: v.tensor_scalar(T.ch[:], T.cu[:], -2048.0, None, Op.add), r=CUK, w=["ch"])
+        thresh(2, 4)
+        compare(0, 0, 16)
         keys(0, "V")
-        diffs(0)
-        tokens(0, 5)
-        tokens(5, 11)
-        compare(1, 0, 3)
-        signs(0, 0, "V")
+        diffs(0, 0)
+        diffs(0, 1)
+        cand(2)
+        gather(176, 200)
+        numbers(2)
+        state(2)
+        thresh(4, 5)
+        state(3)
+        thresh(5, 6)
+        repeat(0, 1)
+        repeat(0, 2)
+        half(0)
+        places(0, -1)
+        signs(0, 0, "A")
         signs(0, 1, "A")
-        compare(1, 3, 5)
+        gather(200, 256)
         places(0, 0)
         places(0, 1)
-        repeat(2, 0)
-        tokens(11, 16)
-        compare(1, 5, 10)
-        ranked(0)
-        compare(1, 10, 16)
-        keys(1, "A")
-        diffs(1)
-        signs(1, 0, "A")
-        RK = [("Rl", m) for m in range(3)]
-        for m in range(3):
-            lands(RK[m], "r%d%d" % (t, m))
-        wr["best"] = wr[RK[2]]
-        compare(2, 0, 16)
+        for p in (0, 1):
+            repeat(1, p)
+            repeat(2, p)
+        for p in range(4):
+            repeat(3, p)
+        if t == 0:
+            late(1)
+        tokens(0)
+        tokens(1)
+        ranked(0, "V")
         commit(-1)
-        keys(2, "A")
+        compare(1, 0, 16)
+        keys(1, "A")
+        diffs(1, 0)
+        diffs(1, 1)
+        half(1)
+        places(1, -1)
+        signs(1, 0, "A")
         signs(1, 1, "V")
         places(1, 0)
         places(1, 1)
-        diffs(2)
+        ranked(1, "A")
+        commit(0)
+        commit(1)
+        commit(11)
+        tokens(2)
+        commit(2)
+        commit(3)
+        compare(2, 0, 16)
+        keys(2, "A")
+        diffs(2, 0)
+        diffs(2, 1)
+        places(2, -1)
         signs(2, 0, "A")
-        signs(2, 1, "A")
-        commit(-2)
-        commit(-3)
-        repeat(1, 1)
-        ranked(1)
+        signs(2, 1, "V")
         places(2, 0)
         places(2, 1)
-        commit(0)
-        repeat(2, 1)
-        ranked(2)
-        commit(4)
-        commit(41)
-        send(rr, T.AW[:, RL + 208:RL + 257], R(208, 257), "r%d2" % t, [("R", 2), "bs"])
-        commit(5)
-        repeat(2, 2)
-        if t == S - 2:
-            top_of(R(0, 256), [("R", m) for m in range(3)], T.bq[:, 0:1], "bq")
-        commit(6)
-        scatter(0, 5, RK[0])
-        commit(7)
-        if t == S - 2:
-            op("V", lambda: v.tensor_scalar(T.X[:, 32 * t + 8:32 * t + 9], T.psl[:, 0:1], -28672.0, None, Op.add), r=["sel"], w=["X"], b=["psl"])
-            send(verifier(rr, t + 1), T.XC[:, 0:16], T.X[:, 32 * t:32 * t + 16], "x%d" % (t + 1), ["X"])
-        else:
-            send(verifier(rr, t + 1), T.Y[:, 272 * (t + 1):272 * (t + 1) + 8], T.X[:, 32 * t:32 * t + 8], "x%d" % (t + 1), ["X"])
-        lands(("Yr", t + 1), "x%d" % (t + 1))
+        best_lists()
+        ranked(2, "A")
+        root_mark()
+        ls = T.ls[:, 16 * t:16 * t + 16]
+        root(0, R(-8, 256), [("R", x) for x in range(3)] + [("Rz", t)], None, None)
+        root(1, None, None, ls, "ls")
+        send(rr, T.l0[:, 16 * t + 16:16 * t + 32], ls, "l%d" % (t + 1), ["ls"])
+        lands(("l0", t + 1), "l%d" % (t + 1))
         repeat(1, 2)
-        repeat(2, 3)
-        repeat(1, 3)
-        repeat(2, 4)
-        repeat(1, 4)
-        scatter(5, 11, RK[1])
-        scatter(11, 13, RK[1])
+        repeat(2, 2)
+        repeat(3, 4)
+        repeat(3, 5)
+        repeat(4)
+        repeat(5)
+        commit(4)
+        commit(5)
+        if t == S - 2:
+            lin("V", T.X[:, 16 * t + 8:16 * t + 9], T.psl[:, 0:1], 1.0, -float(TOP), ["sel"], [("X", t)], ["psl"])
+            send(verifier(rr, t + 1), T.XC[:, 0:16], T.X[:, 16 * t:16 * t + 16], "x%d" % (t + 1), [("X", t)])
+        else:
+            send(verifier(rr, t + 1), T.Y[:, 264 * (t + 1):264 * (t + 1) + 8], T.X[:, 16 * t:16 * t + 8], "x%d" % (t + 1), [("X", t)])
+        lands(("Yr", t + 1), "x%d" % (t + 1))
+        for c in range(0, 16, 2):
+            scatter(c)
+        for lv in range(4):
+            prepare(lv)
+        if t < 2:
+            late(2 + t)
+        RK = [("Rl", t, m) for m in range(3)]
 
     lands("YL0", "yn0")
     lands("XL", "fin")
@@ -759,6 +884,8 @@ def rank_program(g, core, T, topo):
     dma("S", T.yn[:, 176:256], T.YL[:, 176:256], "dout", r=["XL"])
     dma("A", T.yx[:], T.YL[:, 256:264], "dout", r=["XL"])
     dma("A", T.yt[:, 24:32], T.YL[0:128:16, 272:280], "dout", r=["XL"])
+    for nd in arrange(nodes):
+        emit(nd)
     for s in sorted(cnt):
         if max(waited[e].get(s, 0) for e in qu) < cnt[s]:
             need("S" if s == "dout" else "G", (s, cnt[s]))

@@ -10,25 +10,33 @@ DEP = [0]
 for _n in range(1, 32):
     DEP.append(DEP[PAR[_n]] + 1)
 ANC = [(PAR[n] if DEP[n] == 3 else PAR[PAR[n]]) - 10 for n in range(22, 32)]
-LV3 = [28, 29, 30, 31]
-LV2 = [PAR[n] for n in LV3] + list(range(22, 28))
-LV1 = list(range(10, 22)) + [PAR[n] for n in range(22, 28)]
-LV0 = list(range(0, 10)) + [1, 1, 2, 1, 2, 2, 3, 3, 4, 4]
-LEVELS = [LV0, LV1, LV2, LV3]
+L, U, B = 1, 2, 3
+LEVELS = [[(1, B), (0, L), (2, B), (3, U), (3, L), (4, B), (5, U), (6, L), (7, U), (8, L), (9, U), (9, U)],
+          [(10, L), (11, U), (14, L), (18, U), (15, U), (11, B), (18, L), (19, U), (12, L), (13, U), (16, L), (17, U), (20, L), (21, U)],
+          [(22, B), (23, U), (24, L), (25, U), (26, L), (27, U)],
+          [(28, L), (29, U), (30, L), (31, U)]]
+LOFF = [0, 96, 208, 256, 288]
+PC = [(0, 5), (5, 11), (11, 14), (14, 16)]
 
 
-def _blocks(lv, nxt):
-    have = [tuple(lv[i:i + 2]) for i in range(0, len(lv), 2)]
-    return [have.index((PAR[nxt[i]], PAR[nxt[i + 1]])) for i in range(0, len(nxt), 2)]
+def _end(lv, pair):
+    now = [None, None]
+    for i, (n, who) in enumerate(LEVELS[lv]):
+        now = [n if who & L else now[0], n if who & U else now[1]]
+        if tuple(now) == pair:
+            return 8 * i + 7
 
 
-TAKE = [_blocks(LV0, LV1) + [0] + list(range(5)) + [0], list(range(6)) + _blocks(LV1, LV2) + [0] * 5]
-LOFF = [0, 160, 304, 384, 416]
-FP, FD, FA, FT, FE = 416, 672, 928, 1008, 1040
-PC = [(0, 5), (5, 11), (11, 16)]
-OWN = [(0, 5, 0), (5, 11, 160), (11, 14, 336), (14, 16, 384)]
-POS = [(0, 96), (96, 200), (200, 256)]
-DD = [(0, 4, 160), (4, 10, 304), (10, 16, 416)]
+OWN = [[_end(lv, (2 * c, 2 * c + 1)) for c in range(*PC[lv])] for lv in range(4)]
+NEXT = [[_end(lv, (PAR[x[0]], PAR[y[0]])) for x, y in zip(LEVELS[lv + 1][0::2], LEVELS[lv + 1][1::2])] for lv in range(3)]
+MINE = [8, 0, 2, 0]
+THEN = [0, 6, 0]
+TAKE = [[(OWN[lv][x - MINE[lv]] if 0 <= x - MINE[lv] < len(OWN[lv]) else NEXT[lv][min(x - THEN[lv], len(NEXT[lv]) - 1)])
+         for x in range(16)] for lv in range(3)]
+FC, FP, FA, FT, FE, FD = 288, 576, 832, 912, 960, 960
+POS = [(0, 64), (64, 128), (128, 200), (200, 256)]
+BACK = [(0, 128), (128, 200), (200, 256)]
+DD = [(0, 4, 96), (4, 10, 208), (10, 16, 288)]
 RL = V + 32
 TOP = 28672
 QCUT = 2560
@@ -38,11 +46,12 @@ SCRATCH = {
     "Q": ("sbuf", [128, V], "int32"), "K": ("sbuf", [128, V], "bfloat16"), "AW": ("sbuf", [128, RL + 256], "int32"),
     "IO": ("sbuf", [128, V], "float32"), "IOb": ("sbuf", [128, 144], "bfloat16"),
     "xs": ("sbuf", [128, 8], "float32"), "IK": ("sbuf", [128, 256], "bfloat16"), "IG": ("sbuf", [128, 128], "bfloat16"),
-    "IJ": ("sbuf", [128, 256], "bfloat16"), "IS": ("sbuf", [128, 256], "bfloat16"),
+    "IJ": ("sbuf", [128, 256], "bfloat16"), "IS": ("sbuf", [128, FC], "bfloat16"),
+    "FX": ("sbuf", [128, FC], "bfloat16"), "RX": ("sbuf", [128, FC], "bfloat16"), "c0": ("sbuf", [128, 16], "uint16"),
     "BO": ("sbuf", [128, 128], "float16"), "BO16": ("sbuf", [128, 128], "float16"), "Ib": ("sbuf", [128, 128], "bfloat16"),
     "I16": ("sbuf", [128, 256], "bfloat16"), "GT": ("sbuf", [128, 256], "bfloat16"), "one": ("sbuf", [128, 2], "float16"),
-    "D1": ("sbuf", [128, 176], "bfloat16"), "F2": ("sbuf", [128, FP], "bfloat16"), "GM": ("sbuf", [128, 8], "float32"),
-    "RZ": ("sbuf", [128, 256], "bfloat16"), "sc": ("sbuf", [128, FP], "float32"), "GL": ("sbuf", [128, 4], "uint16"),
+    "D1": ("sbuf", [128, 2 * FC], "bfloat16"), "F2": ("sbuf", [128, FC], "bfloat16"), "GM": ("sbuf", [128, 8], "float32"),
+    "RZ": ("sbuf", [128, 256], "bfloat16"), "sc": ("sbuf", [128, FC], "float32"), "GL": ("sbuf", [128, 6], "uint16"),
     "AL": ("sbuf", [128, 6], "uint16"), "ok3": ("sbuf", [128, 80], "bfloat16"),
     "TM": ("sbuf", [128, 256], "bfloat16"), "LX": ("sbuf", [128, 16], "uint16"),
     "kp": ("sbuf", [128, 4], "float32"), "pi": ("sbuf", [128, 32], "int32"), "pj": ("sbuf", [128, 32], "int32"),
@@ -54,13 +63,13 @@ SCRATCH = {
     "cb": ("sbuf", [128, 128], "float16"), "hx": ("sbuf", [128, 16], "float32"), "cm": ("sbuf", [128, 2], "float32"),
     "TIE": ("sbuf", [128, 256], "bfloat16"),
     "DL": ("sbuf", [128, 16], "uint16"), "DL2": ("sbuf", [128, 6], "uint16"),
-    "ch": ("sbuf", [128, 256], "float16"), "F": ("sbuf", [128, FE], "bfloat16"),
+    "cf": ("sbuf", [128, 256], "float32"), "F": ("sbuf", [128, FD + 256], "bfloat16"),
     "PL": ("sbuf", [128, 16], "uint16"), "PL2": ("sbuf", [128, 12], "uint16"),
     "CX": ("sbuf", [128, 8], "uint16"), "SCL": ("sbuf", [128, 256], "float32"), "ISC": ("sbuf", [128, 264], "float32"),
     "bf": ("sbuf", [128, 4], "float32"), "M": ("sbuf", [128, 16], "float32"), "bl": ("sbuf", [128, 8], "uint16"),
     "w1": ("sbuf", [128, 128], "float16"), "l0": ("sbuf", [128, 64], "uint16"), "ls": ("sbuf", [128, 48], "uint16"),
     "wf": ("sbuf", [128, 176], "float32"), "wh": ("sbuf", [128, 176], "float16"),
-    "O0": ("sbuf", [128, 64], "uint16"), "O1": ("sbuf", [128, 64], "uint16"), "O2": ("sbuf", [128, 32], "uint16"),
+    "O": ("sbuf", [128, 256], "uint16"),
     "LM": ("sbuf", [128, 96], "uint16"), "Y": ("sbuf", [128, 4 * 264], "float32"),
     "cu": ("sbuf", [128, 256], "uint16"), "kn": ("sbuf", [128, 256], "float32"),
     "kc": ("sbuf", [128, 4096], "bfloat16"), "bits": ("sbuf", [128, 4096], "float16"),
@@ -78,8 +87,29 @@ SCRATCH = {
     "pa1": ("psum", [128, 512], "float32"), "pb1": ("psum", [128, 512], "float32"),
 }
 SEMAPHORES = (["sv", "sa", "sp", "sq", "sent", "dtok", "dx", "dkap", "dk", "dout", "yn0", "fin", "dq0", "dq1", "dq2", "sent0"]
-              + ["m%d%d" % (t, i) for t in range(S) for i in range(3)] + ["r%d%d" % (t, i) for t in range(3) for i in range(3)]
+              + ["m%d%d" % (t, i) for t in range(S) for i in range(4)] + ["c0"] + ["r%d%d" % (t, i) for t in range(3) for i in range(3)]
               + ["x%d" % t for t in range(S)] + ["l%d" % t for t in range(1, S)])
+
+
+STEP = """pick 0, emitted, listed 0, pick 1, listed 1, pick 2, cand 0 A, listed 2, numbers 0, state 0, gather 0 24 A,
+gather 24 40 V, gather 40 64 A, thresh 0 2, pick 3, cand 1 A, numbers 1, listed 3, once 0,
+repeat 0 0, repeat 1 0, repeat 2 0, repeat 0 1, repeat 1 1, repeat 2 1, repeat 3 0, repeat 3 1, repeat 3 2, repeat 3 3,
+repeat 4 0, repeat 5 0, gather 64 80 A, state 1, gather 80 104 A, gather 104 128 A, thresh 2 4,
+compare 0 0 16, keys 0 V, diffs 0 0, diffs 0 1, half 0 A, gather 128 152 A, gather 152 176 A, cand 2 A, numbers 2, state 2,
+thresh 4 5, compare 1 0 16, signs 0 2 V, places 0 0, places 0 1, keys 1 V, diffs 1 0, diffs 1 1, gather 176 200 A, ranked 0,
+half 1 A, compare 2 0 16, signs 1 2 A, places 1 0, places 1 1, cand 3 A, gather 200 224 A, gather 224 256 A, numbers 3,
+state 3, thresh 5 6, keys 2 V, diffs 2 0, diffs 2 1, ranked 1, half 2 A, compare 3 0 16, signs 2 0 A, signs 2 1 A,
+places 2 0, places 2 1, tokens 0 A, tokens 1 A, once 1, commit -1, commit 0, commit 1, commit 11, keys 3 V, ranked 2,
+diffs 3 0, diffs 3 1, tokens 2 A, tokens 3 A, commit 2, half 3 A, signs 3 0 A, signs 3 1 V, places 3 0, places 3 1,
+commit 3, best, ranked 3, commit 4, commit 5, passed, mark, roots 0, roots 1,
+repeat 0 2, repeat 0 3, repeat 1 2, repeat 2 2, repeat 3 4, repeat 3 5, repeat 3 6, repeat 3 7, repeat 4 1, repeat 5 1,
+scatter 0, scatter 2, scatter 4, scatter 6, scatter 8, scatter 10, scatter 12, scatter 14,
+prepare 0, prepare 1, prepare 2, prepare 3, once 2"""
+LAST = """chain 0 0, pick 0, commit -1, chain 0 1, emitted, listed 0, chain 0 2, pick 1, chain 0 3, chain 1 0, listed 1, chain 1 1,
+pick 2, chain 1 2, tokens 0 A, listed 2, chain 1 3, chain 2 0, numbers 0, pick 3, chain 2 1, state 0, tokens 1 A, numbers 1,
+chain 2 2, listed 3, chain 2 3, chain 3 0, commit 0, numbers 2, chain 3 1, tokens 2 A, commit 1, state 1, chain 3 2,
+unscale 2 3, commit 11, state 2, chain 3 3, chain 4 0, unscale 0 1, tokens 3 A, numbers 3, commit 2, chain 4 1, unscale 3 4,
+state 3, unscale 1 2, commit 3, results 0, unscale 4 5, chain 4 2, results 1, chain 4 3, results 2"""
 
 
 def runs(vals):
@@ -102,7 +132,7 @@ def ramps(vals):
     return out
 
 
-CYCLE, WAKE, ISSUE, FLIGHT, PER_BYTE = 0.00091, 0.1, 0.35, 1.35, 0.0013
+CYCLE, WAKE, ISSUE, FLIGHT, PER_BYTE = 0.00104, 0.115, 0.35, 1.35, 0.0013
 TURNS = 2
 ITEM = {"float32": 4, "int32": 4, "bfloat16": 2, "float16": 2, "uint16": 2}
 
@@ -126,10 +156,10 @@ def cost(name, fn, args, kw):
         rate = 2.0
     if name in ("copy", "scan") and all(ITEM[x[2]] == 2 for x in sides):
         rate = 0.5
-    return (0.06 if name == "act" else 0.03) + max(64, rate * size(args[1 if name == "reduce" else 0])) * CYCLE
+    return (0.02 if name == "act" else 0.005) + max(64, rate * size(args[1 if name == "reduce" else 0])) * CYCLE
 
 
-def arrange(nodes):
+def arrange(nodes, tables):
     wr, rd, bank, far = {}, {}, {}, {nd["far"]: i for i, nd in enumerate(nodes) if "far" in nd}
     deps, kids, turns = [], [[] for nd in nodes], []
     for i, nd in enumerate(nodes):
@@ -186,7 +216,10 @@ def arrange(nodes):
                 if not left[k]:
                     ready.append(k)
         return end
-    best, chain = None, {i: -i for i in chain}
+    best, rank = None, {}
+    for i in chain:
+        rank[i] = max([-i if i >= tables else -1e9] + [rank[k] + 1e-6 for k in kids[i]])
+    chain = rank
     for turn in range(TURNS):
         end = place(deps, kids, gap, lambda i: 0.0, chain)
         total = max(end[i] + nodes[i]["lag"] for i in end)
@@ -282,18 +315,18 @@ def rank_program(g, core, T, topo):
     def dma(e, out, in_, sem, r=(), w=(), lag=1.4, turn=0):
         nodes.append(dict(e=e, turn=turn, calls=[("dma_start", qu[e].dma_start, (out, in_), {})], r=r, w=w, b=(), sem=sem, busy=0.05, lag=lag))
 
-    def send(to, out, in_, sem, r, local="sent", w=()):
+    def send(to, out, in_, sem, r, local="sent", w=(), turn=0):
         dst = T.cores[to]
         rid, pid = topo.addr(dst)[:2]
         mask = sum(1 << e for e in topo.engines(core, dst)[:NE])
-        nodes.append(dict(e="G", calls=[("remote_dma", g.remote_dma, (out, in_, T.sem[sem], T.sem[local], pid, rid, mask), {})],
+        nodes.append(dict(e="G", turn=turn, calls=[("remote_dma", g.remote_dma, (out, in_, T.sem[sem], T.sem[local], pid, rid, mask), {})],
                           r=r, w=w, b=(), sem=local, far=sem, busy=ISSUE, lag=FLIGHT + size(in_) * ITEM[SCRATCH[in_.name][2]] * PER_BYTE))
 
     def lands(key, sem):
         nodes.append(dict(e="L", calls=[], r=(), w=[key], b=(), sem=sem, busy=0.0, lag=0.0))
 
     C = lambda i: T.C[:, i:i + 1]
-    KF, G16, SC, NB, NK, KB, Z15, PF, GI, ZC, SP0, BC, NKP, KT, KR, SP1, KX = range(17)
+    KF, G16, SC, NB, NK, KB, Z15, PF, GI, ZC, SP0, BC, NKP, KT, KR, SP1, KX, HC, UP, KS = range(20)
 
     def lin(e, out, in_, mul, add, r, w, b=()):
         if e == "A":
@@ -325,7 +358,7 @@ def rank_program(g, core, T, topo):
     iota(T.IO[:, 0:256], [[1, 256]], "IO0")
     op("G", lambda: gp.iota(T.pi[:, 16:32], [[-1, 16]], 16, 1), w=["pi2"])
     iota(T.IJ[:], [[1, 32], [0, 8]], "IJ")
-    iota(T.IK[:], [[0, 16], [1, 16]], "IK")
+    iota(T.IS[:], [[0, 36], [1, 8]], "IS")
     iota(T.IG[:], [[16, 8], [0, 16]], "IG")
     op("V", lambda: v.memset(T.M[:], 0.0), w=["M"])
     op("V", lambda: v.memset(T.bf[:], 0.5), w=["bf"])
@@ -337,10 +370,10 @@ def rank_program(g, core, T, topo):
     op("V", lambda: v.tensor_copy(T.IOb[:], T.IO[:, 0:144]), r=["IO0"], w=["IOb"])
     op("V", lambda: v.tensor_scalar(T.CJ[:], T.pj[:, 16:32], C(G16), None, Op.add), r=["pj2", "C0"], w=["CJ"])
     for col, src, mul, add in ((Z15, G16, 1.0, 15.0), (KT, KF, 4096.0, -2048.0), (ZC, KF, -4096.0, 2048.0), (GI, G16, 0.0625, 0.0),
-                               (BC, NB, -0.125, 1.0), (KR, KF, -4096.0, 32768.0), (NK, KF, -4096.0, 0.0), (KB, KF, -1.0, -121.0),
+                               (BC, NB, -0.125, 1.0), (HC, NB, -0.125, 2.0), (UP, NB, 0.125, 0.0), (KS, KF, -4096.0, 30720.0), (KR, KF, -4096.0, 32768.0), (NK, KF, -4096.0, 0.0), (KB, KF, -1.0, -121.0),
                                (SP0, KF, 1.0, float(V)), (SP1, KF, 1.0, float(V + 16))):
         lin("A", C(col), C(src), mul, add, ["C0"], [("C", col)])
-    CK = ["C0", "C1"] + [("C", c) for c in (Z15, KT, ZC, GI, BC, KR, NK, KB, SP0, SP1)]
+    CK = ["C0", "C1"] + [("C", c) for c in (Z15, KT, ZC, GI, BC, HC, UP, KS, KR, NK, KB, SP0, SP1)]
 
     def shifts(j0, j1):
         for j in range(j0, j1):
@@ -355,49 +388,50 @@ def rank_program(g, core, T, topo):
        r=[("DM", x) for x in range(9, 16)], w=["DMb"])
     shifts(0, 1)
     DK = [("DM", 0), "DMa", "DMb"]
-    rows = [ROW[n] for lv in LEVELS for n in lv]
+    rows = [ROW[n] for lv in LEVELS for n, who in lv]
     todo = [(FP + 8 * lo, FP + 8 * hi, T.IJ, 8 * p, 8 * d) for lo, hi, p, d in ramps(PAR)]
     todo += [(FD + 8 * lo, FD + 8 * hi, T.IJ, 16 * p, 0) for lo, hi, p in runs(DEP)]
     todo += [(FA + 8 * lo, FA + 8 * hi, T.IJ, 8 * p, 8 * d) for lo, hi, p, d in ramps(ANC)]
-    todo += [(FT + lo, FT + hi, T.IOb, 16 * p + 15, 16 * d) for lo, hi, p, d in ramps(TAKE[0] + TAKE[1])]
-    nsel = len(todo)
+    todo += [(FT + lo, FT + hi, T.IOb, p, d) for lo, hi, p, d in ramps(TAKE[0] + TAKE[1] + TAKE[2])]
     todo += [(8 * lo, 8 * hi, T.IJ, 4096 * p - 30720, 4096 * d) for lo, hi, p, d in ramps(rows)]
-    FK = []
+    todo += [(FC + 8 * lo, FC + 8 * hi, T.IJ, p, d) for lo, hi, p, d in ramps([who for lv in LEVELS for n, who in lv])]
     for i, (lo, hi, src, val, d) in enumerate(todo):
-        FK.append(("F", i))
-        lin("V" if i % 3 == 2 else "A", T.F[:, lo:hi], src[:, 0:hi - lo], float(d), float(val), ["IJ", "IOb"], [FK[-1]])
+        lin("VA"[i % 2], T.F[:, lo:hi], src[:, 0:hi - lo], float(d), float(val), ["IJ", "IOb"], [("F", lo)])
+    fk = lambda lo, hi: [("F", x[0]) for x in todo if lo <= x[0] < hi]
+    FK = fk(0, FP)
     cmp(T.Zb[:], T.IOb[:], C(Z15), 1.0, Op.is_equal, ["IOb"] + CK, ["Zb"])
 
-    def select():
-        ins = None
-        for i in range(16):
-            ins = pe.matmul(T.ps1[:, 0:39], T.Zb[:, 15 - i:143 - i], T.F[:, FP + i:FE:16], i == 0, i == 15)
-        return ins
-    op("P", select, r=FK[:nsel] + ["Zb"], w=["tab"], b=["ps1"])
+    def select(lo, hi, outs):
+        op("P", lambda: [pe.matmul(T.ps1[:, 0:(hi - lo) // 16], T.Zb[:, 15 - i:143 - i], T.F[:, lo + i:hi:16], i == 0, i == 15) for i in range(16)],
+           r=fk(lo, hi) + ["Zb"], w=[("S", 1)], b=["ps1"])
+        for dst, c0, c1, s2, key in outs:
+            lin("V", dst, T.ps1[:, c0:c1], 0.0625, s2, [("S", 1)] + CK, [key], ["ps1"])
+    select(FT, FE, [(T.GL[:, 0:6:2], 0, 3, 0.0, "GL")])
     cmp(T.GM[:], T.IO[:, 0:8], C(GI), 16.0, Op.is_equal, ["IO0"] + CK, ["GM"])
     lin("V", T.one[:], T.IO[:, 0:2], 0.0, 1.0, ["IO0"], ["one"])
     lin("V", T.AW[:, V:RL], T.IO[:, 0:32], 0.0, C(ZC), ["IO0"] + CK, ["spare"])
     cmp(T.Ib[:], T.IOb[:, 0:128], C(PF), 1.0, Op.is_equal, ["IOb"] + CK, ["Ib"])
-    cmp(T.D1[:], T.IK[:, 0:176], C(KF), -65536.0, Op.not_equal, ["IK"] + CK, ["D1"])
-    cmp(T.RZ[:], T.IK[:], 0.0, -1048576.0, Op.is_equal, ["IK"], ["RZ"])
     cmp(T.BO[:], T.IG[:], C(G16), 1.0, Op.is_equal, ["IG"] + CK, ["BO"])
-    lin("A", T.F2[:], T.F[:, 0:FP], 1.0, C(KR), FK + CK, ["F2"])
+    lin("A", T.F2[:], T.F[:, 0:FC], 1.0, C(KR), FK + CK, ["F2"])
+    cmp(T.D1[:, 0:FC], T.IS[:], C(SC), -65536.0, Op.not_equal, ["IS"] + CK, ["D1"])
+    cmp(T.D1[:, FC:2 * FC], T.F[:, FC:FP], C(HC), -65536.0, Op.is_equal, FK + CK, ["D2"])
+    op("V", lambda: v.memset(T.RX[:], 0.0), w=["RX"])
+    cmp(T.RX[:, 0:FC:8], T.F[:, FC:FP:8], C(HC), -1048576.0, Op.not_equal, FK + CK, ["RX"])
+    op("P", lambda: [pe.matmul(T.ps0[:, 0:FC], T.Ib[:], x, i == 0, i == 2) for i, x in enumerate((T.F[:, 0:FC], T.D1[:, 0:FC], T.D1[:, FC:2 * FC]))],
+       r=["Ib", "D1", "D2"] + FK, w=["fx"], b=["ps0"])
+    lin("A", T.FX[:], T.ps0[:, 0:FC], 1.0, 0.0, ["fx"], ["FX"], ["ps0"])
     PB = [T.pa1, T.pb1, T.pa0, T.pb0]
 
     def prepare(lv):
-        n, lo = 8 * len(LEVELS[lv]), LOFF[lv]
-
-        def mm():
-            pe.matmul(PB[lv][:, 0:n], T.Ib[:], T.F[:, lo:lo + n], True, False)
-            return pe.matmul(PB[lv][:, 0:n], T.Ib[:], T.D1[:, 0:n], False, False)
-        op("P", mm, r=["Ib", "D1"] + FK, w=[PB[lv].name], b=[PB[lv].name])
+        op("P", lambda: pe.matmul(PB[lv][:, 0:LOFF[lv + 1] - LOFF[lv]], T.Ib[:], T.FX[:, LOFF[lv]:LOFF[lv + 1]], True, False),
+           r=["Ib", "FX"], w=[PB[lv].name], b=[PB[lv].name])
 
     def best_lists():
         lin("V", T.bl[:], T.GM[:], T.bf[:, 0:1], C(SC), ["bf", "GM"] + CK, ["bl"])
         lin("V", T.bq[:, 0:1], T.bf[:, 0:1], 16.0, C(SC), ["bf"] + CK, ["bq"])
 
     def root_mark():
-        op("V", lambda: v.tensor_scalar(T.M[:, 0:1], T.bq[:, 0:1], float(RL - 8 + TOP), C(BC), Op.add, Op.mult), r=["bq", "M"] + CK, w=["M0"])
+        op("V", lambda: v.tensor_scalar(T.M[:, 0:1], T.bq[:, 0:1], float(RL - 8 + TOP), C(UP), Op.add, Op.mult), r=["bq", "M"] + CK, w=["M0"])
 
     def root(i, win, keys, out, okey):
         if i == 0:
@@ -410,22 +444,27 @@ def rank_program(g, core, T, topo):
     root(0, T.AW[:, RL - 8:RL + 8], ["Rl", "spare"], None, None)
     for lv in range(4):
         prepare(lv)
-    for dst, lo, hi, s2, key in ((T.GL[:, 0:4:2], 37, 39, 0.0, "GL"), (T.PL[:], 0, 16, C(SC), "PL"), (T.PL2[:, 0:11], 5, 16, C(SC), "PL2"),
-                                 (T.DL[:], 16, 32, C(SC), "DL"), (T.DL2[:, 0:5], 27, 32, C(SC), "DL2"), (T.AL[:, 0:5], 32, 37, C(SC), "AL")):
-        lin("V", dst, T.ps1[:, lo:hi], 0.0625, s2, ["tab"] + CK, [key], ["ps1"])
+    select(FP, FT, [(T.PL[:], 0, 16, C(SC), "PL"), (T.PL2[:, 0:11], 5, 16, C(SC), "PL2"), (T.AL[:, 0:5], 16, 21, C(SC), "AL")])
     root(1, None, None, T.l0[:, 0:16], ("l0", 0))
     RK = ["Rl"]
     cmp(T.Zh[:], T.IOb[:], C(Z15), 1.0, Op.is_equal, ["IOb"] + CK, ["Zh"])
     cmp(T.Ih[:], T.IOb[:, 0:128], C(PF), 1.0, Op.is_equal, ["IOb"] + CK, ["Ih"])
     cmp(T.I16[:, 0:128], T.IOb[:, 0:128], C(PF), 16384.0, Op.is_equal, ["IOb"] + CK, ["I16"])
     cmp(T.I16[:, 128:256], T.IOb[:, 0:128], C(PF), 32768.0, Op.is_equal, ["IOb"] + CK, ["I32"])
+    op("V", lambda: v.tensor_tensor(T.IK[:, 0:128], T.IOb[:, 0:128], T.IG[:], Op.subtract), r=["IOb", "IG"], w=["IK0"])
+    op("V", lambda: v.tensor_copy(T.IK[:, 128:256], T.IK[:, 0:128]), r=["IK0"], w=["IK"])
     cmp(T.GT[:], T.IK[:], C(KF), 0.5, Op.is_gt, ["IK"] + CK, ["GT"])
     lin("A", C(KX), C(BC), 8.0, C(SC), CK, ["KX"])
     for n in SWAP:
         cmp(T.GT[:, 8 * n:8 * n + 16], T.IK[:, 8:24], C(KX), 0.5, Op.is_gt, ["IK", "KX", "GT"], [("GT", n)])
-    for c0, c1, p in OWN:
-        lin("V", T.LX[:, c0:c1], T.IO[:, 0:c1 - c0], 16.0, float(p + 15), ["IO0"], [("LX", c0)])
-    LXK = [("LX", x[0]) for x in OWN]
+    cmp(T.RZ[:], T.IK[:], 0.0, -1048576.0, Op.is_equal, ["IK"], ["RZ"])
+    LXK = []
+    for c0, c1, p, d in ramps([LOFF[lv] + x for lv in range(4) for x in OWN[lv]]):
+        LXK.append(("LX", c0))
+        lin("A", T.LX[:, c0:c1], T.IO[:, 0:c1 - c0], float(d), float(p), ["IO0"], [LXK[-1]])
+    cmp(T.CT[:, 512:768], T.IS[:, 0:256], C(SC), -128.0, Op.not_equal, ["IS"] + CK, ["CTm"])
+    lin("V", T.TM[:], T.IJ[:], 0.5, 0.0, ["IJ"], ["TM0", "TM1"])
+    op("V", lambda: v.tensor_tensor(T.CT[:, 0:256], T.TM[:], T.CT[:, 512:768], Op.add), r=["TM0", "TM1", "CTm"], w=["CTw"])
     cmp(T.BOb[:, 0:128], T.IG[:], C(G16), 1.0, Op.is_equal, ["IG"] + CK, ["BOb0"])
     cmp(T.BOb[:, 128:256], T.IG[:], C(G16), 16.0, Op.is_equal, ["IG"] + CK, ["BOb"])
     for i, n in enumerate((256, 512, 1024, 2048)):
@@ -438,13 +477,10 @@ def rank_program(g, core, T, topo):
     SK, IK = [("SCL", d) for d in range(5)], [("ISC", d) for d in range(5)]
 
     def late(i):
-        if i == 0:
-            iota(T.IS[:], [[0, 32], [1, 8]], "IS")
         if i == 1:
             for lo, hi, d in runs(DEP):
-                lin("A", T.CT[:, 8 * lo:8 * hi], T.IJ[:, 8 * lo:8 * hi], 0.5, 0.5 - 16 * d, ["IJ"], [("CT", d)])
+                lin("A", T.CT[:, 8 * lo:8 * hi], T.CT[:, 8 * lo:8 * hi], 1.0, 0.5 - 16 * d, ["CTw"], [("CT", d)])
                 lin("A", T.ISC[:, 8 * lo + (8 if d else 0):8 * hi + 8], T.IO[:, 0:8 * (hi - lo) + (0 if d else 8)], 0.0, 0.5 ** d, ["IO0"], [("ISC", d)])
-            cmp(T.CT[:, 512:768], T.IS[:], C(SC), -128.0, Op.not_equal, ["IS"] + CK, ["CTm"])
             for x in range(3):
                 lin("A", T.R[:, 264 * x:264 * x + 8], T.IO[:, 0:8], 0.0, C(ZC), ["IO0"] + CK, [("Rz", x)])
         if i == 2:
@@ -452,26 +488,28 @@ def rank_program(g, core, T, topo):
             lin("A", C(NKP), T.kp[:, 0:1], -1.0, 0.0, ["kp"], ["NKP"])
             lin("A", T.TM[:, 128:256], T.IK[:, 0:128], -1.0, 15.0, ["IK"], ["TM1"])
             lin("A", T.TM[:, 0:128], T.TM[:, 0:128], -512.0, 0.0, ["TM0"], ["TM0"])
-            lin("A", T.CT[:, 256:512], T.F[:, FD:FA], -0.9375, 0.0, FK, ["CTl"])
+            for lo, hi, d in runs(DEP):
+                lin("A", T.CT[:, 256 + 8 * lo:256 + 8 * hi], T.CT[:, 512 + 8 * lo:512 + 8 * hi], 1.0, -15.0 * d, ["CTm"], [("CTl", d)])
             lin("A", T.CX[:], T.IO[:, 0:8], 1.0, 0.0, ["IO0"], ["CX"])
         if i == 3:
+            select(FD, FD + 256, [(T.DL[:], 0, 16, C(SC), "DL"), (T.DL2[:, 0:5], 11, 16, C(SC), "DL2")])
             op("V", lambda: v.tensor_tensor(T.TIE[:, 0:128], T.TM[:, 0:128], T.TM[:, 128:256], Op.add), r=["TM0", "TM1"], w=["TIE0"])
             lin("A", T.TIE[:, 128:256], T.TIE[:, 0:128], 1.0, 0.5, ["TIE0"], ["TIE"])
             lin("A", T.BO16[:], T.BOb[:, 128:256], 1.0, 0.0, ["BOb"], ["BO16"])
-    CTK = [("CT", d) for d in range(5)] + ["CTm"]
 
+    tables = len(nodes)
     for t in range(S):
         q, rr = verifier(rank, t), drafter(rank, t)
         last = t == S - 1
-        o0, o1, o2 = T.O0, T.O1, T.O2
         l0 = T.l0[:, 16 * t:16 * t + 16]
-        outs = [o0[:, 16 * t:16 * t + 16], o1[:, 16 * t:16 * t + 16], o2[:, 8 * t:8 * t + 5], o2[:, 8 * t + 5:8 * t + 7]]
-        lists = [l0[:, 0:10], o0[:, 16 * t:16 * t + 9], o1[:, 16 * t + 6:16 * t + 11], o2[:, 8 * t:8 * t + 2]]
-        mine = [o0[:, 16 * t + 10:16 * t + 15], o1[:, 16 * t:16 * t + 6], o2[:, 8 * t + 2:8 * t + 7]]
-        mineK = [[("L", 1)], [("L", 2)], [("L", 3), ("L", 4)]]
-        lm = lambda c0, c1: T.LM[:, 24 * t + c0 + (c0 > 0):24 * t + c1 + (c0 > 0)]
-        mk = lambda c: ("LM", t, 0 if c < 5 else 1 if c < 11 else 2)
-        for i in range(3):
+        O = lambda lv, lo, n: T.O[:, 64 * t + 16 * lv + lo:64 * t + 16 * lv + lo + n]
+        outs = [O(0, 0, 16), O(1, 0, 16), O(2, 0, 16), O(3, 0, 2)]
+        lists = [l0[:, 0:6]] + [O(lv, THEN[lv], len(NEXT[lv])) for lv in range(3)]
+        mine = [O(lv, MINE[lv], len(OWN[lv])) for lv in range(4)]
+        mineK = [[("L", lv + 1)] for lv in range(4)]
+        lm = lambda c0, c1: T.LM[:, 24 * t + c0 + (c0 > 0) + (c0 > 13):24 * t + c1 + (c0 > 0) + (c0 > 13)]
+        mk = lambda c: ("LM", t, [c < hi for lo, hi in PC].index(True))
+        for i in range(4):
             lands(("LM", t, i), "m%d%d" % (t, i))
 
         def pick(lv):
@@ -484,13 +522,11 @@ def rank_program(g, core, T, topo):
 
         def listed(lv):
             n, lo = 8 * len(LEVELS[lv]), LOFF[lv]
-            op("V", lambda: v.tensor_tensor_scan(T.sc[:, lo:lo + n], T.RZ[:, 0:n], PB[lv][:, 0:n], 0.0, Op.add, Op.max),
-               r=[PB[lv].name, "RZ"], w=[("sc", lv)], b=[PB[lv].name])
-            src = ind(T.sc[:, lo:lo + n], T.GL[:, 2 * lv:2 * lv + 1]) if lv < 2 else T.sc[:, lo + 15:lo + n:16]
+            op("V", lambda: v.tensor_tensor_scan(T.sc[:, lo:lo + n], T.RX[:, lo:lo + n], PB[lv][:, 0:n], 0.0, Op.add, Op.max),
+               r=[PB[lv].name, "RX"], w=[("sc", lv)], b=[PB[lv].name])
+            src = ind(T.sc[:, lo:lo + n], T.GL[:, 2 * lv:2 * lv + 1]) if lv < 3 else T.sc[:, lo + 15:lo + n:16]
             op("V", lambda: v.tensor_scalar(outs[lv], src, 2048.0, None, Op.add), r=[("sc", lv), "GL"], w=[("L", lv + 1)])
-            if lv != 2:
-                p = min(lv, 2)
-                send(q, lm(PC[p][0], PC[p][1]), mine[p], "m%d%d" % (t, p), mineK[p], *(("sent0", ["left"]) if (t, lv) == (0, 3) else ()))
+            send(q, lm(*PC[lv]), mine[lv], "m%d%d" % (t, lv), mineK[lv] + (DK if t == 0 else []), *(("sent0", ["left"]) if (t, lv) == (0, 3) else ()))
 
         def emitted():
             if t > 0:
@@ -504,7 +540,7 @@ def rank_program(g, core, T, topo):
             if i == 0:
                 lo, hi = 16 * PC[p][0], 16 * PC[p][1]
                 op("A", lambda: a.activation(T.Bo[:, lo:hi], ind(T.IO[:], mine[p]), Fn.Identity, bias=-2048.0), r=mineK[p] + IOK, w=[("Bo", p)])
-            bk = [("Bo", x) for x in range(p + 1)]
+            bk = [("Bo", x) for x in range(p + 1 + p // 2)]
             if i == 1:
                 op("V", lambda: v.tensor_tensor(T.ed[:, 16 * c0:16 * c1], ind(T.sc[:, 0:end], T.LX[:, c0:c1]), T.Bo[:, 16 * c0:16 * c1], Op.is_equal),
                    r=sk + bk + LXK, w=[("ed", 0, p)])
@@ -512,40 +548,41 @@ def rank_program(g, core, T, topo):
                 op("V", lambda: v.tensor_tensor(T.ed[:, 256 + 16 * c0:256 + 16 * c2], ind(T.sc[:, 0:end], T.LX[:, c0:c2]),
                                                 T.Bo[:, 16 * c0 + 16:16 * c2 + 16], Op.is_equal), r=sk + bk + LXK, w=[("ed", 1, p)])
             if i == 3:
-                lo, hi, lhs, rhs, key = ((0, 256, T.I16[:, 0:128], T.GT[:], [("GT", n) for n in SWAP]),
-                                         (0, 160, T.I16[:, 0:128], T.ed[:, 0:160], [("ed", 0, 0), ("ed", 0, 1)]),
-                                         (0, 160, T.I16[:, 128:256], T.ed[:, 256:416], [("ed", 1, 0), ("ed", 1, 1)]),
-                                         (0, 256, T.Ih[:], T.Bo[:], [("Bo", x) for x in range(3)]),
-                                         (160, 256, T.I16[:, 0:128], T.ed[:, 160:256], [("ed", 0, 2)]),
-                                         (160, 240, T.I16[:, 128:256], T.ed[:, 416:496], [("ed", 1, 2)]))[p]
-                op("P", lambda: pe.matmul(T.pb0[:, lo:hi], lhs, rhs, p == 0, p == 5), r=key + ["I16", "I32", "Ih"], w=["pb0"], b=["pb0"])
+                x, part = p % 4, p // 4
+                lo, hi = ((0, 160), (160, 240 if x == 3 else 256))[part]
+                lhs, rhs, key = ((T.I16[:, 0:128], T.GT[:, lo:hi], [("GT", n) for n in SWAP]),
+                                 (T.Ih[:], T.Bo[:, lo:hi], [("Bo", y) for y in range(part, 2 + 2 * part)]),
+                                 (T.I16[:, 0:128], T.ed[:, lo:hi], [("ed", 0, y) for y in range(2 * part, 2 + part)]),
+                                 (T.I16[:, 128:256], T.ed[:, 256 + lo:256 + hi], [("ed", 1, y) for y in range(2 * part, 2 + part)]))[x]
+                op("P", lambda: pe.matmul(T.pb1[:, lo:hi], lhs, rhs, x == 0, x == 3), r=key + ["I16", "I32", "Ih"], w=["pb1"], b=["pb1"])
+            lo, hi = ((0, 160), (160, 256))[p % 2]
             if i == 4:
-                op("V", lambda: v.tensor_tensor_scan(T.ds[:], T.RZ[:], T.pb0[:, 0:256], 0.0, Op.add, Op.max), r=["pb0", "RZ"], w=["ds"], b=["pb0"])
+                op("V", lambda: v.tensor_tensor_scan(T.ds[:, lo:hi], T.RZ[:, lo:hi], T.pb1[:, lo:hi], 0.0, Op.add, Op.max), r=["pb1", "RZ"], w=[("ds", p)], b=["pb1"])
             if i == 5:
                 for h in range(2):
-                    op("V", lambda: v.tensor_scalar(T.OF[:, h:16:2], T.ds[:, 16 * h + 15:256:32], 2048.0 - 16384.0, C(SP1 if h else SP0), Op.add, Op.min),
-                       r=["ds"] + CK, w=[("OF", h)])
+                    op("V", lambda: v.tensor_scalar(T.OF[:, lo // 16 + h:hi // 16:2], T.ds[:, lo + 16 * h + 15:hi:32], 2048.0 - 16384.0, C(SP1 if h else SP0), Op.add, Op.min),
+                       r=[("ds", p)] + CK, w=[("OF", p, h)])
 
         def scatter(c):
-            keys = [("Rl", t, m) for m in range(3) if POS[m][0] < 16 * c + 32 and 16 * c < POS[m][1]]
+            keys = [("Rl", t, m) for m in range(3) if BACK[m][0] < 16 * c + 32 and 16 * c < BACK[m][1]]
             op("V", lambda: v.tensor_copy(ind(T.AW[:, 0:RL], T.OF[:, c:c + 2]), T.AW[:, RL + 16 * c:RL + 16 * c + 32]),
-               r=keys + [("OF", 0), ("OF", 1)], w=["A", "A0", "spare"])
+               r=keys + [("OF", c // 10, 0), ("OF", c // 10, 1)], w=["A", "A0", "spare"])
 
         qwin, QK = (T.AW[:, 0:V], ["A", "A0"]) if t == 0 else (T.Q[:], ["Q"])
         y0 = 264 * t + 8
         Y = lambda j0, j1: T.Y[:, y0 + j0:y0 + j1]
         R = lambda j0, j1: T.R[:, y0 + j0:y0 + j1]
-        piece = lambda j: 0 if j < 80 else 1 if j < 176 else 2
-        KCK = [[], [], []]
-        DB = [(T.pa0, T.pb0), (T.pa1, T.pb1), (T.pa0, T.pb1)]
+        piece = lambda j: mk(j // 16)[2]
+        KCK = [[] for x in POS]
+        DB = [((T.pa0, 0), (T.pa0, 256)), ((T.pa1, 0), (T.pa1, 256)), ((T.pa0, 0), (T.pb0, 0)), ((T.pa1, 0), (T.pb0, 0))]
 
         def cand(p, e="A"):
             c0, c1 = PC[p]
             lin(e, T.cu[:, 16 * c0:16 * c1], ind(qwin, lm(c0, c1)), 1.0, 0.0, QK + [mk(c0)], [("cu", p)])
 
         def half(m, e="A"):
-            lo, hi = (0, POS[0][1]) if m == 0 else (POS[0][1], 256)
-            lin(e, T.ch[:, lo:hi], T.cu[:, lo:hi], 1.0, -2048.0, [("cu", p) for p in range(piece(hi - 1) + 1)], [("ch", m)])
+            lo, hi = POS[m]
+            lin(e, T.cf[:, lo:hi], T.cu[:, lo:hi], 1.0, C(KS), [("cu", p) for p in range(piece(hi - 1) + 1)] + CK, [("cf", m)])
 
         def gather(j0, j1, e="A"):
             lin(e, T.kc[:, 16 * j0:16 * j1], ind(T.K[:], T.cu[:, j0:j1]), 1.0, 0.0, ["K", ("cu", piece(j0))], [("kc", j0)])
@@ -558,7 +595,7 @@ def rank_program(g, core, T, topo):
 
         def state(i):
             j0, j1, win, lst, kk = ((0, 80, T.XC[:, 0:8] if last else Y(-8, 0), T.PL[:, 0:5], 0), (80, 176, Y(0, 80), T.PL2[:, 0:6], 1),
-                                    (176, 224, Y(0, 176), T.PL2[:, 6:9], 2), (224, 256, Y(0, 224), T.PL[:, 14:16], 2))[i]
+                                    (176, 224, Y(0, 176), T.PL2[:, 6:9], 2), (224, 256, Y(0, 224), T.PL[:, 14:16], 3))[i]
             op("V", lambda: v.tensor_tensor(Y(j0, j1), ind(win, lst), T.kn[:, j0:j1], Op.add),
                r=["PL", "PL2", ("kn", kk), ("Y", i - 1) if i else ("Yr", t)], w=[("Y", i)])
 
@@ -589,24 +626,22 @@ def rank_program(g, core, T, topo):
         def diffs(m, h):
             j0, j1 = POS[m]
             n = j1 - j0
-            pd = DB[m][h]
+            pd, o = DB[m][h]
 
             def mm():
-                ins = None
                 for jj in range(4):
                     j = 1 + 4 * h + jj
-                    ins = pe.matmul(pd[:, n * jj:n * jj + n], T.DM[:, 128 * j:128 * j + 128], T.key[:, j0:j1], True, True)
-                return ins
+                    pe.matmul(pd[:, o + n * jj:o + n * jj + n], T.DM[:, 128 * j:128 * j + 128], T.key[:, j0:j1], True, True)
             op("P", mm, r=[("key", m)] + DK, w=[pd.name], b=[pd.name])
 
         def signs(m, h, e):
             n = POS[m][1] - POS[m][0]
-            pd = DB[m][h]
-            so = 8 * POS[m][0] + 4 * n * h
+            pd, so, w = DB[m][h % 2][0], 8 * POS[m][0] + 4 * n * (h % 2), (8 if h == 2 else 4) * n
+            wk = [("sg", m, x) for x in ((0, 1) if h == 2 else (h,))]
             if e == "A":
-                op("A", lambda: a.activation(T.sg[:, so:so + 4 * n], pd[:, 0:4 * n], Fn.Sign), r=[pd.name], w=[("sg", m, h)], b=[pd.name])
+                op("A", lambda: a.activation(T.sg[:, so:so + w], pd[:, 0:w], Fn.Sign), r=[pd.name], w=wk, b=[pd.name])
             else:
-                op("V", lambda: v.tensor_scalar(T.sg[:, so:so + 4 * n], pd[:, 0:4 * n], -1.0, 1.0, Op.max, Op.min), r=[pd.name], w=[("sg", m, h)], b=[pd.name])
+                op("V", lambda: v.tensor_scalar(T.sg[:, so:so + w], pd[:, 0:w], -1.0, 1.0, Op.max, Op.min), r=[pd.name], w=wk, b=[pd.name])
 
         def places(m, h):
             n = POS[m][1] - POS[m][0]
@@ -614,33 +649,29 @@ def rank_program(g, core, T, topo):
             ps = T["ps%d" % (m % 2)]
 
             def mm():
-                ins = None
-                if h < 0:
-                    return pe.matmul(ps[:, 128:128 + n], T.Ih[:], T.ch[:, POS[m][0]:POS[m][1]], True, False)
                 for jj in range(4):
                     j = 1 + 4 * h + jj
                     dj = 16 - j if j < 8 else 0
-                    ins = pe.matmul(ps[:, 128:128 + n], T.DM[:, 128 * dj:128 * dj + 128], T.sg[:, so + n * jj:so + n * jj + n], False, j == 8)
-                return ins
-            op("P", mm, r=([("ch", min(m, 1)), "Ih"] if h < 0 else [("sg", m, h)]) + DK, w=[("Rp", m % 2)], b=[ps.name])
+                    pe.matmul(ps[:, 128:128 + n], T.DM[:, 128 * dj:128 * dj + 128], T.sg[:, so + n * jj:so + n * jj + n], j == 1, j == 8)
+            op("P", mm, r=[("sg", m, h)] + DK, w=[("Rp", m % 2)], b=[ps.name])
 
-        def ranked(m, e):
+        def ranked(m):
             lo, hi = POS[m]
             ps = T["ps%d" % (m % 2)]
-            lin(e, R(lo, hi), ps[:, 128:128 + hi - lo], 1.0, C(KR), [("Rp", m % 2)] + CK, [("R", m)], [ps.name])
-            send(rr, T.AW[:, RL + lo:RL + hi], R(lo, hi), "r%d%d" % (t, m), [("R", m)])
+            op("V", lambda: v.tensor_tensor(R(lo, hi), ps[:, 128:128 + hi - lo], T.cf[:, lo:hi], Op.add), r=[("Rp", m % 2), ("cf", m)], w=[("R", m)], b=[ps.name])
+            if m:
+                lo = BACK[m - 1][0]
+                send(rr, T.AW[:, RL + lo:RL + hi], R(lo, hi), "r%d%d" % (t, m - 1), [("R", x) for x in range(m + 1) if POS[x][0] >= lo])
 
-        def tokens(p):
+        def tokens(p, e="A"):
             c0, c1 = PC[p]
-            op("A", lambda: a.activation(T.B[:, 16 * c0:16 * c1], ind(T.IO[:], lm(c0, c1)), Fn.Identity, bias=0.0 if last else C(NK)),
-               r=IOK + CK + [mk(c0)], w=[("B", p)])
+            lin(e, T.B[:, 16 * c0:16 * c1], ind(T.IO[:], lm(c0, c1)), 1.0, 0.0 if last else C(NK), IOK + CK + [mk(c0)], [("B", p)])
 
         def paths(early):
             bo = T.BOb[:, 0:128] if last else T.BOb[:, 128:256]
             ins = None
             if early == 0:
-                pe.matmul(T.psl[:, 0:256], T.Ib[:], T.CT[:, 256:512] if last else T.CT[:, 0:256], True, False)
-                ins = pe.matmul(T.psl[:, 0:256], T.Ib[:], T.CT[:, 512:768], False, False)
+                ins = pe.matmul(T.psl[:, 0:256], T.Ib[:], T.CT[:, 256:512] if last else T.CT[:, 0:256], True, False)
             elif early == 1:
                 pe.matmul(T.psl[:, 8:88], bo, T.eq[:, 8:88], False, False)
                 pe.matmul(T.psl[:, 88:176], bo, T.ok2[:, 8:96], False, False)
@@ -653,20 +684,20 @@ def rank_program(g, core, T, topo):
 
         def commit(i):
             if i == 0:
-                src = ind(T.CB[:, 0:48], T.DL[:, 0:11]) if last else ind(R(0, 80), T.PL[:, 0:11])
+                src = ind(T.CB[:, 0:48], T.DL[:, 0:11]) if last else ind(R(0, 40), T.PL[:, 0:11])
                 op("V", lambda: v.tensor_tensor(T.eq[:, 0:176], src, T.B[:, 0:176], Op.is_equal),
-                   r=[("B", 0), ("B", 1), "PL", "DL"] + ([("CB", d) for d in range(3)] if last else [("R", 0)]), w=["eqa"])
+                   r=[("B", 0), ("B", 1), "PL"] + (["DL"] + [("CB", d) for d in range(3)] if last else [("R", 0)]), w=["eqa"])
             if i == 1:
                 op("V", lambda: v.tensor_tensor(T.ok2[:], ind(T.eq[:, 0:80], T.PL2[:, 0:6]), T.eq[:, 80:176], Op.add), r=["eqa", "PL2"], w=["ok2"])
                 lin("A", T.ok3[:], ind(T.ok2[:], T.AL[:, 0:5]), 1.0, 0.0, ["ok2", "AL"], ["ok3"])
             if i == -1:
-                op("P", lambda: paths(0), r=["Ib"] + (["CTl", "CTm"] if last else CTK), w=["sel"], b=["psl"])
+                op("P", lambda: paths(0), r=["Ib"] + [("CTl" if last else "CT", d) for d in range(5)], w=["sel"], b=["psl"])
             if i == 11:
                 op("P", lambda: paths(1), r=["eqa", "ok2", "ok3", "BOb", "BOb0"], w=["sel"], b=["psl"])
             if i == 2:
                 src = ind(T.CB[:, 0:80], T.DL2[:, 0:5]) if last else ind(R(0, 200), T.PL2[:, 6:11])
                 op("V", lambda: v.tensor_tensor(T.eq[:, 176:256], src, T.B[:, 176:256], Op.is_equal),
-                   r=[("B", 2), "DL2", "PL2"] + ([("CB", d) for d in range(5)] if last else [("R", 0), ("R", 1)]), w=["eq"])
+                   r=[("B", 2), ("B", 3), "PL2"] + (["DL2"] + [("CB", d) for d in range(5)] if last else [("R", 0), ("R", 1), ("R", 2)]), w=["eq"])
                 op("P", lambda: paths(2), r=["eq"], w=["sel"], b=["psl"])
             if i == 3:
                 op("V", lambda: v.tensor_reduce(T.bf[:, 0:1], T.psl[:, 0:256], Ax.X, Op.max), r=["sel"], w=["bf"], b=["psl"])
@@ -677,11 +708,9 @@ def rank_program(g, core, T, topo):
                    r=["bq", "ig", ("Y", 3)], w=[("X", t)])
 
         def chain(i, st):
-            c, xk = T.cc[:, 2 * i:2 * i + 1], ("XC", i) if i else ("Yr", t)
+            c, xk = (T.cc[:, 2 * i:2 * i + 1], ("XC", i)) if i else (T.c0[:, 2:3], ("Yr", t))
             if st == 0:
-                if i == 0:
-                    op("V", lambda: v.tensor_copy(c, T.XC[:, 8:9]), r=[xk], w=[("cc", 0)])
-                else:
+                if i:
                     op("V", lambda: v.tensor_tensor(T.XC[:, 16 * i:16 * i + 16], ind(T.K[:], c), T.hx[:], Op.add), r=["K", ("cc", i), "hx"], w=[xk])
                 op("A", lambda: a.activation(T.thx[:], ind(T.XC[:, 16 * i:16 * i + 8], T.CX[:]), Fn.Identity, bias=C(NKP)),
                    r=[xk, "CX", "NKP"], w=["thx"])
@@ -712,170 +741,49 @@ def rank_program(g, core, T, topo):
                     lin("A", T.YN[:, 8 * (lo + x):8 * (hi + x)], Y(8 * lo, 8 * hi), 0.5 ** d, 0.0, [("Y", 1 if d < 3 else d - 1)], [("YN", lo)])
         YNK = lambda d0, d1: [("YN", lo) for lo, hi, (d, x) in runs([(DEP[n], NODE[n] - n) for n in range(32)]) if d0 <= d < d1]
 
-        if last:
-            pick(0)
-            chain(0, 0)
-            emitted()
-            listed(0)
-            chain(0, 1)
-            pick(1)
-            chain(0, 2)
-            listed(1)
-            chain(0, 3)
-            pick(2)
-            chain(1, 0)
-            listed(2)
-            chain(1, 1)
-            pick(3)
-            chain(1, 2)
-            listed(3)
-            chain(1, 3)
-            chain(2, 0)
-            tokens(0)
-            numbers(0)
-            chain(2, 1)
-            state(0)
-            numbers(1)
-            chain(2, 2)
-            chain(2, 3)
-            tokens(1)
-            chain(3, 0)
-            state(1)
-            chain(3, 1)
-            commit(0)
-            unscale(0, 3)
-            send(rr, T.YL[:, 0:176], T.YN[:, 0:176], "yn0", YNK(0, 3))
-            chain(3, 2)
-            commit(1)
-            commit(-1)
-            commit(11)
-            chain(3, 3)
-            tokens(2)
-            chain(4, 0)
-            numbers(2)
-            chain(4, 1)
-            commit(2)
-            state(2)
-            chain(4, 2)
-            state(3)
-            unscale(3, 5)
-            commit(3)
-            chain(4, 3)
-            lin("V", T.bq[:, 0:1], T.bf[:, 0:1], 16.0, C(SC), ["bf"] + CK, ["bq"])
-            op("V", lambda: v.tensor_copy(T.YN[:, 256:272], ind(T.XC[:], T.bq[:, 0:1])), r=["bq", ("Yr", t)] + [("XC", d) for d in range(1, 5)], w=["X"])
-            op("V", lambda: v.tensor_copy(T.YN[:, 272:288], ind(T.CB[:, 16:96], T.bq[:, 0:1])),
-               r=["bq"] + [("CB", d) for d in range(6)], w=["X2"])
-            send(rr, T.YL[:, 176:280], T.YN[:, 176:280], "fin", ["X", "X2"] + YNK(3, 5))
-            break
+        def results(i):
+            if i == 0:
+                send(rr, T.YL[:, 0:176], T.YN[:, 0:176], "yn0", YNK(0, 3))
+            if i == 1:
+                lin("V", T.bq[:, 0:1], T.bf[:, 0:1], 16.0, C(SC), ["bf"] + CK, ["bq"])
+                op("V", lambda: v.tensor_copy(T.YN[:, 256:272], ind(T.XC[:], T.bq[:, 0:1])), r=["bq", ("Yr", t)] + [("XC", d) for d in range(1, 5)], w=["X"])
+            if i == 2:
+                op("V", lambda: v.tensor_copy(T.YN[:, 272:288], ind(T.CB[:, 16:96], T.bq[:, 0:1])),
+                   r=["bq"] + [("CB", d) for d in range(6)], w=["X2"])
+                send(rr, T.YL[:, 176:280], T.YN[:, 176:280], "fin", ["X", "X2"] + YNK(3, 5))
 
-        for m in range(3):
+        def roots(i):
+            ls = T.ls[:, 16 * t:16 * t + 16]
+            root(i, R(-8, 256), [("R", x) for x in range(4)] + [("Rz", t)], ls, "ls")
+            if i == 1:
+                if t == S - 2:
+                    send(verifier(rr, t + 1), T.c0[:], ls, "c0", ["ls"], turn=1)
+                    lands(("cc", 0), "c0")
+                send(rr, T.l0[:, 16 * t + 16:16 * t + 32], ls, "l%d" % (t + 1), ["ls"], turn=t == S - 2)
+                lands(("l0", t + 1), "l%d" % (t + 1))
+
+        def passed():
+            n = 16 if t == S - 2 else 8
+            send(verifier(rr, t + 1), T.XC[:, 0:16] if t == S - 2 else Y(256, 264), T.X[:, 16 * t:16 * t + n], "x%d" % (t + 1), [("X", t)], turn=t == S - 2)
+            lands(("Yr", t + 1), "x%d" % (t + 1))
+
+        def once(i):
+            if (t, i) == (0, 0):
+                dma("S", T.Q[:], T.qt[:], "dq2", r=["left"], w=["Q"], lag=7.0)
+            if (t, i) == (0, 1) or (t < 2 and i == 2):
+                late(i + t)
+
+        for m in range(0 if last else 3):
             lands(("Rl", t, m), "r%d%d" % (t, m))
-        pick(0)
-        emitted()
-        listed(0)
-        repeat(0, 0)
-        for lv in (1, 2, 3):
-            pick(lv)
-            listed(lv)
-        if t == 0:
-            late(0)
-            dma("S", T.Q[:], T.qt[:], "dq2", r=["left"], w=["Q"], lag=7.0)
-        cand(0)
-        gather(0, 80)
-        numbers(0)
-        state(0)
-        thresh(0, 2)
-        cand(1)
-        gather(80, POS[0][1])
-        gather(POS[0][1], 176)
-        numbers(1)
-        state(1)
-        thresh(2, 4)
-        compare(0, 0, 16)
-        keys(0, "V")
-        diffs(0, 0)
-        diffs(0, 1)
-        cand(2)
-        gather(176, 200)
-        numbers(2)
-        state(2)
-        thresh(4, 5)
-        state(3)
-        thresh(5, 6)
-        repeat(0, 1)
-        repeat(0, 2)
-        half(0)
-        places(0, -1)
-        signs(0, 0, "A")
-        signs(0, 1, "A")
-        gather(200, 256)
-        places(0, 0)
-        places(0, 1)
-        for p in (0, 1):
-            repeat(1, p)
-            repeat(2, p)
-        for p in range(4):
-            repeat(3, p)
-        if t == 0:
-            late(1)
-        tokens(0)
-        tokens(1)
-        ranked(0, "V")
-        commit(-1)
-        compare(1, 0, 16)
-        keys(1, "A")
-        diffs(1, 0)
-        diffs(1, 1)
-        half(1)
-        places(1, -1)
-        signs(1, 0, "A")
-        signs(1, 1, "V")
-        places(1, 0)
-        places(1, 1)
-        ranked(1, "A")
-        commit(0)
-        commit(1)
-        commit(11)
-        tokens(2)
-        commit(2)
-        commit(3)
-        compare(2, 0, 16)
-        keys(2, "A")
-        diffs(2, 0)
-        diffs(2, 1)
-        places(2, -1)
-        signs(2, 0, "A")
-        signs(2, 1, "V")
-        places(2, 0)
-        places(2, 1)
-        best_lists()
-        ranked(2, "A")
-        root_mark()
-        ls = T.ls[:, 16 * t:16 * t + 16]
-        root(0, R(-8, 256), [("R", x) for x in range(3)] + [("Rz", t)], None, None)
-        root(1, None, None, ls, "ls")
-        send(rr, T.l0[:, 16 * t + 16:16 * t + 32], ls, "l%d" % (t + 1), ["ls"])
-        lands(("l0", t + 1), "l%d" % (t + 1))
-        repeat(1, 2)
-        repeat(2, 2)
-        repeat(3, 4)
-        repeat(3, 5)
-        repeat(4)
-        repeat(5)
-        commit(4)
-        commit(5)
-        if t == S - 2:
-            lin("V", T.X[:, 16 * t + 8:16 * t + 9], T.psl[:, 0:1], 1.0, -float(TOP), ["sel"], [("X", t)], ["psl"])
-            send(verifier(rr, t + 1), T.XC[:, 0:16], T.X[:, 16 * t:16 * t + 16], "x%d" % (t + 1), [("X", t)])
-        else:
-            send(verifier(rr, t + 1), T.Y[:, 264 * (t + 1):264 * (t + 1) + 8], T.X[:, 16 * t:16 * t + 8], "x%d" % (t + 1), [("X", t)])
-        lands(("Yr", t + 1), "x%d" % (t + 1))
-        for c in range(0, 16, 2):
-            scatter(c)
-        for lv in range(4):
-            prepare(lv)
-        if t < 2:
-            late(2 + t)
+        named = dict(pick=pick, listed=listed, emitted=emitted, repeat=repeat, scatter=scatter, cand=cand, half=half, gather=gather,
+                     numbers=numbers, state=state, thresh=thresh, compare=compare, keys=keys, diffs=diffs, signs=signs, places=places,
+                     ranked=ranked, tokens=tokens, commit=commit, chain=chain, unscale=unscale, results=results, roots=roots,
+                     passed=passed, once=once, prepare=prepare, best=best_lists, mark=root_mark)
+        for call in (LAST if last else STEP).replace("\n", " ").split(","):
+            words, n0 = call.split(), len(nodes)
+            named[words[0]](*[x if x in "VA" else int(x) for x in words[1:]])
+            for nd in nodes[n0:]:
+                nd["tag"] = (t, " ".join(words))
         RK = [("Rl", t, m) for m in range(3)]
 
     lands("YL0", "yn0")
@@ -884,7 +792,7 @@ def rank_program(g, core, T, topo):
     dma("S", T.yn[:, 176:256], T.YL[:, 176:256], "dout", r=["XL"])
     dma("A", T.yx[:], T.YL[:, 256:264], "dout", r=["XL"])
     dma("A", T.yt[:, 24:32], T.YL[0:128:16, 272:280], "dout", r=["XL"])
-    for nd in arrange(nodes):
+    for nd in arrange(nodes, tables):
         emit(nd)
     for s in sorted(cnt):
         if max(waited[e].get(s, 0) for e in qu) < cnt[s]:

@@ -132,7 +132,7 @@ def ramps(vals):
     return out
 
 
-CYCLE, WAKE, ISSUE, FLIGHT, PER_BYTE = 0.00104, 0.115, 0.35, 1.35, 0.0013
+CYCLE, WAKE, ISSUE, FLIGHT, PER_BYTE = 0.00087, 0.175, 0.35, 1.3, 0.0013
 TURNS = 2
 ITEM = {"float32": 4, "int32": 4, "bfloat16": 2, "float16": 2, "uint16": 2}
 
@@ -646,19 +646,19 @@ def rank_program(g, core, T, topo):
         def places(m, h):
             n = POS[m][1] - POS[m][0]
             so = 8 * POS[m][0] + 4 * n * h
-            ps = T["ps%d" % (m % 2)]
+            ps = DB[m][0][0]
 
             def mm():
                 for jj in range(4):
                     j = 1 + 4 * h + jj
                     dj = 16 - j if j < 8 else 0
-                    pe.matmul(ps[:, 128:128 + n], T.DM[:, 128 * dj:128 * dj + 128], T.sg[:, so + n * jj:so + n * jj + n], j == 1, j == 8)
-            op("P", mm, r=[("sg", m, h)] + DK, w=[("Rp", m % 2)], b=[ps.name])
+                    pe.matmul(ps[:, 0:n], T.DM[:, 128 * dj:128 * dj + 128], T.sg[:, so + n * jj:so + n * jj + n], j == 1, j == 8)
+            op("P", mm, r=[("sg", m, h)] + DK, w=[ps.name], b=[ps.name])
 
         def ranked(m):
             lo, hi = POS[m]
-            ps = T["ps%d" % (m % 2)]
-            op("V", lambda: v.tensor_tensor(R(lo, hi), ps[:, 128:128 + hi - lo], T.cf[:, lo:hi], Op.add), r=[("Rp", m % 2), ("cf", m)], w=[("R", m)], b=[ps.name])
+            ps = DB[m][0][0]
+            op("V", lambda: v.tensor_tensor(R(lo, hi), ps[:, 0:hi - lo], T.cf[:, lo:hi], Op.add), r=[ps.name, ("cf", m)], w=[("R", m)], b=[ps.name])
             if m:
                 lo = BACK[m - 1][0]
                 send(rr, T.AW[:, RL + lo:RL + hi], R(lo, hi), "r%d%d" % (t, m - 1), [("R", x) for x in range(m + 1) if POS[x][0] >= lo])

@@ -52,7 +52,7 @@ SCRATCH = {
     "I16": ("sbuf", [128, 256], "bfloat16"), "GT": ("sbuf", [128, 256], "bfloat16"), "one": ("sbuf", [128, 2], "float16"),
     "D1": ("sbuf", [128, 2 * FC], "bfloat16"), "F2": ("sbuf", [128, FC], "bfloat16"), "GM": ("sbuf", [128, 8], "float32"),
     "RZ": ("sbuf", [128, 256], "bfloat16"), "sc": ("sbuf", [128, FC], "float32"), "GL": ("sbuf", [128, 6], "uint16"),
-    "AL": ("sbuf", [128, 6], "uint16"), "ok3": ("sbuf", [128, 80], "bfloat16"),
+    "AL": ("sbuf", [128, 6], "uint16"), "ok3": ("sbuf", [128, 112], "bfloat16"),
     "TM": ("sbuf", [128, 256], "bfloat16"), "LX": ("sbuf", [128, 16], "uint16"),
     "kp": ("sbuf", [128, 4], "float32"), "pi": ("sbuf", [128, 32], "int32"), "pj": ("sbuf", [128, 32], "int32"),
     "C": ("sbuf", [128, 20], "float32"), "CJ": ("sbuf", [128, 16], "float32"),
@@ -65,7 +65,7 @@ SCRATCH = {
     "DL": ("sbuf", [128, 16], "uint16"), "DL2": ("sbuf", [128, 6], "uint16"),
     "cf": ("sbuf", [128, 256], "float32"), "F": ("sbuf", [128, FD + 256], "bfloat16"),
     "PL": ("sbuf", [128, 16], "uint16"), "PL2": ("sbuf", [128, 12], "uint16"),
-    "CX": ("sbuf", [128, 8], "uint16"), "SCL": ("sbuf", [128, 256], "float32"), "ISC": ("sbuf", [128, 264], "float32"),
+    "CX": ("sbuf", [128, 8], "uint16"), "SE": ("sbuf", [128, 18], "uint16"),
     "bf": ("sbuf", [128, 4], "float32"), "M": ("sbuf", [128, 16], "float32"), "bl": ("sbuf", [128, 8], "uint16"),
     "w1": ("sbuf", [128, 128], "float16"), "l0": ("sbuf", [128, 64], "uint16"), "ls": ("sbuf", [128, 48], "uint16"),
     "wf": ("sbuf", [128, 176], "float32"), "wh": ("sbuf", [128, 176], "float16"),
@@ -86,30 +86,35 @@ SCRATCH = {
     "pa0": ("psum", [128, 512], "float32"), "pb0": ("psum", [128, 512], "float32"),
     "pa1": ("psum", [128, 512], "float32"), "pb1": ("psum", [128, 512], "float32"),
 }
-SEMAPHORES = (["sv", "sa", "sp", "sq", "sent", "dtok", "dx", "dkap", "dk", "dout", "yn0", "fin", "dq0", "dq1", "dq2", "sent0"]
+SEMAPHORES = (["sv", "sa", "sp", "sq", "sent", "dtok", "dx", "dkap", "dk", "dout", "yn0", "yn1", "fin", "dq0", "dq1", "dq2", "sent3"]
               + ["m%d%d" % (t, i) for t in range(S) for i in range(4)] + ["c0"] + ["r%d%d" % (t, i) for t in range(3) for i in range(3)]
               + ["x%d" % t for t in range(S)] + ["l%d" % t for t in range(1, S)])
 
 
-STEP = """pick 0, emitted, listed 0, pick 1, listed 1, pick 2, cand 0 A, listed 2, numbers 0, state 0, gather 0 24 A,
-gather 24 40 V, gather 40 64 A, thresh 0 2, pick 3, cand 1 A, numbers 1, listed 3, once 0,
+STEP = """pick 0, emitted, listed 0, once 2, pick 1, listed 1, pick 2, halves 0 A, thresh 0, cand 0 A, listed 2, state 0, gather 0 24 A,
+gather 24 40 V, gather 40 64 A, thresh 1, pick 3, cand 1 V, halves 1 A, listed 3, once 0,
 repeat 0 0, repeat 1 0, repeat 2 0, repeat 0 1, repeat 1 1, repeat 2 1, repeat 3 0, repeat 3 1, repeat 3 2, repeat 3 3,
-repeat 4 0, repeat 5 0, gather 64 80 A, state 1, gather 80 104 A, gather 104 128 A, thresh 2 4,
-compare 0 0 16, keys 0 V, diffs 0 0, diffs 0 1, half 0 A, gather 128 152 A, gather 152 176 A, cand 2 A, numbers 2, state 2,
-thresh 4 5, compare 1 0 16, signs 0 2 V, places 0 0, places 0 1, keys 1 V, diffs 1 0, diffs 1 1, gather 176 200 A, ranked 0,
-half 1 A, compare 2 0 16, signs 1 2 A, places 1 0, places 1 1, cand 3 A, gather 200 224 A, gather 224 256 A, numbers 3,
-state 3, thresh 5 6, keys 2 V, diffs 2 0, diffs 2 1, ranked 1, half 2 A, compare 3 0 16, signs 2 0 A, signs 2 1 A,
-places 2 0, places 2 1, tokens 0 A, tokens 1 A, once 1, commit -1, commit 0, commit 1, commit 11, keys 3 V, ranked 2,
-diffs 3 0, diffs 3 1, tokens 2 A, tokens 3 A, commit 2, half 3 A, signs 3 0 A, signs 3 1 V, places 3 0, places 3 1,
-commit 3, best, ranked 3, commit 4, commit 5, passed, mark, roots 0, roots 1,
+repeat 4 0, repeat 5 0, gather 64 80 A, state 1, gather 80 104 A, gather 104 128 A, thresh 2,
+compare 0 0 16, keys 0 V, diffs 0 0, half 0 A, gather 128 152 A, gather 152 176 A, cand 2 V, halves 2 V, state 2,
+thresh 3, compare 1 0 16, signs 0 0 V, places 0 0, keys 1 V, diffs 1 0, gather 176 200 A, ranked 0,
+half 1 V, compare 2 0 16, signs 1 0 A, places 1 0, cand 3 V, gather 200 224 A, gather 224 256 A, halves 3 A,
+state 3, thresh 4, keys 2 V, diffs 2 0, diffs 2 1, ranked 1, half 2 V, compare 3 0 16, signs 2 0 A, signs 2 1 A,
+places 2 0, places 2 1, tokens 0 V, tokens 1 A, once 1, commit -1, commit 0, commit 1, commit 11, tokens 2 A, commit 12,
+commit 13, keys 3 V, ranked 2, diffs 3 0, diffs 3 1, diffs 3 2, tokens 3 A, commit 2, half 3 V,
+signs 3 0 A, signs 3 1 A, signs 3 2 V, places 3 0, places 3 1, places 3 2,
+commit 3, best, ranked 3, commit 5, passed, mark, roots 0, roots 1,
 repeat 0 2, repeat 0 3, repeat 1 2, repeat 2 2, repeat 3 4, repeat 3 5, repeat 3 6, repeat 3 7, repeat 4 1, repeat 5 1,
 scatter 0, scatter 2, scatter 4, scatter 6, scatter 8, scatter 10, scatter 12, scatter 14,
-prepare 0, prepare 1, prepare 2, prepare 3, once 2"""
+prepare 0, prepare 1, prepare 2, prepare 3"""
 LAST = """chain 0 0, pick 0, commit -1, chain 0 1, emitted, listed 0, chain 0 2, pick 1, chain 0 3, chain 1 0, listed 1, chain 1 1,
-pick 2, chain 1 2, tokens 0 A, listed 2, chain 1 3, chain 2 0, numbers 0, pick 3, chain 2 1, state 0, tokens 1 A, numbers 1,
-chain 2 2, listed 3, chain 2 3, chain 3 0, commit 0, numbers 2, chain 3 1, tokens 2 A, commit 1, state 1, chain 3 2,
-unscale 2 3, commit 11, state 2, chain 3 3, chain 4 0, unscale 0 1, tokens 3 A, numbers 3, commit 2, chain 4 1, unscale 3 4,
-state 3, unscale 1 2, commit 3, results 0, unscale 4 5, chain 4 2, results 1, chain 4 3, results 2"""
+pick 2, chain 1 2, tokens 0 A, listed 2, chain 1 3, chain 2 0, halves 0 A, pick 3, chain 2 1, state 0, tokens 1 A, halves 1 A,
+chain 2 2, listed 3, chain 2 3, chain 3 0, commit 0, chain 3 1, tokens 2 A, commit 1, state 1, halves 2 A, chain 3 2,
+reseat 0 A, commit 11, commit 12, commit 13, state 2, halves 3 A, chain 3 3, chain 4 0, tokens 3 A, commit 2, chain 4 1,
+state 3, commit 3, results 0, reseat 1 A, chain 4 2, results 1, chain 4 3, results 2"""
+HASTE = [{"diffs": 2.0, "ranked": 1.5, "compare 2": 1.5, "signs 2": 1.5, "commit 13": 1.5, "keys 3": 1.0, "commit 0": 1.0,
+          "roots 0": 1.0, "gather": 0.3, "commit 1": 0.3, "compare": -0.3, "cand": -0.6, "listed": -0.6, "diffs 3": -0.6,
+          "once": -1.0, "signs": -1.0, "places 3": -1.0, "half": -1.0, "scatter": -1.5, "state": -1.5},
+         {"results": -0.3, "pick": -1.0, "halves": -1.0}]
 
 
 def runs(vals):
@@ -132,8 +137,8 @@ def ramps(vals):
     return out
 
 
-CYCLE, WAKE, ISSUE, FLIGHT, PER_BYTE = 0.00087, 0.175, 0.35, 1.3, 0.0013
-TURNS = 2
+CYCLE, WAKE, ISSUE, FLIGHT, PER_BYTE = 0.00092, 0.165, 0.4, 1.3, 0.0013
+TURNS, FIRST = 2, 0
 ITEM = {"float32": 4, "int32": 4, "bfloat16": 2, "float16": 2, "uint16": 2}
 
 
@@ -169,7 +174,7 @@ def arrange(nodes, tables):
         if nd["e"] == "L":
             d.add(far[nd["sem"]])
         if nd.get("turn"):
-            d |= set(turns[-1:])
+            d |= set([j for j in turns if nodes[j]["turn"] == nd["turn"]][-1:])
             turns.append(i)
         d.discard(i)
         deps.append(d)
@@ -225,7 +230,8 @@ def arrange(nodes, tables):
         total = max(end[i] + nodes[i]["lag"] for i in end)
         if best is None or total < best[0]:
             best = (total, end)
-        chain = place(kids, deps, lambda j, i: gap(i, j), lambda i: nodes[i]["lag"], end)
+        back = place(kids, deps, lambda j, i: gap(i, j), lambda i: nodes[i]["lag"], {i: end[i] - nodes[i].get("haste", 0.0) for i in end})
+        chain = {i: back[i] + nodes[i].get("haste", 0.0) for i in back}
     return [nodes[i] for i in sorted(best[1], key=lambda i: (round(best[1][i] - nodes[i]["busy"], 6), depth[i]))]
 
 
@@ -307,9 +313,9 @@ def rank_program(g, core, T, topo):
     def ind(win, lst):
         return (win.indirect(lst),)
 
-    def op(e, fn, r=(), w=(), b=()):
+    def op(e, fn, r=(), w=(), b=(), turn=0):
         fn()
-        nodes.append(dict(e=e, calls=said[:], r=r, w=w, b=b, sem=semof[e], busy=sum(cost(*c) for c in said), lag=0.0))
+        nodes.append(dict(e=e, turn=turn, calls=said[:], r=r, w=w, b=b, sem=semof[e], busy=sum(cost(*c) for c in said), lag=0.0))
         del said[:]
 
     def dma(e, out, in_, sem, r=(), w=(), lag=1.4, turn=0):
@@ -379,15 +385,13 @@ def rank_program(g, core, T, topo):
         for j in range(j0, j1):
             cmp(T.DM[:, 128 * j:128 * j + 128], T.IOb[:, 0:128], T.CJ[:, j:j + 1], 2048.0 if j <= 8 else -2048.0, Op.is_equal, ["IOb", "CJ"], [("DM", j)])
     shifts(1, 9)
-    send(verifier(rank, 0), T.Y[:, 0:8], T.xs[:], "x0", ["xs"])
+    send(verifier(rank, 0), T.Y[:, 0:8], T.xs[:], "x0", ["xs"], turn=2)
     lands(("Yr", 0), "x0")
+    op("G", lambda: gp.iota(T.IO[:, V - 1024:V], [[1, 1024]], V - 1024, 0, allow_small_or_imprecise_dtypes=True), w=["IO5"], turn=2)
     op("G", lambda: gp.affine_select(T.DM[:, 128:1152], T.DM[:, 128:1152], [[0, 8], [-1, 128]], Op.not_equal, -2048.0, 0, 1),
-       r=[("DM", x) for x in range(1, 9)], w=["DMa"])
+       r=[("DM", x) for x in range(1, 9)], w=["DMa"], turn=2)
     shifts(9, 16)
-    op("G", lambda: gp.affine_select(T.DM[:, 1152:2048], T.DM[:, 1152:2048], [[0, 7], [-1, 128]], Op.not_equal, 2048.0, 0, 1),
-       r=[("DM", x) for x in range(9, 16)], w=["DMb"])
     shifts(0, 1)
-    DK = [("DM", 0), "DMa", "DMb"]
     rows = [ROW[n] for lv in LEVELS for n, who in lv]
     todo = [(FP + 8 * lo, FP + 8 * hi, T.IJ, 8 * p, 8 * d) for lo, hi, p, d in ramps(PAR)]
     todo += [(FD + 8 * lo, FD + 8 * hi, T.IJ, 16 * p, 0) for lo, hi, p in runs(DEP)]
@@ -433,10 +437,10 @@ def rank_program(g, core, T, topo):
     def root_mark():
         op("V", lambda: v.tensor_scalar(T.M[:, 0:1], T.bq[:, 0:1], float(RL - 8 + TOP), C(UP), Op.add, Op.mult), r=["bq", "M"] + CK, w=["M0"])
 
-    def root(i, win, keys, out, okey):
+    def root(i, win, keys, out, okey, turn=0):
         if i == 0:
             op("V", lambda: v.tensor_scalar(T.w1[:], ind(win, T.bl[:]), C(KT), 2048.0, Op.add, Op.min), r=keys + ["bl"] + CK, w=["w1"])
-            op("P", lambda: pe.matmul(T.psl[:, 0:1], T.w1[:], T.one[:, 0:1], True, True), r=["w1", "one"], w=["sel"], b=["psl"])
+            op("P", lambda: pe.matmul(T.psl[:, 0:1], T.w1[:], T.one[:, 0:1], True, True), r=["w1", "one"], w=["sel"], b=["psl"], turn=turn)
         else:
             op("V", lambda: v.tensor_scalar(out, T.M[:], T.psl[:, 0:1], float(TOP), Op.max, Op.subtract), r=["M0", "sel"], w=[okey], b=["psl"])
     best_lists()
@@ -463,24 +467,20 @@ def rank_program(g, core, T, topo):
         LXK.append(("LX", c0))
         lin("A", T.LX[:, c0:c1], T.IO[:, 0:c1 - c0], float(d), float(p), ["IO0"], [LXK[-1]])
     cmp(T.CT[:, 512:768], T.IS[:, 0:256], C(SC), -128.0, Op.not_equal, ["IS"] + CK, ["CTm"])
-    lin("V", T.TM[:], T.IJ[:], 0.5, 0.0, ["IJ"], ["TM0", "TM1"])
-    op("V", lambda: v.tensor_tensor(T.CT[:, 0:256], T.TM[:], T.CT[:, 512:768], Op.add), r=["TM0", "TM1", "CTm"], w=["CTw"])
+    op("P", lambda: [pe.matmul(T.ps0[:, 0:256], T.Ib[:], x, i == 0, i == 1) for i, x in enumerate((T.IJ[:], T.CT[:, 512:768]))],
+       r=["Ib", "IJ", "CTm"], w=["fx"], b=["ps0"])
+    for lo, hi, d in runs(DEP):
+        lin("A", T.CT[:, 8 * lo:8 * hi], T.ps0[:, 8 * lo:8 * hi], 0.5, 0.5 - 16 * d, ["fx"], [("CT", d)], ["ps0"])
     cmp(T.BOb[:, 0:128], T.IG[:], C(G16), 1.0, Op.is_equal, ["IG"] + CK, ["BOb0"])
     cmp(T.BOb[:, 128:256], T.IG[:], C(G16), 16.0, Op.is_equal, ["IG"] + CK, ["BOb"])
     for i, n in enumerate((256, 512, 1024, 2048)):
-        m = min(2 * n, V)
+        m = min(2 * n, V - 1024)
         lin("A", T.IO[:, n:m], T.IO[:, 0:m - n], 1.0, float(n), ["IO%d" % j for j in range(i + 1)], ["IO%d" % (i + 1)])
-    IOK = ["IO%d" % j for j in range(5)]
-    lin("V", T.SCL[:, 0:8], T.IO[:, 0:8], 0.0, 0.0, ["IO0"], [("SCL", 0)])
-    for lo, hi, d in runs(DEP)[1:]:
-        lin("V", T.SCL[:, 8 * lo:8 * hi], T.IJ[:, 8 * lo:8 * hi], 0.0, 2.0 ** d, ["IJ"], [("SCL", d)])
-    SK, IK = [("SCL", d) for d in range(5)], [("ISC", d) for d in range(5)]
+    IOK = ["IO%d" % j for j in range(6)]
+    SEK = [("SE", n) for n in SWAP]
 
     def late(i):
         if i == 1:
-            for lo, hi, d in runs(DEP):
-                lin("A", T.CT[:, 8 * lo:8 * hi], T.CT[:, 8 * lo:8 * hi], 1.0, 0.5 - 16 * d, ["CTw"], [("CT", d)])
-                lin("A", T.ISC[:, 8 * lo + (8 if d else 0):8 * hi + 8], T.IO[:, 0:8 * (hi - lo) + (0 if d else 8)], 0.0, 0.5 ** d, ["IO0"], [("ISC", d)])
             for x in range(3):
                 lin("A", T.R[:, 264 * x:264 * x + 8], T.IO[:, 0:8], 0.0, C(ZC), ["IO0"] + CK, [("Rz", x)])
         if i == 2:
@@ -491,11 +491,17 @@ def rank_program(g, core, T, topo):
             for lo, hi, d in runs(DEP):
                 lin("A", T.CT[:, 256 + 8 * lo:256 + 8 * hi], T.CT[:, 512 + 8 * lo:512 + 8 * hi], 1.0, -15.0 * d, ["CTm"], [("CTl", d)])
             lin("A", T.CX[:], T.IO[:, 0:8], 1.0, 0.0, ["IO0"], ["CX"])
+            lin("A", T.SE[:, 0:11], T.IO[:, 0:11], 16.0, C(KF), ["IO0"] + CK, ["SEa"])
+            lin("A", T.SE[:, 12:17], T.IO[:, 11:16], 16.0, C(KF), ["IO0"] + CK, ["SEb"])
+            for n in SWAP:
+                x = n // 2 + (n > 21)
+                lin("A", T.SE[:, x:x + 1], T.IO[:, n // 2:n // 2 + 1], 16.0, C(KX), ["IO0", "KX", "SEa", "SEb"], [("SE", n)])
         if i == 3:
             select(FD, FD + 256, [(T.DL[:], 0, 16, C(SC), "DL"), (T.DL2[:, 0:5], 11, 16, C(SC), "DL2")])
             op("V", lambda: v.tensor_tensor(T.TIE[:, 0:128], T.TM[:, 0:128], T.TM[:, 128:256], Op.add), r=["TM0", "TM1"], w=["TIE0"])
             lin("A", T.TIE[:, 128:256], T.TIE[:, 0:128], 1.0, 0.5, ["TIE0"], ["TIE"])
             lin("A", T.BO16[:], T.BOb[:, 128:256], 1.0, 0.0, ["BOb"], ["BO16"])
+            lin("A", T.CB[:, 80:96], T.IO[:, 0:16], 0.0, 0.0, ["IO0"], [("CB", 5)])
 
     tables = len(nodes)
     for t in range(S):
@@ -526,7 +532,8 @@ def rank_program(g, core, T, topo):
                r=[PB[lv].name, "RX"], w=[("sc", lv)], b=[PB[lv].name])
             src = ind(T.sc[:, lo:lo + n], T.GL[:, 2 * lv:2 * lv + 1]) if lv < 3 else T.sc[:, lo + 15:lo + n:16]
             op("V", lambda: v.tensor_scalar(outs[lv], src, 2048.0, None, Op.add), r=[("sc", lv), "GL"], w=[("L", lv + 1)])
-            send(q, lm(*PC[lv]), mine[lv], "m%d%d" % (t, lv), mineK[lv] + (DK if t == 0 else []), *(("sent0", ["left"]) if (t, lv) == (0, 3) else ()))
+            send(q, lm(*PC[lv]), mine[lv], "m%d%d" % (t, lv), mineK[lv] + (["DMa", "IO5"] if t == 0 else []),
+                 *(("sent3", [("left", 3)]) if (t, lv) == (0, 3) else ()))
 
         def emitted():
             if t > 0:
@@ -554,7 +561,8 @@ def rank_program(g, core, T, topo):
                                  (T.Ih[:], T.Bo[:, lo:hi], [("Bo", y) for y in range(part, 2 + 2 * part)]),
                                  (T.I16[:, 0:128], T.ed[:, lo:hi], [("ed", 0, y) for y in range(2 * part, 2 + part)]),
                                  (T.I16[:, 128:256], T.ed[:, 256 + lo:256 + hi], [("ed", 1, y) for y in range(2 * part, 2 + part)]))[x]
-                op("P", lambda: pe.matmul(T.pb1[:, lo:hi], lhs, rhs, x == 0, x == 3), r=key + ["I16", "I32", "Ih"], w=["pb1"], b=["pb1"])
+                op("P", lambda: pe.matmul(T.pb1[:, lo:hi], lhs, rhs, x == 0, x == 3), r=key + ["I16", "I32", "Ih"], w=["pb1"], b=["pb1"],
+                   turn={3: 10 + t, 4: 20 + t}.get(p, 0))
             lo, hi = ((0, 160), (160, 256))[p % 2]
             if i == 4:
                 op("V", lambda: v.tensor_tensor_scan(T.ds[:, lo:hi], T.RZ[:, lo:hi], T.pb1[:, lo:hi], 0.0, Op.add, Op.max), r=["pb1", "RZ"], w=[("ds", p)], b=["pb1"])
@@ -574,7 +582,7 @@ def rank_program(g, core, T, topo):
         R = lambda j0, j1: T.R[:, y0 + j0:y0 + j1]
         piece = lambda j: mk(j // 16)[2]
         KCK = [[] for x in POS]
-        DB = [((T.pa0, 0), (T.pa0, 256)), ((T.pa1, 0), (T.pa1, 256)), ((T.pa0, 0), (T.pb0, 0)), ((T.pa1, 0), (T.pb0, 0))]
+        DB = [[(T.pa0, 1, 9)], [(T.pa1, 1, 9)], [(T.pa0, 1, 5), (T.pb0, 5, 9)], [(T.pa1, 1, 4), (T.pb0, 4, 7), (T.ps0, 7, 9)]]
 
         def cand(p, e="A"):
             c0, c1 = PC[p]
@@ -588,24 +596,25 @@ def rank_program(g, core, T, topo):
             lin(e, T.kc[:, 16 * j0:16 * j1], ind(T.K[:], T.cu[:, j0:j1]), 1.0, 0.0, ["K", ("cu", piece(j0))], [("kc", j0)])
             KCK[[lo <= j0 < hi for lo, hi in POS].index(True)].append(("kc", j0))
 
-        def numbers(p):
-            c0, c1 = PC[p]
-            op("V", lambda: v.tensor_tensor(T.kn[:, 16 * c0:16 * c1], ind(T.K[:], lm(c0, c1)), T.SCL[:, 16 * c0:16 * c1], Op.mult),
-               r=["K", mk(c0)] + SK, w=[("kn", p)])
+        x_in = T.XC[:, 0:8] if last else Y(-8, 0)
+
+        def halves(i, e):
+            win, lst = ((x_in, T.PL[:, 0:5]), (Y(0, 80), T.PL2[:, 0:6]), (Y(0, 176), T.PL2[:, 6:9]), (Y(0, 224), T.PL[:, 14:16]))[i]
+            lin(e, T.kn[:, 16 * PC[i][0]:16 * PC[i][1]], ind(win, lst), 0.5, 0.0, ["PL", "PL2"] + ([("Y", i - 1), "Y0"] if i else [("Yr", t)]), [("kn", i)])
 
         def state(i):
-            j0, j1, win, lst, kk = ((0, 80, T.XC[:, 0:8] if last else Y(-8, 0), T.PL[:, 0:5], 0), (80, 176, Y(0, 80), T.PL2[:, 0:6], 1),
-                                    (176, 224, Y(0, 176), T.PL2[:, 6:9], 2), (224, 256, Y(0, 224), T.PL[:, 14:16], 3))[i]
-            op("V", lambda: v.tensor_tensor(Y(j0, j1), ind(win, lst), T.kn[:, j0:j1], Op.add),
-               r=["PL", "PL2", ("kn", kk), ("Y", i - 1) if i else ("Yr", t)], w=[("Y", i)])
+            c0, c1 = PC[i]
+            op("V", lambda: v.tensor_tensor(Y(16 * c0, 16 * c1), ind(T.K[:], lm(c0, c1)), T.kn[:, 16 * c0:16 * c1], Op.add),
+               r=["K", mk(c0), ("kn", i)], w=[("Y", i)] + ([] if i else ["Y0"]))
+            if i == 0:
+                lin("A", Y(0, 8), x_in, 1.0, 0.0, [("Yr", t)], ["Y0"])
 
-        TH = [(0, 8, 0), (8, 80, 0), (80, 88, 1), (88, 176, 1), (176, 224, 2), (224, 256, 3)]
+        TH = [(0, 8, ("Yr", t)), (8, 80, ("Y", 0)), (80, 176, ("Y", 1)), (176, 224, ("Y", 2)), (224, 256, ("Y", 3))]
         THK = [[j0 for j0, j1, i in TH if j0 < hi and lo < j1] for lo, hi in POS]
 
-        def thresh(i0, i1):
-            for j0, j1, i in TH[i0:i1]:
-                op("V", lambda: v.tensor_scalar(T.pth[:, j0:j1], Y(j0, j1), 0.5 ** DEP[j0 // 8], T.kp[:, 0:1], Op.mult, Op.subtract),
-                   r=[("Y", i), "kp"], w=[("th", j0)])
+        def thresh(i):
+            j0, j1, key = TH[i]
+            op("V", lambda: v.tensor_scalar(T.pth[:, j0:j1], Y(j0, j1) if i else x_in, T.kp[:, 0:1], None, Op.subtract), r=[key, "kp"], w=[("th", j0)])
 
         def compare(m, k0, k1):
             j0, j1 = POS[m]
@@ -616,7 +625,7 @@ def rank_program(g, core, T, topo):
                 op("V", lambda: v.tensor_tensor(T.bits[:, bo:bo + n], T.kc[:, 16 * j0 + k:16 * j1:16], T.pth[:, j0:j1], Op.is_ge),
                    r=KCK[m] + [("th", x) for x in THK[m]], w=[("bits", m, k)])
                 op("P", lambda: pe.matmul(ps[:, 0:n], T.Zh[:, 15 - k:143 - k], T.bits[:, bo:bo + n], k == 0, k == 15),
-                   r=[("bits", m, k), "Zh"], w=[("S", m % 2)], b=[ps.name] if k in (0, 15) else [])
+                   r=[("bits", m, k), "Zh"], w=[("S", m % 2)], b=[ps.name] if k in (0, 15) else [], turn=10 + t if (m, k) == (0, FIRST) else 0)
 
         def keys(m, e):
             j0, j1 = POS[m]
@@ -626,34 +635,24 @@ def rank_program(g, core, T, topo):
         def diffs(m, h):
             j0, j1 = POS[m]
             n = j1 - j0
-            pd, o = DB[m][h]
-
-            def mm():
-                for jj in range(4):
-                    j = 1 + 4 * h + jj
-                    pe.matmul(pd[:, o + n * jj:o + n * jj + n], T.DM[:, 128 * j:128 * j + 128], T.key[:, j0:j1], True, True)
-            op("P", mm, r=[("key", m)] + DK, w=[pd.name], b=[pd.name])
+            pd, lo, hi = DB[m][h]
+            op("P", lambda: [pe.matmul(pd[:, n * (j - lo):n * (j - lo + 1)], T.DM[:, 128 * j:128 * j + 128], T.key[:, j0:j1], True, True) for j in range(lo, hi)],
+               r=[("key", m), "DMa"], w=[pd.name], b=[pd.name])
 
         def signs(m, h, e):
             n = POS[m][1] - POS[m][0]
-            pd, so, w = DB[m][h % 2][0], 8 * POS[m][0] + 4 * n * (h % 2), (8 if h == 2 else 4) * n
-            wk = [("sg", m, x) for x in ((0, 1) if h == 2 else (h,))]
+            pd, lo, hi = DB[m][h]
+            so, w = 8 * POS[m][0] + n * (lo - 1), n * (hi - lo)
             if e == "A":
-                op("A", lambda: a.activation(T.sg[:, so:so + w], pd[:, 0:w], Fn.Sign), r=[pd.name], w=wk, b=[pd.name])
+                op("A", lambda: a.activation(T.sg[:, so:so + w], pd[:, 0:w], Fn.Sign), r=[pd.name], w=[("sg", m, h)], b=[pd.name])
             else:
-                op("V", lambda: v.tensor_scalar(T.sg[:, so:so + w], pd[:, 0:w], -1.0, 1.0, Op.max, Op.min), r=[pd.name], w=wk, b=[pd.name])
+                op("V", lambda: v.tensor_scalar(T.sg[:, so:so + w], pd[:, 0:w], -1.0, 1.0, Op.max, Op.min), r=[pd.name], w=[("sg", m, h)], b=[pd.name])
 
         def places(m, h):
             n = POS[m][1] - POS[m][0]
-            so = 8 * POS[m][0] + 4 * n * h
-            ps = DB[m][0][0]
-
-            def mm():
-                for jj in range(4):
-                    j = 1 + 4 * h + jj
-                    dj = 16 - j if j < 8 else 0
-                    pe.matmul(ps[:, 0:n], T.DM[:, 128 * dj:128 * dj + 128], T.sg[:, so + n * jj:so + n * jj + n], j == 1, j == 8)
-            op("P", mm, r=[("sg", m, h)] + DK, w=[ps.name], b=[ps.name])
+            so, ps = 8 * POS[m][0] - n, DB[m][0][0]
+            op("P", lambda: [pe.matmul(ps[:, 0:n], T.DM[:, 128 * (16 - j if j < 8 else 0):128 * (17 - j if j < 8 else 1)], T.sg[:, so + n * j:so + n * j + n], j == 1, j == 8)
+                             for j in range(*DB[m][h][1:])], r=[("sg", m, h), ("DM", 0), "DMb"], w=[ps.name], b=[ps.name])
 
         def ranked(m):
             lo, hi = POS[m]
@@ -668,19 +667,21 @@ def rank_program(g, core, T, topo):
             lin(e, T.B[:, 16 * c0:16 * c1], ind(T.IO[:], lm(c0, c1)), 1.0, 0.0 if last else C(NK), IOK + CK + [mk(c0)], [("B", p)])
 
         def paths(early):
-            bo = T.BOb[:, 0:128] if last else T.BOb[:, 128:256]
-            ins = None
+            bo, ct = (T.BOb[:, 0:128], 256) if last else (T.BOb[:, 128:256], 0)
             if early == 0:
-                ins = pe.matmul(T.psl[:, 0:256], T.Ib[:], T.CT[:, 256:512] if last else T.CT[:, 0:256], True, False)
-            elif early == 1:
+                pe.matmul(T.psl[:, 0:208], T.Ib[:], T.CT[:, ct:ct + 208], True, False)
+            if early == 1:
                 pe.matmul(T.psl[:, 8:88], bo, T.eq[:, 8:88], False, False)
                 pe.matmul(T.psl[:, 88:176], bo, T.ok2[:, 8:96], False, False)
-                ins = pe.matmul(T.psl[:, 176:256], bo, T.ok3[:], False, False)
-            else:
-                pe.matmul(T.psl[:, 176:256], bo, T.eq[:, 176:256], False, False)
-                for n in range(28, 32):
-                    ins = pe.matmul(T.psl[:, 8 * n:8 * n + 8], bo, T.eq[:, 8 * PAR[n]:8 * PAR[n] + 8], False, n == 31)
-            return ins
+                pe.matmul(T.psl[:, 176:208], bo, T.ok3[:, 0:32], False, False)
+            if early == 2:
+                pe.matmul(T.psl[:, 176:208], bo, T.eq[:, 176:208], False, True)
+            if early == 3:
+                pe.matmul(T.psl[:, 208:256], T.Ib[:], T.CT[:, ct + 208:ct + 256], True, False)
+                pe.matmul(T.psl[:, 208:256], bo, T.ok3[:, 32:80], False, False)
+                pe.matmul(T.psl[:, 224:256], bo, T.ok3[:, 80:112], False, False)
+            if early == 4:
+                pe.matmul(T.psl[:, 208:256], bo, T.eq[:, 208:256], False, True)
 
         def commit(i):
             if i == 0:
@@ -689,23 +690,29 @@ def rank_program(g, core, T, topo):
                    r=[("B", 0), ("B", 1), "PL"] + (["DL"] + [("CB", d) for d in range(3)] if last else [("R", 0)]), w=["eqa"])
             if i == 1:
                 op("V", lambda: v.tensor_tensor(T.ok2[:], ind(T.eq[:, 0:80], T.PL2[:, 0:6]), T.eq[:, 80:176], Op.add), r=["eqa", "PL2"], w=["ok2"])
-                lin("A", T.ok3[:], ind(T.ok2[:], T.AL[:, 0:5]), 1.0, 0.0, ["ok2", "AL"], ["ok3"])
+                lin("A", T.ok3[:, 0:80], ind(T.ok2[:], T.AL[:, 0:5]), 1.0, 0.0, ["ok2", "AL"], ["ok3"])
             if i == -1:
                 op("P", lambda: paths(0), r=["Ib"] + [("CTl" if last else "CT", d) for d in range(5)], w=["sel"], b=["psl"])
             if i == 11:
                 op("P", lambda: paths(1), r=["eqa", "ok2", "ok3", "BOb", "BOb0"], w=["sel"], b=["psl"])
+            if i == 12:
+                src = ind(T.CB[:, 0:64], T.DL2[:, 0:2]) if last else ind(R(0, 128), T.PL2[:, 6:8])
+                op("V", lambda: v.tensor_tensor(T.eq[:, 176:208], src, T.B[:, 176:208], Op.is_equal),
+                   r=[("B", 2), "PL2"] + (["DL2"] + [("CB", d) for d in range(4)] if last else [("R", 0), ("R", 1)]), w=["eqm"])
+                op("P", lambda: paths(2), r=["eqm"], w=["sel"], b=["psl"])
+                lin("A", T.ok3[:, 80:112], ind(T.eq[:, 0:208], T.PL[:, 14:16]), 1.0, 0.0, ["eqa", "eqm", "PL"], ["ok4"])
+            if i == 13:
+                op("V", lambda: v.tensor_reduce(T.psl[:, 256:257], T.psl[:, 0:208], Ax.X, Op.max), r=["sel"], w=["sel"], b=["psl"])
+                op("P", lambda: paths(3), r=["ok4", "ok3"], w=["sel"], b=["psl"])
             if i == 2:
-                src = ind(T.CB[:, 0:80], T.DL2[:, 0:5]) if last else ind(R(0, 200), T.PL2[:, 6:11])
-                op("V", lambda: v.tensor_tensor(T.eq[:, 176:256], src, T.B[:, 176:256], Op.is_equal),
+                src = ind(T.CB[:, 0:80], T.DL2[:, 2:5]) if last else ind(R(0, 200), T.PL2[:, 8:11])
+                op("V", lambda: v.tensor_tensor(T.eq[:, 208:256], src, T.B[:, 208:256], Op.is_equal),
                    r=[("B", 2), ("B", 3), "PL2"] + (["DL2"] + [("CB", d) for d in range(5)] if last else [("R", 0), ("R", 1), ("R", 2)]), w=["eq"])
-                op("P", lambda: paths(2), r=["eq"], w=["sel"], b=["psl"])
+                op("P", lambda: paths(4), r=["eq"], w=["sel"], b=["psl"])
             if i == 3:
-                op("V", lambda: v.tensor_reduce(T.bf[:, 0:1], T.psl[:, 0:256], Ax.X, Op.max), r=["sel"], w=["bf"], b=["psl"])
-            if i == 4:
-                op("A", lambda: a.activation(T.ig[:], ind(T.ISC[:], T.bq[:, 0:1]), Fn.Copy), r=["bq"] + IK, w=["ig"])
+                op("V", lambda: v.tensor_reduce(T.bf[:, 0:1], T.psl[:, 208:257], Ax.X, Op.max), r=["sel"], w=["bf"], b=["psl"])
             if i == 5:
-                op("V", lambda: v.tensor_tensor(T.X[:, 16 * t:16 * t + 16], ind(Y(-8, 256), T.bq[:, 0:1]), T.ig[:], Op.mult),
-                   r=["bq", "ig", ("Y", 3)], w=[("X", t)])
+                lin("A", T.X[:, 16 * t:16 * t + 16], ind(Y(-8, 256), T.bq[:, 0:1]), 1.0, 0.0, ["bq", "Y0", ("Y", 3)], [("X", t)])
 
         def chain(i, st):
             c, xk = (T.cc[:, 2 * i:2 * i + 1], ("XC", i)) if i else (T.c0[:, 2:3], ("Yr", t))
@@ -723,74 +730,77 @@ def rank_program(g, core, T, topo):
                 op("A", lambda: a.activation(T.CB[:, 16 * i:16 * i + 16], ind(T.IO[:], c), Fn.Copy), r=[("cc", i)] + IOK, w=[("CB", i)])
             if st == 1:
                 op("V", lambda: v.tensor_tensor(T.cb[:], ind(T.K[:], T.ccu[:, 0:8]), T.thx[:], Op.is_ge), r=["K", "ccu", "thx"], w=["cb"])
+                op("P", lambda: pe.matmul(T.ps1[:, 0:128], T.Ih[:], T.tkh[:], False, False), r=["tkh", "Ih"], w=["cB"], b=["ps1"])
                 op("P", lambda: pe.matmul(T.ps0[:, 0:128], T.BO16[:], T.cb[:], False, True), r=["cb", "BO16"], w=["cA"], b=["ps0"])
-                op("P", lambda: pe.matmul(T.ps1[:, 0:128], T.BO16[:], T.cb[:], False, False), r=["cb", "BO16"], w=["cB"], b=["ps1"])
-                op("P", lambda: pe.matmul(T.ps1[:, 0:128], T.Ih[:], T.tkh[:], False, True), r=["tkh", "Ih"], w=["cB"], b=["ps1"])
+                op("P", lambda: pe.matmul(T.ps1[:, 0:128], T.BO16[:], T.cb[:], False, True), r=["cb", "BO16"], w=["cB"], b=["ps1"])
             if st == 2:
                 op("V", lambda: v.tensor_reduce(T.cm[:, 0:1], T.ps0[:, 0:128], Ax.X, Op.max), r=["cA"], w=["m2"], b=["ps0"])
                 op("V", lambda: v.tensor_reduce(T.cm[:, 1:2], T.ps1[:, 0:128], Ax.X, Op.max), r=["cB"], w=["m1"], b=["ps1"])
             if st == 3:
                 c1 = T.cc[:, 2 * i + 2:2 * i + 3]
-                op("V", lambda: v.tensor_scalar(c1, T.cm[:, 1:2], T.cm[:, 0:1], 4096.0, Op.subtract, Op.mult), r=["m1", "m2"], w=[("cc", i + 1)])
-                if i == 4:
-                    op("A", lambda: a.activation(T.CB[:, 80:96], ind(T.IO[:], c1), Fn.Copy), r=[("cc", 5)] + IOK, w=[("CB", 5)])
+                op("V", lambda: v.tensor_scalar(c1, T.cm[:, 1:2], T.cm[:, 0:1], T.bf[:, 1:2] if i == 4 else 4096.0, Op.subtract, Op.mult),
+                   r=["m1", "m2"] + (["deep"] if i == 4 else []), w=[("cc", i + 1)])
 
-        def unscale(d0, d1):
-            for lo, hi, (d, x) in runs([(DEP[n], NODE[n] - n) for n in range(32)]):
-                if d0 <= d < d1:
-                    lin("A", T.YN[:, 8 * (lo + x):8 * (hi + x)], Y(8 * lo, 8 * hi), 0.5 ** d, 0.0, [("Y", 1 if d < 3 else d - 1)], [("YN", lo)])
-        YNK = lambda d0, d1: [("YN", lo) for lo, hi, (d, x) in runs([(DEP[n], NODE[n] - n) for n in range(32)]) if d0 <= d < d1]
+        def reseat(h, e):
+            lo, hi, lst = ((0, 176, T.SE[:, 0:11]), (176, 256, T.SE[:, 12:17]))[h]
+            lin(e, T.YN[:, lo:hi], ind(Y(0, hi), lst), 1.0, 0.0, ["Y0", ("Y", 1 + 2 * h)] + SEK, [("YN", h)])
 
         def results(i):
             if i == 0:
-                send(rr, T.YL[:, 0:176], T.YN[:, 0:176], "yn0", YNK(0, 3))
+                send(rr, T.YL[:, 0:176], T.YN[:, 0:176], "yn0", [("YN", 0)])
             if i == 1:
                 lin("V", T.bq[:, 0:1], T.bf[:, 0:1], 16.0, C(SC), ["bf"] + CK, ["bq"])
-                op("V", lambda: v.tensor_copy(T.YN[:, 256:272], ind(T.XC[:], T.bq[:, 0:1])), r=["bq", ("Yr", t)] + [("XC", d) for d in range(1, 5)], w=["X"])
+                cmp(T.bf[:, 1:2], T.bf[:, 0:1], 3.5, 4096.0, Op.is_gt, ["bf"], ["deep"])
+                lin("A", T.YN[:, 256:272], ind(T.XC[:], T.bq[:, 0:1]), 1.0, 0.0, ["bq", ("Yr", t)] + [("XC", d) for d in range(1, 5)], ["X"])
+                lin("A", T.ig[:], ind(T.CB[:, 16:96], T.bq[:, 0:1]), 1.0, 0.0, ["bq"] + [("CB", d) for d in range(6)], ["ig"])
+                send(rr, T.YL[:, 176:264], T.YN[:, 176:264], "yn1", ["X", ("YN", 1)])
             if i == 2:
-                op("V", lambda: v.tensor_copy(T.YN[:, 272:288], ind(T.CB[:, 16:96], T.bq[:, 0:1])),
-                   r=["bq"] + [("CB", d) for d in range(6)], w=["X2"])
-                send(rr, T.YL[:, 176:280], T.YN[:, 176:280], "fin", ["X", "X2"] + YNK(3, 5))
+                op("V", lambda: v.tensor_tensor(T.YN[:, 272:288], ind(T.IO[:], T.cc[:, 10:11]), T.ig[:], Op.add), r=["ig", ("cc", 5)] + IOK, w=["X2"])
+                send(rr, T.YL[:, 272:280], T.YN[:, 272:280], "fin", ["X2"])
 
         def roots(i):
             ls = T.ls[:, 16 * t:16 * t + 16]
-            root(i, R(-8, 256), [("R", x) for x in range(4)] + [("Rz", t)], ls, "ls")
+            root(i, R(-8, 256), [("R", x) for x in range(4)] + [("Rz", t)], ls, "ls", 20 + t)
             if i == 1:
                 if t == S - 2:
-                    send(verifier(rr, t + 1), T.c0[:], ls, "c0", ["ls"], turn=1)
+                    send(verifier(rr, t + 1), T.c0[:], ls, "c0", ["ls"], turn=3)
                     lands(("cc", 0), "c0")
-                send(rr, T.l0[:, 16 * t + 16:16 * t + 32], ls, "l%d" % (t + 1), ["ls"], turn=t == S - 2)
+                send(rr, T.l0[:, 16 * t + 16:16 * t + 32], ls, "l%d" % (t + 1), ["ls"], turn=3 * (t == S - 2))
                 lands(("l0", t + 1), "l%d" % (t + 1))
 
         def passed():
             n = 16 if t == S - 2 else 8
-            send(verifier(rr, t + 1), T.XC[:, 0:16] if t == S - 2 else Y(256, 264), T.X[:, 16 * t:16 * t + n], "x%d" % (t + 1), [("X", t)], turn=t == S - 2)
+            send(verifier(rr, t + 1), T.XC[:, 0:16] if t == S - 2 else Y(256, 264), T.X[:, 16 * t:16 * t + n], "x%d" % (t + 1), [("X", t)], turn=3 * (t == S - 2))
             lands(("Yr", t + 1), "x%d" % (t + 1))
 
         def once(i):
             if (t, i) == (0, 0):
-                dma("S", T.Q[:], T.qt[:], "dq2", r=["left"], w=["Q"], lag=7.0)
-            if (t, i) == (0, 1) or (t < 2 and i == 2):
-                late(i + t)
+                dma("S", T.Q[:], T.qt[:], "dq2", r=[("left", 3)], w=["Q"], lag=7.0)
+                op("G", lambda: gp.affine_select(T.DM[:, 1152:2048], T.DM[:, 1152:2048], [[0, 7], [-1, 128]], Op.not_equal, 2048.0, 0, 1),
+                   r=[("DM", x) for x in range(9, 16)] + [("left", 3)], w=["DMb"])
+            if (t, i) == (0, 1) or (t > 0 and i == 2):
+                late(i + t - (t > 0))
 
         for m in range(0 if last else 3):
             lands(("Rl", t, m), "r%d%d" % (t, m))
         named = dict(pick=pick, listed=listed, emitted=emitted, repeat=repeat, scatter=scatter, cand=cand, half=half, gather=gather,
-                     numbers=numbers, state=state, thresh=thresh, compare=compare, keys=keys, diffs=diffs, signs=signs, places=places,
-                     ranked=ranked, tokens=tokens, commit=commit, chain=chain, unscale=unscale, results=results, roots=roots,
+                     halves=halves, state=state, thresh=thresh, compare=compare, keys=keys, diffs=diffs, signs=signs, places=places,
+                     ranked=ranked, tokens=tokens, commit=commit, chain=chain, reseat=reseat, results=results, roots=roots,
                      passed=passed, once=once, prepare=prepare, best=best_lists, mark=root_mark)
         for call in (LAST if last else STEP).replace("\n", " ").split(","):
             words, n0 = call.split(), len(nodes)
             named[words[0]](*[x if x in "VA" else int(x) for x in words[1:]])
             for nd in nodes[n0:]:
                 nd["tag"] = (t, " ".join(words))
+                nd["haste"] = HASTE[last].get(" ".join(words[:2]), HASTE[last].get(words[0], 0.0))
         RK = [("Rl", t, m) for m in range(3)]
 
     lands("YL0", "yn0")
+    lands("YL1", "yn1")
     lands("XL", "fin")
     dma("S", T.yn[:, 0:176], T.YL[:, 0:176], "dout", r=["YL0"])
-    dma("S", T.yn[:, 176:256], T.YL[:, 176:256], "dout", r=["XL"])
-    dma("A", T.yx[:], T.YL[:, 256:264], "dout", r=["XL"])
+    dma("S", T.yn[:, 176:256], T.YL[:, 176:256], "dout", r=["YL1"])
+    dma("S", T.yx[:], T.YL[:, 256:264], "dout", r=["YL1"])
     dma("A", T.yt[:, 24:32], T.YL[0:128:16, 272:280], "dout", r=["XL"])
     for nd in arrange(nodes, tables):
         emit(nd)

from concourse.mybir import AluOpType as Op, AxisListType as Ax, ActivationFunctionType as Fn

V, S = 3840, 4
PAR = [0, 0, 0, 0, 0, 0, 0, 0, 0, 0, 0, 1, 1, 1, 1, 2, 2, 2, 3, 3, 4, 4, 11, 11, 11, 15, 15, 18, 22, 22, 23, 25]
ROW = [0, 0, 1, 2, 3, 4, 5, 6, 7, 8, 9, 0, 10, 11, 1, 0, 12, 13, 0, 14, 0, 15, 0, 1, 2, 0, 3, 0, 0, 5, 0, 0]
SWAP = (14, 24, 30)
NODE = [n ^ 1 if n - n % 2 in SWAP else n for n in range(32)]
PAR, ROW = [NODE.index(PAR[n]) for n in NODE], [ROW[n] for n in NODE]
DEP = [0]
for _n in range(1, 32):
    DEP.append(DEP[PAR[_n]] + 1)
ANC = [(PAR[n] if DEP[n] == 3 else PAR[PAR[n]]) - 10 for n in range(22, 32)]
L, U, B = 1, 2, 3
LEVELS = [[(1, B), (0, L), (2, B), (3, U), (3, L), (4, B), (5, U), (6, L), (7, U), (8, L), (9, U), (9, U)],
          [(10, L), (11, U), (14, L), (18, U), (15, U), (11, B), (18, L), (19, U), (12, L), (13, U), (16, L), (17, U), (20, L), (21, U)],
          [(22, B), (23, U), (24, L), (25, U), (26, L), (27, U)],
          [(28, L), (29, U), (30, L), (31, U)]]
LOFF = [0, 96, 208, 256, 288]
PC = [(0, 5), (5, 11), (11, 14), (14, 16)]


def _end(lv, pair):
    now = [None, None]
    for i, (n, who) in enumerate(LEVELS[lv]):
        now = [n if who & L else now[0], n if who & U else now[1]]
        if tuple(now) == pair:
            return 8 * i + 7


OWN = [[_end(lv, (2 * c, 2 * c + 1)) for c in range(*PC[lv])] for lv in range(4)]
NEXT = [[_end(lv, (PAR[x[0]], PAR[y[0]])) for x, y in zip(LEVELS[lv + 1][0::2], LEVELS[lv + 1][1::2])] for lv in range(3)]
MINE = [8, 0, 2, 0]
THEN = [0, 6, 0]
TAKE = [[(OWN[lv][x - MINE[lv]] if 0 <= x - MINE[lv] < len(OWN[lv]) else NEXT[lv][min(x - THEN[lv], len(NEXT[lv]) - 1)])
         for x in range(16)] for lv in range(3)]
FC, FP, FA, FT, FE, FD = 288, 576, 832, 912, 960, 960
POS = [(0, 64), (64, 128), (128, 200), (200, 256)]
BACK = [(0, 128), (128, 200), (200, 256)]
DD = [(0, 4, 96), (4, 10, 208), (10, 16, 288)]
RL = V + 32
TOP = 28672
QCUT = 2560
NE = 8

SCRATCH = {
    "Q": ("sbuf", [128, V], "int32"), "K": ("sbuf", [128, V], "bfloat16"), "AW": ("sbuf", [128, RL + 256], "int32"),
    "IO": ("sbuf", [128, V], "float32"), "IOb": ("sbuf", [128, 144], "bfloat16"),
    "xs": ("sbuf", [128, 8], "float32"), "IK": ("sbuf", [128, 256], "bfloat16"), "IG": ("sbuf", [128, 128], "bfloat16"),
    "IJ": ("sbuf", [128, 256], "bfloat16"), "IS": ("sbuf", [128, FC], "bfloat16"),
    "FX": ("sbuf", [128, FC], "bfloat16"), "RX": ("sbuf", [128, FC], "bfloat16"), "c0": ("sbuf", [128, 16], "uint16"),
    "BO": ("sbuf", [128, 128], "float16"), "BO16": ("sbuf", [128, 128], "float16"), "Ib": ("sbuf", [128, 128], "bfloat16"),
    "I16": ("sbuf", [128, 256], "bfloat16"), "GT": ("sbuf", [128, 256], "bfloat16"), "one": ("sbuf", [128, 2], "float16"),
    "D1": ("sbuf", [128, 2 * FC], "bfloat16"), "F2": ("sbuf", [128, FC], "bfloat16"), "GM": ("sbuf", [128, 8], "float32"),
    "RZ": ("sbuf", [128, 256], "bfloat16"), "sc": ("sbuf", [128, FC], "float32"), "GL": ("sbuf", [128, 6], "uint16"),
    "AL": ("sbuf", [128, 6], "uint16"), "ok3": ("sbuf", [128, 112], "bfloat16"),
    "TM": ("sbuf", [128, 256], "bfloat16"), "LX": ("sbuf", [128, 16], "uint16"),
    "kp": ("sbuf", [128, 4], "float32"), "pi": ("sbuf", [128, 32], "int32"), "pj": ("sbuf", [128, 32], "int32"),
    "C": ("sbuf", [128, 20], "float32"), "CJ": ("sbuf", [128, 16], "float32"),
    "Zb": ("sbuf", [128, 144], "bfloat16"), "Zh": ("sbuf", [128, 144], "float16"),
    "Ih": ("sbuf", [128, 128], "float16"), "DM": ("sbuf", [128, 2048], "bfloat16"),
    "XC": ("sbuf", [128, 80], "float32"), "CB": ("sbuf", [128, 96], "float32"), "cc": ("sbuf", [128, 12], "uint16"),
    "ccu": ("sbuf", [128, 16], "uint16"), "thx": ("sbuf", [128, 128], "float32"),
    "cb": ("sbuf", [128, 128], "float16"), "hx": ("sbuf", [128, 16], "float32"), "cm": ("sbuf", [128, 2], "float32"),
    "TIE": ("sbuf", [128, 256], "bfloat16"),
    "DL": ("sbuf", [128, 16], "uint16"), "DL2": ("sbuf", [128, 6], "uint16"),
    "cf": ("sbuf", [128, 256], "float32"), "F": ("sbuf", [128, FD + 256], "bfloat16"),
    "PL": ("sbuf", [128, 16], "uint16"), "PL2": ("sbuf", [128, 12], "uint16"),
    "CX": ("sbuf", [128, 8], "uint16"), "SE": ("sbuf", [128, 18], "uint16"),
    "bf": ("sbuf", [128, 4], "float32"), "M": ("sbuf", [128, 16], "float32"), "bl": ("sbuf", [128, 8], "uint16"),
    "w1": ("sbuf", [128, 128], "float16"), "l0": ("sbuf", [128, 64], "uint16"), "ls": ("sbuf", [128, 48], "uint16"),
    "wf": ("sbuf", [128, 176], "float32"), "wh": ("sbuf", [128, 176], "float16"),
    "O": ("sbuf", [128, 256], "uint16"),
    "LM": ("sbuf", [128, 96], "uint16"), "Y": ("sbuf", [128, 4 * 264], "float32"),
    "cu": ("sbuf", [128, 256], "uint16"), "kn": ("sbuf", [128, 256], "float32"),
    "kc": ("sbuf", [128, 4096], "bfloat16"), "bits": ("sbuf", [128, 4096], "float16"),
    "key": ("sbuf", [128, 256], "bfloat16"), "sg": ("sbuf", [128, 2048], "bfloat16"),
    "R": ("sbuf", [128, 3 * 264], "int32"), "B": ("sbuf", [128, 256], "float32"), "eq": ("sbuf", [128, 256], "bfloat16"),
    "ok2": ("sbuf", [128, 96], "bfloat16"), "BOb": ("sbuf", [128, 256], "bfloat16"),
    "CT": ("sbuf", [128, 768], "bfloat16"), "tkh": ("sbuf", [128, 128], "float16"),
    "bq": ("sbuf", [128, 4], "uint16"), "ig": ("sbuf", [128, 16], "float32"), "X": ("sbuf", [128, 3 * 16], "float32"),
    "Bo": ("sbuf", [128, 256], "float16"), "ed": ("sbuf", [128, 512], "bfloat16"), "ds": ("sbuf", [128, 256], "float32"),
    "OF": ("sbuf", [128, 16], "uint16"), "yb": ("sbuf", [128, 48], "float32"),
    "YN": ("sbuf", [128, 288], "float32"), "YL": ("sbuf", [128, 288], "float32"),
    "pth": ("psum", [128, 512], "float32"), "psl": ("psum", [128, 512], "float32"),
    "ps0": ("psum", [128, 512], "float32"), "ps1": ("psum", [128, 512], "float32"),
    "pa0": ("psum", [128, 512], "float32"), "pb0": ("psum", [128, 512], "float32"),
    "pa1": ("psum", [128, 512], "float32"), "pb1": ("psum", [128, 512], "float32"),
}
SEMAPHORES = (["sv", "sa", "sp", "sq", "sent", "dtok", "dx", "dkap", "dk", "dout", "yn0", "yn1", "fin", "dq0", "dq1", "dq2", "sent3"]
              + ["m%d%d" % (t, i) for t in range(S) for i in range(4)] + ["c0"] + ["r%d%d" % (t, i) for t in range(3) for i in range(3)]
              + ["x%d" % t for t in range(S)] + ["l%d" % t for t in range(1, S)])


STEP = """pick 0, emitted, listed 0, once 2, pick 1, listed 1, pick 2, halves 0 A, thresh 0, cand 0 A, listed 2, state 0, gather 0 24 A,
gather 24 40 V, gather 40 64 A, thresh 1, pick 3, cand 1 V, halves 1 A, listed 3, once 0,
repeat 0 0, repeat 1 0, repeat 2 0, repeat 0 1, repeat 1 1, repeat 2 1, repeat 3 0, repeat 3 1, repeat 3 2, repeat 3 3,
repeat 4 0, repeat 5 0, gather 64 80 A, state 1, gather 80 104 A, gather 104 128 A, thresh 2,
compare 0 0 16, keys 0 V, diffs 0 0, half 0 A, gather 128 152 A, gather 152 176 A, cand 2 V, halves 2 V, state 2,
thresh 3, compare 1 0 16, signs 0 0 V, places 0 0, keys 1 V, diffs 1 0, gather 176 200 A, ranked 0,
half 1 V, compare 2 0 16, signs 1 0 A, places 1 0, cand 3 V, gather 200 224 A, gather 224 256 A, halves 3 A,
state 3, thresh 4, keys 2 V, diffs 2 0, diffs 2 1, ranked 1, half 2 V, compare 3 0 16, signs 2 0 A, signs 2 1 A,
places 2 0, places 2 1, tokens 0 V, tokens 1 A, once 1, commit -1, commit 0, commit 1, commit 11, tokens 2 A, commit 12,
commit 13, keys 3 V, ranked 2, diffs 3 0, diffs 3 1, diffs 3 2, tokens 3 A, commit 2, half 3 V,
signs 3 0 A, signs 3 1 A, signs 3 2 V, places 3 0, places 3 1, places 3 2,
commit 3, best, ranked 3, commit 5, passed, mark, roots 0, roots 1,
repeat 0 2, repeat 0 3, repeat 1 2, repeat 2 2, repeat 3 4, repeat 3 5, repeat 3 6, repeat 3 7, repeat 4 1, repeat 5 1,
scatter 0, scatter 2, scatter 4, scatter 6, scatter 8, scatter 10, scatter 12, scatter 14,
prepare 0, prepare 1, prepare 2, prepare 3"""
LAST = """chain 0 0, pick 0, commit -1, chain 0 1, emitted, listed 0, chain 0 2, pick 1, chain 0 3, chain 1 0, listed 1, chain 1 1,
pick 2, chain 1 2, tokens 0 A, listed 2, chain 1 3, chain 2 0, halves 0 A, pick 3, chain 2 1, state 0, tokens 1 A, halves 1 A,
chain 2 2, listed 3, chain 2 3, chain 3 0, commit 0, chain 3 1, tokens 2 A, commit 1, state 1, halves 2 A, chain 3 2,
reseat 0 A, commit 11, commit 12, commit 13, state 2, halves 3 A, chain 3 3, chain 4 0, tokens 3 A, commit 2, chain 4 1,
state 3, commit 3, results 0, reseat 1 A, chain 4 2, results 1, chain 4 3, results 2"""
HASTE = [{"diffs": 2.0, "ranked": 1.5, "compare 2": 1.5, "signs 2": 1.5, "commit 13": 1.5, "keys 3": 1.0, "commit 0": 1.0,
          "roots 0": 1.0, "gather": 0.3, "commit 1": 0.3, "compare": -0.3, "cand": -0.6, "listed": -0.6, "diffs 3": -0.6,
          "once": -1.0, "signs": -1.0, "places 3": -1.0, "half": -1.0, "scatter": -1.5, "state": -1.5},
         {"results": -0.3, "pick": -1.0, "halves": -1.0}]


def runs(vals):
    out, a = [], 0
    for i in range(1, len(vals) + 1):
        if i == len(vals) or vals[i] != vals[a]:
            out.append((a, i, vals[a]))
            a = i
    return out


def ramps(vals):
    out, a = [], 0
    while a < len(vals):
        b, d = a + 1, (vals[a + 1] - vals[a] if a + 1 < len(vals) else 0)
        while b < len(vals) and vals[b] - vals[b - 1] == d:
            b += 1
        out.append((a, b, vals[a], d))
        a = b
    return out


CYCLE, WAKE, ISSUE, FLIGHT, PER_BYTE = 0.00092, 0.165, 0.4, 1.3, 0.0013
TURNS, FIRST = 2, 0
ITEM = {"float32": 4, "int32": 4, "bfloat16": 2, "float16": 2, "uint16": 2}


def size(ap):
    return ap.shape[-1]


def cost(name, fn, args, kw):
    if name == "matmul":
        return max(64, size(args[2])) * CYCLE
    if name == "iota":
        return 0.15 + 2 * size(args[0]) * CYCLE
    if isinstance(args[0], tuple):
        return 0.05 + 3.8 * size(args[1]) * CYCLE
    if isinstance(args[1], tuple):
        return (0.065 if name == "act" else 0.05) + 1.56 * size(args[0]) * CYCLE
    sides = [SCRATCH[x.name] for x in args[:3 if name in ("pair", "scan") else 2] if not isinstance(x, (int, float))]
    rate = 1.0
    if name == "pair" and all(x[0] == "sbuf" for x in sides[1:]):
        rate = 2.0
    if name in ("copy", "scan") and all(ITEM[x[2]] == 2 for x in sides):
        rate = 0.5
    return (0.02 if name == "act" else 0.005) + max(64, rate * size(args[1 if name == "reduce" else 0])) * CYCLE


def arrange(nodes, tables):
    wr, rd, bank, far = {}, {}, {}, {nd["far"]: i for i, nd in enumerate(nodes) if "far" in nd}
    deps, kids, turns = [], [[] for nd in nodes], []
    for i, nd in enumerate(nodes):
        d = {wr[k] for k in nd["r"]} | {bank[k] for k in nd["b"] if k in bank}
        for k in nd["w"]:
            d |= set(rd.get(k, [])) | ({wr[k]} if k in wr else set())
        if nd["e"] == "L":
            d.add(far[nd["sem"]])
        if nd.get("turn"):
            d |= set([j for j in turns if nodes[j]["turn"] == nd["turn"]][-1:])
            turns.append(i)
        d.discard(i)
        deps.append(d)
        for j in d:
            kids[j].append(i)
        for k in nd["r"]:
            rd.setdefault(k, []).append(i)
        for k in nd["w"]:
            wr[k], rd[k] = i, []
        for k in nd["b"]:
            bank[k] = i

    def gap(j, i):
        if j in turns and i in turns:
            return 0.0
        return nodes[j]["lag"] + (0.0 if nodes[i]["e"] == "L" or nodes[i]["e"] == nodes[j]["e"] == "P" else WAKE)
    chain, depth, left, todo = {}, {}, [len(k) for k in kids], [i for i, k in enumerate(kids) if not k]
    while todo:
        i = todo.pop()
        depth[i] = -len(depth)
        chain[i] = nodes[i]["busy"] + max([gap(i, k) + chain[k] for k in kids[i]] + [nodes[i]["lag"]])
        for j in deps[i]:
            left[j] -= 1
            if not left[j]:
                todo.append(j)

    def place(before, after, wait, first, rank):
        end, taken, left = {}, {}, [len(d) for d in before]
        ready = [i for i, d in enumerate(before) if not d]
        while ready:
            c = max(ready, key=lambda i: (rank[i], -i))
            ready.remove(c)
            t, need = max([end[j] + wait(j, c) for j in before[c]] + [first(c)]), nodes[c]["busy"]
            line = taken.setdefault(nodes[c]["e"], [])
            at = 0
            for at, (lo, hi) in enumerate(line + [(1e9, 1e9)]):
                if t + need <= lo + 1e-9:
                    break
                t = max(t, hi)
            line.insert(at, (t, t + need))
            end[c] = t + need
            for k in after[c]:
                left[k] -= 1
                if not left[k]:
                    ready.append(k)
        return end
    best, rank = None, {}
    for i in chain:
        rank[i] = max([-i if i >= tables else -1e9] + [rank[k] + 1e-6 for k in kids[i]])
    chain = rank
    for turn in range(TURNS):
        end = place(deps, kids, gap, lambda i: 0.0, chain)
        total = max(end[i] + nodes[i]["lag"] for i in end)
        if best is None or total < best[0]:
            best = (total, end)
        back = place(kids, deps, lambda j, i: gap(i, j), lambda i: nodes[i]["lag"], {i: end[i] - nodes[i].get("haste", 0.0) for i in end})
        chain = {i: back[i] + nodes[i].get("haste", 0.0) for i in back}
    return [nodes[i] for i in sorted(best[1], key=lambda i: (round(best[1][i] - nodes[i]["busy"], 6), depth[i]))]


def rank_program(g, core, T, topo):
    rank = T.rank_of(core)
    if rank is None:
        return
    n_ranks = len(T.cores)
    qu = {"V": g.vector, "A": g.scalar, "P": g.tensor, "G": g, "S": g.sync}
    semof = {"V": "sv", "A": "sa", "P": "sp", "G": "sq"}
    cnt = {}
    waited = {e: {} for e in qu}
    wr, rd, bank = {}, {}, {}

    def need(e, tok):
        if tok is not None and waited[e].get(tok[0], 0) < tok[1]:
            qu[e].wait_ge(T.sem[tok[0]], tok[1])
            waited[e][tok[0]] = tok[1]

    def order(e, r, w, b):
        own = semof.get(e)
        best = {}
        toks = [wr[k] for k in r]
        for k in w:
            toks += [t for t in [wr.get(k)] + rd.get(k, []) if t is not None and (e != "P" or t[0] != own)]
        toks += [bank[k] for k in b if k in bank and bank[k][0] != own]
        for t in toks:
            if t is not None:
                best[t[0]] = max(best.get(t[0], 0), t[1])
        for s in best:
            need(e, (s, best[s]))

    def note(tok, r, w, b):
        for k in r:
            rd.setdefault(k, []).append(tok)
        for k in w:
            wr[k] = tok
            rd[k] = []
        for k in b:
            bank[k] = tok

    def emit(nd):
        e, r, w, b, sem = nd["e"], nd["r"], nd["w"], nd["b"], nd["sem"]
        if e == "L":
            note((sem, NE), (), w, ())
            cnt[sem] = NE
            return
        order(e, r, w, b)
        ins = None
        for name, fn, args, kw in nd["calls"]:
            ins = fn(*[x[0] if isinstance(x, tuple) else x for x in args], **kw)
        step = NE if name == "remote_dma" else 16 if name == "dma_start" else 1
        cnt[sem] = cnt.get(sem, 0) + step
        if name == "remote_dma":
            note((sem, cnt[sem]), (), w, ())
        else:
            ins.then_inc(T.sem[sem], step)
            note((sem, cnt[sem]), r, w, b)

    nodes, said = [], []

    def noted(name, fn):
        return lambda *args, **kw: said.append((name, fn, args, kw))

    class v:
        memset, tensor_copy = noted("copy", g.vector.memset), noted("copy", g.vector.tensor_copy)
        tensor_scalar, tensor_tensor = noted("copy", g.vector.tensor_scalar), noted("pair", g.vector.tensor_tensor)
        tensor_reduce, tensor_tensor_scan = noted("reduce", g.vector.tensor_reduce), noted("scan", g.vector.tensor_tensor_scan)

    class a:
        activation = noted("act", g.scalar.activation)

    class pe:
        matmul = noted("matmul", g.tensor.matmul)

    class gp:
        iota, affine_select = noted("iota", g.iota), noted("iota", g.affine_select)

    def ind(win, lst):
        return (win.indirect(lst),)

    def op(e, fn, r=(), w=(), b=(), turn=0):
        fn()
        nodes.append(dict(e=e, turn=turn, calls=said[:], r=r, w=w, b=b, sem=semof[e], busy=sum(cost(*c) for c in said), lag=0.0))
        del said[:]

    def dma(e, out, in_, sem, r=(), w=(), lag=1.4, turn=0):
        nodes.append(dict(e=e, turn=turn, calls=[("dma_start", qu[e].dma_start, (out, in_), {})], r=r, w=w, b=(), sem=sem, busy=0.05, lag=lag))

    def send(to, out, in_, sem, r, local="sent", w=(), turn=0):
        dst = T.cores[to]
        rid, pid = topo.addr(dst)[:2]
        mask = sum(1 << e for e in topo.engines(core, dst)[:NE])
        nodes.append(dict(e="G", turn=turn, calls=[("remote_dma", g.remote_dma, (out, in_, T.sem[sem], T.sem[local], pid, rid, mask), {})],
                          r=r, w=w, b=(), sem=local, far=sem, busy=ISSUE, lag=FLIGHT + size(in_) * ITEM[SCRATCH[in_.name][2]] * PER_BYTE))

    def lands(key, sem):
        nodes.append(dict(e="L", calls=[], r=(), w=[key], b=(), sem=sem, busy=0.0, lag=0.0))

    C = lambda i: T.C[:, i:i + 1]
    KF, G16, SC, NB, NK, KB, Z15, PF, GI, ZC, SP0, BC, NKP, KT, KR, SP1, KX, HC, UP, KS = range(20)

    def lin(e, out, in_, mul, add, r, w, b=()):
        if e == "A":
            op("A", lambda: a.activation(out, in_, Fn.Identity, bias=add, scale=mul), r=r, w=w, b=b)
        else:
            op("V", lambda: v.tensor_scalar(out, in_, mul, add, Op.mult, Op.add), r=r, w=w, b=b)

    def cmp(out, in_, col, mul, how, r, w):
        op("V", lambda: v.tensor_scalar(out, in_, col, mul, how, Op.mult), r=r, w=w)

    def iota(out, pattern, key):
        op("G", lambda: gp.iota(out, pattern, 0, 0, allow_small_or_imprecise_dtypes=True), w=[key])

    def verifier(r, t):
        return (r + 1 + t % (n_ranks - 1)) % n_ranks

    def drafter(q, t):
        return (q - 1 - t % (n_ranks - 1)) % n_ranks

    op("V", lambda: v.memset(T.AW[:, RL:RL + 8], 0), w=["Rl"])
    dma("A", T.xs[:], T.x0[:], "dx", w=["xs"])
    dma("S", T.AW[0:128:16, RL:RL + 8], T.tok[:], "dtok", w=["Rl"], turn=1)
    dma("S", T.AW[:, 0:QCUT], T.qt[:, 0:QCUT], "dq0", w=["A0"], lag=5.2, turn=1)
    dma("A", T.kp[:, 0:1], T.kap[:], "dkap", w=["kp"])
    dma("S", T.AW[:, QCUT:V], T.qt[:, QCUT:V], "dq1", w=["A"], lag=7.1, turn=1)
    dma("S", T.K[:], T.kt[:], "dk", r=["A0"], w=["K"], lag=4.6)

    op("G", lambda: gp.iota(T.pi[:, 0:1], [[0, 1]], 0, 1), w=["pi"])
    iota(T.IO[:, 0:256], [[1, 256]], "IO0")
    op("G", lambda: gp.iota(T.pi[:, 16:32], [[-1, 16]], 16, 1), w=["pi2"])
    iota(T.IJ[:], [[1, 32], [0, 8]], "IJ")
    iota(T.IS[:], [[0, 36], [1, 8]], "IS")
    iota(T.IG[:], [[16, 8], [0, 16]], "IG")
    op("V", lambda: v.memset(T.M[:], 0.0), w=["M"])
    op("V", lambda: v.memset(T.bf[:], 0.5), w=["bf"])
    for col, m in ((0, 15), (1, 112), (2, 7), (3, 8)):
        op("V", lambda: v.tensor_scalar(T.pj[:, col:col + 1], T.pi[:, 0:1], m, None, Op.bitwise_and), r=["pi"], w=[("pj", col)])
    op("V", lambda: v.tensor_copy(C(PF), T.pi[:, 0:1]), r=["pi"], w=["C1"])
    op("V", lambda: v.tensor_copy(T.C[:, 0:4], T.pj[:, 0:4]), r=[("pj", i) for i in range(4)], w=["C0"])
    op("V", lambda: v.tensor_scalar(T.pj[:, 16:32], T.pi[:, 16:32], 15, None, Op.bitwise_and), r=["pi2"], w=["pj2"])
    op("V", lambda: v.tensor_copy(T.IOb[:], T.IO[:, 0:144]), r=["IO0"], w=["IOb"])
    op("V", lambda: v.tensor_scalar(T.CJ[:], T.pj[:, 16:32], C(G16), None, Op.add), r=["pj2", "C0"], w=["CJ"])
    for col, src, mul, add in ((Z15, G16, 1.0, 15.0), (KT, KF, 4096.0, -2048.0), (ZC, KF, -4096.0, 2048.0), (GI, G16, 0.0625, 0.0),
                               (BC, NB, -0.125, 1.0), (HC, NB, -0.125, 2.0), (UP, NB, 0.125, 0.0), (KS, KF, -4096.0, 30720.0), (KR, KF, -4096.0, 32768.0), (NK, KF, -4096.0, 0.0), (KB, KF, -1.0, -121.0),
                               (SP0, KF, 1.0, float(V)), (SP1, KF, 1.0, float(V + 16))):
        lin("A", C(col), C(src), mul, add, ["C0"], [("C", col)])
    CK = ["C0", "C1"] + [("C", c) for c in (Z15, KT, ZC, GI, BC, HC, UP, KS, KR, NK, KB, SP0, SP1)]

    def shifts(j0, j1):
        for j in range(j0, j1):
            cmp(T.DM[:, 128 * j:128 * j + 128], T.IOb[:, 0:128], T.CJ[:, j:j + 1], 2048.0 if j <= 8 else -2048.0, Op.is_equal, ["IOb", "CJ"], [("DM", j)])
    shifts(1, 9)
    send(verifier(rank, 0), T.Y[:, 0:8], T.xs[:], "x0", ["xs"], turn=2)
    lands(("Yr", 0), "x0")
    op("G", lambda: gp.iota(T.IO[:, V - 1024:V], [[1, 1024]], V - 1024, 0, allow_small_or_imprecise_dtypes=True), w=["IO5"], turn=2)
    op("G", lambda: gp.affine_select(T.DM[:, 128:1152], T.DM[:, 128:1152], [[0, 8], [-1, 128]], Op.not_equal, -2048.0, 0, 1),
       r=[("DM", x) for x in range(1, 9)], w=["DMa"], turn=2)
    shifts(9, 16)
    shifts(0, 1)
    rows = [ROW[n] for lv in LEVELS for n, who in lv]
    todo = [(FP + 8 * lo, FP + 8 * hi, T.IJ, 8 * p, 8 * d) for lo, hi, p, d in ramps(PAR)]
    todo += [(FD + 8 * lo, FD + 8 * hi, T.IJ, 16 * p, 0) for lo, hi, p in runs(DEP)]
    todo += [(FA + 8 * lo, FA + 8 * hi, T.IJ, 8 * p, 8 * d) for lo, hi, p, d in ramps(ANC)]
    todo += [(FT + lo, FT + hi, T.IOb, p, d) for lo, hi, p, d in ramps(TAKE[0] + TAKE[1] + TAKE[2])]
    todo += [(8 * lo, 8 * hi, T.IJ, 4096 * p - 30720, 4096 * d) for lo, hi, p, d in ramps(rows)]
    todo += [(FC + 8 * lo, FC + 8 * hi, T.IJ, p, d) for lo, hi, p, d in ramps([who for lv in LEVELS for n, who in lv])]
    for i, (lo, hi, src, val, d) in enumerate(todo):
        lin("VA"[i % 2], T.F[:, lo:hi], src[:, 0:hi - lo], float(d), float(val), ["IJ", "IOb"], [("F", lo)])
    fk = lambda lo, hi: [("F", x[0]) for x in todo if lo <= x[0] < hi]
    FK = fk(0, FP)
    cmp(T.Zb[:], T.IOb[:], C(Z15), 1.0, Op.is_equal, ["IOb"] + CK, ["Zb"])

    def select(lo, hi, outs):
        op("P", lambda: [pe.matmul(T.ps1[:, 0:(hi - lo) // 16], T.Zb[:, 15 - i:143 - i], T.F[:, lo + i:hi:16], i == 0, i == 15) for i in range(16)],
           r=fk(lo, hi) + ["Zb"], w=[("S", 1)], b=["ps1"])
        for dst, c0, c1, s2, key in outs:
            lin("V", dst, T.ps1[:, c0:c1], 0.0625, s2, [("S", 1)] + CK, [key], ["ps1"])
    select(FT, FE, [(T.GL[:, 0:6:2], 0, 3, 0.0, "GL")])
    cmp(T.GM[:], T.IO[:, 0:8], C(GI), 16.0, Op.is_equal, ["IO0"] + CK, ["GM"])
    lin("V", T.one[:], T.IO[:, 0:2], 0.0, 1.0, ["IO0"], ["one"])
    lin("V", T.AW[:, V:RL], T.IO[:, 0:32], 0.0, C(ZC), ["IO0"] + CK, ["spare"])
    cmp(T.Ib[:], T.IOb[:, 0:128], C(PF), 1.0, Op.is_equal, ["IOb"] + CK, ["Ib"])
    cmp(T.BO[:], T.IG[:], C(G16), 1.0, Op.is_equal, ["IG"] + CK, ["BO"])
    lin("A", T.F2[:], T.F[:, 0:FC], 1.0, C(KR), FK + CK, ["F2"])
    cmp(T.D1[:, 0:FC], T.IS[:], C(SC), -65536.0, Op.not_equal, ["IS"] + CK, ["D1"])
    cmp(T.D1[:, FC:2 * FC], T.F[:, FC:FP], C(HC), -65536.0, Op.is_equal, FK + CK, ["D2"])
    op("V", lambda: v.memset(T.RX[:], 0.0), w=["RX"])
    cmp(T.RX[:, 0:FC:8], T.F[:, FC:FP:8], C(HC), -1048576.0, Op.not_equal, FK + CK, ["RX"])
    op("P", lambda: [pe.matmul(T.ps0[:, 0:FC], T.Ib[:], x, i == 0, i == 2) for i, x in enumerate((T.F[:, 0:FC], T.D1[:, 0:FC], T.D1[:, FC:2 * FC]))],
       r=["Ib", "D1", "D2"] + FK, w=["fx"], b=["ps0"])
    lin("A", T.FX[:], T.ps0[:, 0:FC], 1.0, 0.0, ["fx"], ["FX"], ["ps0"])
    PB = [T.pa1, T.pb1, T.pa0, T.pb0]

    def prepare(lv):
        op("P", lambda: pe.matmul(PB[lv][:, 0:LOFF[lv + 1] - LOFF[lv]], T.Ib[:], T.FX[:, LOFF[lv]:LOFF[lv + 1]], True, False),
           r=["Ib", "FX"], w=[PB[lv].name], b=[PB[lv].name])

    def best_lists():
        lin("V", T.bl[:], T.GM[:], T.bf[:, 0:1], C(SC), ["bf", "GM"] + CK, ["bl"])
        lin("V", T.bq[:, 0:1], T.bf[:, 0:1], 16.0, C(SC), ["bf"] + CK, ["bq"])

    def root_mark():
        op("V", lambda: v.tensor_scalar(T.M[:, 0:1], T.bq[:, 0:1], float(RL - 8 + TOP), C(UP), Op.add, Op.mult), r=["bq", "M"] + CK, w=["M0"])

    def root(i, win, keys, out, okey, turn=0):
        if i == 0:
            op("V", lambda: v.tensor_scalar(T.w1[:], ind(win, T.bl[:]), C(KT), 2048.0, Op.add, Op.min), r=keys + ["bl"] + CK, w=["w1"])
            op("P", lambda: pe.matmul(T.psl[:, 0:1], T.w1[:], T.one[:, 0:1], True, True), r=["w1", "one"], w=["sel"], b=["psl"], turn=turn)
        else:
            op("V", lambda: v.tensor_scalar(out, T.M[:], T.psl[:, 0:1], float(TOP), Op.max, Op.subtract), r=["M0", "sel"], w=[okey], b=["psl"])
    best_lists()
    root_mark()
    root(0, T.AW[:, RL - 8:RL + 8], ["Rl", "spare"], None, None)
    for lv in range(4):
        prepare(lv)
    select(FP, FT, [(T.PL[:], 0, 16, C(SC), "PL"), (T.PL2[:, 0:11], 5, 16, C(SC), "PL2"), (T.AL[:, 0:5], 16, 21, C(SC), "AL")])
    root(1, None, None, T.l0[:, 0:16], ("l0", 0))
    RK = ["Rl"]
    cmp(T.Zh[:], T.IOb[:], C(Z15), 1.0, Op.is_equal, ["IOb"] + CK, ["Zh"])
    cmp(T.Ih[:], T.IOb[:, 0:128], C(PF), 1.0, Op.is_equal, ["IOb"] + CK, ["Ih"])
    cmp(T.I16[:, 0:128], T.IOb[:, 0:128], C(PF), 16384.0, Op.is_equal, ["IOb"] + CK, ["I16"])
    cmp(T.I16[:, 128:256], T.IOb[:, 0:128], C(PF), 32768.0, Op.is_equal, ["IOb"] + CK, ["I32"])
    op("V", lambda: v.tensor_tensor(T.IK[:, 0:128], T.IOb[:, 0:128], T.IG[:], Op.subtract), r=["IOb", "IG"], w=["IK0"])
    op("V", lambda: v.tensor_copy(T.IK[:, 128:256], T.IK[:, 0:128]), r=["IK0"], w=["IK"])
    cmp(T.GT[:], T.IK[:], C(KF), 0.5, Op.is_gt, ["IK"] + CK, ["GT"])
    lin("A", C(KX), C(BC), 8.0, C(SC), CK, ["KX"])
    for n in SWAP:
        cmp(T.GT[:, 8 * n:8 * n + 16], T.IK[:, 8:24], C(KX), 0.5, Op.is_gt, ["IK", "KX", "GT"], [("GT", n)])
    cmp(T.RZ[:], T.IK[:], 0.0, -1048576.0, Op.is_equal, ["IK"], ["RZ"])
    LXK = []
    for c0, c1, p, d in ramps([LOFF[lv] + x for lv in range(4) for x in OWN[lv]]):
        LXK.append(("LX", c0))
        lin("A", T.LX[:, c0:c1], T.IO[:, 0:c1 - c0], float(d), float(p), ["IO0"], [LXK[-1]])
    cmp(T.CT[:, 512:768], T.IS[:, 0:256], C(SC), -128.0, Op.not_equal, ["IS"] + CK, ["CTm"])
    op("P", lambda: [pe.matmul(T.ps0[:, 0:256], T.Ib[:], x, i == 0, i == 1) for i, x in enumerate((T.IJ[:], T.CT[:, 512:768]))],
       r=["Ib", "IJ", "CTm"], w=["fx"], b=["ps0"])
    for lo, hi, d in runs(DEP):
        lin("A", T.CT[:, 8 * lo:8 * hi], T.ps0[:, 8 * lo:8 * hi], 0.5, 0.5 - 16 * d, ["fx"], [("CT", d)], ["ps0"])
    cmp(T.BOb[:, 0:128], T.IG[:], C(G16), 1.0, Op.is_equal, ["IG"] + CK, ["BOb0"])
    cmp(T.BOb[:, 128:256], T.IG[:], C(G16), 16.0, Op.is_equal, ["IG"] + CK, ["BOb"])
    for i, n in enumerate((256, 512, 1024, 2048)):
        m = min(2 * n, V - 1024)
        lin("A", T.IO[:, n:m], T.IO[:, 0:m - n], 1.0, float(n), ["IO%d" % j for j in range(i + 1)], ["IO%d" % (i + 1)])
    IOK = ["IO%d" % j for j in range(6)]
    SEK = [("SE", n) for n in SWAP]

    def late(i):
        if i == 1:
            for x in range(3):
                lin("A", T.R[:, 264 * x:264 * x + 8], T.IO[:, 0:8], 0.0, C(ZC), ["IO0"] + CK, [("Rz", x)])
        if i == 2:
            op("V", lambda: v.tensor_scalar(T.TM[:, 0:128], T.IG[:], 0.0625, C(SC), Op.mult, Op.not_equal), r=["IG"] + CK, w=["TM0"])
            lin("A", C(NKP), T.kp[:, 0:1], -1.0, 0.0, ["kp"], ["NKP"])
            lin("A", T.TM[:, 128:256], T.IK[:, 0:128], -1.0, 15.0, ["IK"], ["TM1"])
            lin("A", T.TM[:, 0:128], T.TM[:, 0:128], -512.0, 0.0, ["TM0"], ["TM0"])
            for lo, hi, d in runs(DEP):
                lin("A", T.CT[:, 256 + 8 * lo:256 + 8 * hi], T.CT[:, 512 + 8 * lo:512 + 8 * hi], 1.0, -15.0 * d, ["CTm"], [("CTl", d)])
            lin("A", T.CX[:], T.IO[:, 0:8], 1.0, 0.0, ["IO0"], ["CX"])
            lin("A", T.SE[:, 0:11], T.IO[:, 0:11], 16.0, C(KF), ["IO0"] + CK, ["SEa"])
            lin("A", T.SE[:, 12:17], T.IO[:, 11:16], 16.0, C(KF), ["IO0"] + CK, ["SEb"])
            for n in SWAP:
                x = n // 2 + (n > 21)
                lin("A", T.SE[:, x:x + 1], T.IO[:, n // 2:n // 2 + 1], 16.0, C(KX), ["IO0", "KX", "SEa", "SEb"], [("SE", n)])
        if i == 3:
            select(FD, FD + 256, [(T.DL[:], 0, 16, C(SC), "DL"), (T.DL2[:, 0:5], 11, 16, C(SC), "DL2")])
            op("V", lambda: v.tensor_tensor(T.TIE[:, 0:128], T.TM[:, 0:128], T.TM[:, 128:256], Op.add), r=["TM0", "TM1"], w=["TIE0"])
            lin("A", T.TIE[:, 128:256], T.TIE[:, 0:128], 1.0, 0.5, ["TIE0"], ["TIE"])
            lin("A", T.BO16[:], T.BOb[:, 128:256], 1.0, 0.0, ["BOb"], ["BO16"])
            lin("A", T.CB[:, 80:96], T.IO[:, 0:16], 0.0, 0.0, ["IO0"], [("CB", 5)])

    tables = len(nodes)
    for t in range(S):
        q, rr = verifier(rank, t), drafter(rank, t)
        last = t == S - 1
        l0 = T.l0[:, 16 * t:16 * t + 16]
        O = lambda lv, lo, n: T.O[:, 64 * t + 16 * lv + lo:64 * t + 16 * lv + lo + n]
        outs = [O(0, 0, 16), O(1, 0, 16), O(2, 0, 16), O(3, 0, 2)]
        lists = [l0[:, 0:6]] + [O(lv, THEN[lv], len(NEXT[lv])) for lv in range(3)]
        mine = [O(lv, MINE[lv], len(OWN[lv])) for lv in range(4)]
        mineK = [[("L", lv + 1)] for lv in range(4)]
        lm = lambda c0, c1: T.LM[:, 24 * t + c0 + (c0 > 0) + (c0 > 13):24 * t + c1 + (c0 > 0) + (c0 > 13)]
        mk = lambda c: ("LM", t, [c < hi for lo, hi in PC].index(True))
        for i in range(4):
            lands(("LM", t, i), "m%d%d" % (t, i))

        def pick(lv):
            n, lo = 8 * len(LEVELS[lv]), LOFF[lv]
            win = T.AW[:, 0:RL + (256 if t else 8)] if lv == 0 else T.AW[:, 0:V]
            op("V", lambda: v.tensor_tensor(T.wf[:, 0:n], ind(win, lists[lv]), T.F2[:, lo:lo + n], Op.subtract),
               r=["A", "A0", "spare", "F2"] + (RK + [("l0", t)] if lv == 0 else [("L", lv)]), w=["wf"])
            op("V", lambda: v.tensor_scalar(T.wh[:, 0:n], T.wf[:, 0:n], -2048.0, 2048.0, Op.max, Op.min), r=["wf"], w=["wh"])
            op("P", lambda: pe.matmul(PB[lv][:, 0:n], T.BO[:], T.wh[:, 0:n], False, True), r=["wh", "BO"], w=[PB[lv].name], b=[PB[lv].name])

        def listed(lv):
            n, lo = 8 * len(LEVELS[lv]), LOFF[lv]
            op("V", lambda: v.tensor_tensor_scan(T.sc[:, lo:lo + n], T.RX[:, lo:lo + n], PB[lv][:, 0:n], 0.0, Op.add, Op.max),
               r=[PB[lv].name, "RX"], w=[("sc", lv)], b=[PB[lv].name])
            src = ind(T.sc[:, lo:lo + n], T.GL[:, 2 * lv:2 * lv + 1]) if lv < 3 else T.sc[:, lo + 15:lo + n:16]
            op("V", lambda: v.tensor_scalar(outs[lv], src, 2048.0, None, Op.add), r=[("sc", lv), "GL"], w=[("L", lv + 1)])
            send(q, lm(*PC[lv]), mine[lv], "m%d%d" % (t, lv), mineK[lv] + (["DMa", "IO5"] if t == 0 else []),
                 *(("sent3", [("left", 3)]) if (t, lv) == (0, 3) else ()))

        def emitted():
            if t > 0:
                op("A", lambda: a.activation(T.yb[:, 16 * t - 16:16 * t], ind(T.IO[:], l0[:, 2:3]), Fn.Copy), r=[("l0", t)] + IOK, w=[("yb", t)])
                dma("S", T.yt[:, 8 * t - 8:8 * t], T.yb[0:128:16, 16 * t - 16:16 * t - 8], "dout", r=[("yb", t)])

        def repeat(i, p=0):
            c0, c1, end = DD[min(p, 2)]
            c2 = min(c1, 15)
            sk = [("sc", lv) for lv in range(4) if LOFF[lv] < end]
            if i == 0:
                lo, hi = 16 * PC[p][0], 16 * PC[p][1]
                op("A", lambda: a.activation(T.Bo[:, lo:hi], ind(T.IO[:], mine[p]), Fn.Identity, bias=-2048.0), r=mineK[p] + IOK, w=[("Bo", p)])
            bk = [("Bo", x) for x in range(p + 1 + p // 2)]
            if i == 1:
                op("V", lambda: v.tensor_tensor(T.ed[:, 16 * c0:16 * c1], ind(T.sc[:, 0:end], T.LX[:, c0:c1]), T.Bo[:, 16 * c0:16 * c1], Op.is_equal),
                   r=sk + bk + LXK, w=[("ed", 0, p)])
            if i == 2:
                op("V", lambda: v.tensor_tensor(T.ed[:, 256 + 16 * c0:256 + 16 * c2], ind(T.sc[:, 0:end], T.LX[:, c0:c2]),
                                                T.Bo[:, 16 * c0 + 16:16 * c2 + 16], Op.is_equal), r=sk + bk + LXK, w=[("ed", 1, p)])
            if i == 3:
                x, part = p % 4, p // 4
                lo, hi = ((0, 160), (160, 240 if x == 3 else 256))[part]
                lhs, rhs, key = ((T.I16[:, 0:128], T.GT[:, lo:hi], [("GT", n) for n in SWAP]),
                                 (T.Ih[:], T.Bo[:, lo:hi], [("Bo", y) for y in range(part, 2 + 2 * part)]),
                                 (T.I16[:, 0:128], T.ed[:, lo:hi], [("ed", 0, y) for y in range(2 * part, 2 + part)]),
                                 (T.I16[:, 128:256], T.ed[:, 256 + lo:256 + hi], [("ed", 1, y) for y in range(2 * part, 2 + part)]))[x]
                op("P", lambda: pe.matmul(T.pb1[:, lo:hi], lhs, rhs, x == 0, x == 3), r=key + ["I16", "I32", "Ih"], w=["pb1"], b=["pb1"],
                   turn={3: 10 + t, 4: 20 + t}.get(p, 0))
            lo, hi = ((0, 160), (160, 256))[p % 2]
            if i == 4:
                op("V", lambda: v.tensor_tensor_scan(T.ds[:, lo:hi], T.RZ[:, lo:hi], T.pb1[:, lo:hi], 0.0, Op.add, Op.max), r=["pb1", "RZ"], w=[("ds", p)], b=["pb1"])
            if i == 5:
                for h in range(2):
                    op("V", lambda: v.tensor_scalar(T.OF[:, lo // 16 + h:hi // 16:2], T.ds[:, lo + 16 * h + 15:hi:32], 2048.0 - 16384.0, C(SP1 if h else SP0), Op.add, Op.min),
                       r=[("ds", p)] + CK, w=[("OF", p, h)])

        def scatter(c):
            keys = [("Rl", t, m) for m in range(3) if BACK[m][0] < 16 * c + 32 and 16 * c < BACK[m][1]]
            op("V", lambda: v.tensor_copy(ind(T.AW[:, 0:RL], T.OF[:, c:c + 2]), T.AW[:, RL + 16 * c:RL + 16 * c + 32]),
               r=keys + [("OF", c // 10, 0), ("OF", c // 10, 1)], w=["A", "A0", "spare"])

        qwin, QK = (T.AW[:, 0:V], ["A", "A0"]) if t == 0 else (T.Q[:], ["Q"])
        y0 = 264 * t + 8
        Y = lambda j0, j1: T.Y[:, y0 + j0:y0 + j1]
        R = lambda j0, j1: T.R[:, y0 + j0:y0 + j1]
        piece = lambda j: mk(j // 16)[2]
        KCK = [[] for x in POS]
        DB = [[(T.pa0, 1, 9)], [(T.pa1, 1, 9)], [(T.pa0, 1, 5), (T.pb0, 5, 9)], [(T.pa1, 1, 4), (T.pb0, 4, 7), (T.ps0, 7, 9)]]

        def cand(p, e="A"):
            c0, c1 = PC[p]
            lin(e, T.cu[:, 16 * c0:16 * c1], ind(qwin, lm(c0, c1)), 1.0, 0.0, QK + [mk(c0)], [("cu", p)])

        def half(m, e="A"):
            lo, hi = POS[m]
            lin(e, T.cf[:, lo:hi], T.cu[:, lo:hi], 1.0, C(KS), [("cu", p) for p in range(piece(hi - 1) + 1)] + CK, [("cf", m)])

        def gather(j0, j1, e="A"):
            lin(e, T.kc[:, 16 * j0:16 * j1], ind(T.K[:], T.cu[:, j0:j1]), 1.0, 0.0, ["K", ("cu", piece(j0))], [("kc", j0)])
            KCK[[lo <= j0 < hi for lo, hi in POS].index(True)].append(("kc", j0))

        x_in = T.XC[:, 0:8] if last else Y(-8, 0)

        def halves(i, e):
            win, lst = ((x_in, T.PL[:, 0:5]), (Y(0, 80), T.PL2[:, 0:6]), (Y(0, 176), T.PL2[:, 6:9]), (Y(0, 224), T.PL[:, 14:16]))[i]
            lin(e, T.kn[:, 16 * PC[i][0]:16 * PC[i][1]], ind(win, lst), 0.5, 0.0, ["PL", "PL2"] + ([("Y", i - 1), "Y0"] if i else [("Yr", t)]), [("kn", i)])

        def state(i):
            c0, c1 = PC[i]
            op("V", lambda: v.tensor_tensor(Y(16 * c0, 16 * c1), ind(T.K[:], lm(c0, c1)), T.kn[:, 16 * c0:16 * c1], Op.add),
               r=["K", mk(c0), ("kn", i)], w=[("Y", i)] + ([] if i else ["Y0"]))
            if i == 0:
                lin("A", Y(0, 8), x_in, 1.0, 0.0, [("Yr", t)], ["Y0"])

        TH = [(0, 8, ("Yr", t)), (8, 80, ("Y", 0)), (80, 176, ("Y", 1)), (176, 224, ("Y", 2)), (224, 256, ("Y", 3))]
        THK = [[j0 for j0, j1, i in TH if j0 < hi and lo < j1] for lo, hi in POS]

        def thresh(i):
            j0, j1, key = TH[i]
            op("V", lambda: v.tensor_scalar(T.pth[:, j0:j1], Y(j0, j1) if i else x_in, T.kp[:, 0:1], None, Op.subtract), r=[key, "kp"], w=[("th", j0)])

        def compare(m, k0, k1):
            j0, j1 = POS[m]
            n = j1 - j0
            ps = T["ps%d" % (m % 2)]
            for k in range(k0, k1):
                bo = 16 * j0 + n * k
                op("V", lambda: v.tensor_tensor(T.bits[:, bo:bo + n], T.kc[:, 16 * j0 + k:16 * j1:16], T.pth[:, j0:j1], Op.is_ge),
                   r=KCK[m] + [("th", x) for x in THK[m]], w=[("bits", m, k)])
                op("P", lambda: pe.matmul(ps[:, 0:n], T.Zh[:, 15 - k:143 - k], T.bits[:, bo:bo + n], k == 0, k == 15),
                   r=[("bits", m, k), "Zh"], w=[("S", m % 2)], b=[ps.name] if k in (0, 15) else [], turn=10 + t if (m, k) == (0, FIRST) else 0)

        def keys(m, e):
            j0, j1 = POS[m]
            ps = T["ps%d" % (m % 2)]
            lin(e, T.key[:, j0:j1], ps[:, 0:j1 - j0], 16.0, C(KB), [("S", m % 2)] + CK, [("key", m)], [ps.name])

        def diffs(m, h):
            j0, j1 = POS[m]
            n = j1 - j0
            pd, lo, hi = DB[m][h]
            op("P", lambda: [pe.matmul(pd[:, n * (j - lo):n * (j - lo + 1)], T.DM[:, 128 * j:128 * j + 128], T.key[:, j0:j1], True, True) for j in range(lo, hi)],
               r=[("key", m), "DMa"], w=[pd.name], b=[pd.name])

        def signs(m, h, e):
            n = POS[m][1] - POS[m][0]
            pd, lo, hi = DB[m][h]
            so, w = 8 * POS[m][0] + n * (lo - 1), n * (hi - lo)
            if e == "A":
                op("A", lambda: a.activation(T.sg[:, so:so + w], pd[:, 0:w], Fn.Sign), r=[pd.name], w=[("sg", m, h)], b=[pd.name])
            else:
                op("V", lambda: v.tensor_scalar(T.sg[:, so:so + w], pd[:, 0:w], -1.0, 1.0, Op.max, Op.min), r=[pd.name], w=[("sg", m, h)], b=[pd.name])

        def places(m, h):
            n = POS[m][1] - POS[m][0]
            so, ps = 8 * POS[m][0] - n, DB[m][0][0]
            op("P", lambda: [pe.matmul(ps[:, 0:n], T.DM[:, 128 * (16 - j if j < 8 else 0):128 * (17 - j if j < 8 else 1)], T.sg[:, so + n * j:so + n * j + n], j == 1, j == 8)
                             for j in range(*DB[m][h][1:])], r=[("sg", m, h), ("DM", 0), "DMb"], w=[ps.name], b=[ps.name])

        def ranked(m):
            lo, hi = POS[m]
            ps = DB[m][0][0]
            op("V", lambda: v.tensor_tensor(R(lo, hi), ps[:, 0:hi - lo], T.cf[:, lo:hi], Op.add), r=[ps.name, ("cf", m)], w=[("R", m)], b=[ps.name])
            if m:
                lo = BACK[m - 1][0]
                send(rr, T.AW[:, RL + lo:RL + hi], R(lo, hi), "r%d%d" % (t, m - 1), [("R", x) for x in range(m + 1) if POS[x][0] >= lo])

        def tokens(p, e="A"):
            c0, c1 = PC[p]
            lin(e, T.B[:, 16 * c0:16 * c1], ind(T.IO[:], lm(c0, c1)), 1.0, 0.0 if last else C(NK), IOK + CK + [mk(c0)], [("B", p)])

        def paths(early):
            bo, ct = (T.BOb[:, 0:128], 256) if last else (T.BOb[:, 128:256], 0)
            if early == 0:
                pe.matmul(T.psl[:, 0:208], T.Ib[:], T.CT[:, ct:ct + 208], True, False)
            if early == 1:
                pe.matmul(T.psl[:, 8:88], bo, T.eq[:, 8:88], False, False)
                pe.matmul(T.psl[:, 88:176], bo, T.ok2[:, 8:96], False, False)
                pe.matmul(T.psl[:, 176:208], bo, T.ok3[:, 0:32], False, False)
            if early == 2:
                pe.matmul(T.psl[:, 176:208], bo, T.eq[:, 176:208], False, True)
            if early == 3:
                pe.matmul(T.psl[:, 208:256], T.Ib[:], T.CT[:, ct + 208:ct + 256], True, False)
                pe.matmul(T.psl[:, 208:256], bo, T.ok3[:, 32:80], False, False)
                pe.matmul(T.psl[:, 224:256], bo, T.ok3[:, 80:112], False, False)
            if early == 4:
                pe.matmul(T.psl[:, 208:256], bo, T.eq[:, 208:256], False, True)

        def commit(i):
            if i == 0:
                src = ind(T.CB[:, 0:48], T.DL[:, 0:11]) if last else ind(R(0, 40), T.PL[:, 0:11])
                op("V", lambda: v.tensor_tensor(T.eq[:, 0:176], src, T.B[:, 0:176], Op.is_equal),
                   r=[("B", 0), ("B", 1), "PL"] + (["DL"] + [("CB", d) for d in range(3)] if last else [("R", 0)]), w=["eqa"])
            if i == 1:
                op("V", lambda: v.tensor_tensor(T.ok2[:], ind(T.eq[:, 0:80], T.PL2[:, 0:6]), T.eq[:, 80:176], Op.add), r=["eqa", "PL2"], w=["ok2"])
                lin("A", T.ok3[:, 0:80], ind(T.ok2[:], T.AL[:, 0:5]), 1.0, 0.0, ["ok2", "AL"], ["ok3"])
            if i == -1:
                op("P", lambda: paths(0), r=["Ib"] + [("CTl" if last else "CT", d) for d in range(5)], w=["sel"], b=["psl"])
            if i == 11:
                op("P", lambda: paths(1), r=["eqa", "ok2", "ok3", "BOb", "BOb0"], w=["sel"], b=["psl"])
            if i == 12:
                src = ind(T.CB[:, 0:64], T.DL2[:, 0:2]) if last else ind(R(0, 128), T.PL2[:, 6:8])
                op("V", lambda: v.tensor_tensor(T.eq[:, 176:208], src, T.B[:, 176:208], Op.is_equal),
                   r=[("B", 2), "PL2"] + (["DL2"] + [("CB", d) for d in range(4)] if last else [("R", 0), ("R", 1)]), w=["eqm"])
                op("P", lambda: paths(2), r=["eqm"], w=["sel"], b=["psl"])
                lin("A", T.ok3[:, 80:112], ind(T.eq[:, 0:208], T.PL[:, 14:16]), 1.0, 0.0, ["eqa", "eqm", "PL"], ["ok4"])
            if i == 13:
                op("V", lambda: v.tensor_reduce(T.psl[:, 256:257], T.psl[:, 0:208], Ax.X, Op.max), r=["sel"], w=["sel"], b=["psl"])
                op("P", lambda: paths(3), r=["ok4", "ok3"], w=["sel"], b=["psl"])
            if i == 2:
                src = ind(T.CB[:, 0:80], T.DL2[:, 2:5]) if last else ind(R(0, 200), T.PL2[:, 8:11])
                op("V", lambda: v.tensor_tensor(T.eq[:, 208:256], src, T.B[:, 208:256], Op.is_equal),
                   r=[("B", 2), ("B", 3), "PL2"] + (["DL2"] + [("CB", d) for d in range(5)] if last else [("R", 0), ("R", 1), ("R", 2)]), w=["eq"])
                op("P", lambda: paths(4), r=["eq"], w=["sel"], b=["psl"])
            if i == 3:
                op("V", lambda: v.tensor_reduce(T.bf[:, 0:1], T.psl[:, 208:257], Ax.X, Op.max), r=["sel"], w=["bf"], b=["psl"])
            if i == 5:
                lin("A", T.X[:, 16 * t:16 * t + 16], ind(Y(-8, 256), T.bq[:, 0:1]), 1.0, 0.0, ["bq", "Y0", ("Y", 3)], [("X", t)])

        def chain(i, st):
            c, xk = (T.cc[:, 2 * i:2 * i + 1], ("XC", i)) if i else (T.c0[:, 2:3], ("Yr", t))
            if st == 0:
                if i:
                    op("V", lambda: v.tensor_tensor(T.XC[:, 16 * i:16 * i + 16], ind(T.K[:], c), T.hx[:], Op.add), r=["K", ("cc", i), "hx"], w=[xk])
                op("A", lambda: a.activation(T.thx[:], ind(T.XC[:, 16 * i:16 * i + 8], T.CX[:]), Fn.Identity, bias=C(NKP)),
                   r=[xk, "CX", "NKP"], w=["thx"])
                op("V", lambda: v.tensor_copy(T.ccu[:], ind(T.Q[:], c)), r=QK + [("cc", i)], w=["ccu"])
                op("P", lambda: pe.matmul(T.ps0[:, 0:128], T.Ib[:], T.TIE[:, 0:128], True, False), r=["TIE", "Ib"], w=["cA"], b=["ps0"])
                op("P", lambda: pe.matmul(T.ps1[:, 0:128], T.Ib[:], T.TIE[:, 128:256], True, False), r=["TIE", "Ib"], w=["cB"], b=["ps1"])
                lin("A", T.tkh[:], ind(T.IO[:], T.ccu[:, 0:8]), 0.5 ** 12, -0.5, ["ccu"] + IOK, ["tkh"])
                if i < 4:
                    lin("A", T.hx[:], T.XC[:, 16 * i:16 * i + 16], 0.5, 0.0, [xk], ["hx"])
                op("A", lambda: a.activation(T.CB[:, 16 * i:16 * i + 16], ind(T.IO[:], c), Fn.Copy), r=[("cc", i)] + IOK, w=[("CB", i)])
            if st == 1:
                op("V", lambda: v.tensor_tensor(T.cb[:], ind(T.K[:], T.ccu[:, 0:8]), T.thx[:], Op.is_ge), r=["K", "ccu", "thx"], w=["cb"])
                op("P", lambda: pe.matmul(T.ps1[:, 0:128], T.Ih[:], T.tkh[:], False, False), r=["tkh", "Ih"], w=["cB"], b=["ps1"])
                op("P", lambda: pe.matmul(T.ps0[:, 0:128], T.BO16[:], T.cb[:], False, True), r=["cb", "BO16"], w=["cA"], b=["ps0"])
                op("P", lambda: pe.matmul(T.ps1[:, 0:128], T.BO16[:], T.cb[:], False, True), r=["cb", "BO16"], w=["cB"], b=["ps1"])
            if st == 2:
                op("V", lambda: v.tensor_reduce(T.cm[:, 0:1], T.ps0[:, 0:128], Ax.X, Op.max), r=["cA"], w=["m2"], b=["ps0"])
                op("V", lambda: v.tensor_reduce(T.cm[:, 1:2], T.ps1[:, 0:128], Ax.X, Op.max), r=["cB"], w=["m1"], b=["ps1"])
            if st == 3:
                c1 = T.cc[:, 2 * i + 2:2 * i + 3]
                op("V", lambda: v.tensor_scalar(c1, T.cm[:, 1:2], T.cm[:, 0:1], T.bf[:, 1:2] if i == 4 else 4096.0, Op.subtract, Op.mult),
                   r=["m1", "m2"] + (["deep"] if i == 4 else []), w=[("cc", i + 1)])

        def reseat(h, e):
            lo, hi, lst = ((0, 176, T.SE[:, 0:11]), (176, 256, T.SE[:, 12:17]))[h]
            lin(e, T.YN[:, lo:hi], ind(Y(0, hi), lst), 1.0, 0.0, ["Y0", ("Y", 1 + 2 * h)] + SEK, [("YN", h)])

        def results(i):
            if i == 0:
                send(rr, T.YL[:, 0:176], T.YN[:, 0:176], "yn0", [("YN", 0)])
            if i == 1:
                lin("V", T.bq[:, 0:1], T.bf[:, 0:1], 16.0, C(SC), ["bf"] + CK, ["bq"])
                cmp(T.bf[:, 1:2], T.bf[:, 0:1], 3.5, 4096.0, Op.is_gt, ["bf"], ["deep"])
                lin("A", T.YN[:, 256:272], ind(T.XC[:], T.bq[:, 0:1]), 1.0, 0.0, ["bq", ("Yr", t)] + [("XC", d) for d in range(1, 5)], ["X"])
                lin("A", T.ig[:], ind(T.CB[:, 16:96], T.bq[:, 0:1]), 1.0, 0.0, ["bq"] + [("CB", d) for d in range(6)], ["ig"])
                send(rr, T.YL[:, 176:264], T.YN[:, 176:264], "yn1", ["X", ("YN", 1)])
            if i == 2:
                op("V", lambda: v.tensor_tensor(T.YN[:, 272:288], ind(T.IO[:], T.cc[:, 10:11]), T.ig[:], Op.add), r=["ig", ("cc", 5)] + IOK, w=["X2"])
                send(rr, T.YL[:, 272:280], T.YN[:, 272:280], "fin", ["X2"])

        def roots(i):
            ls = T.ls[:, 16 * t:16 * t + 16]
            root(i, R(-8, 256), [("R", x) for x in range(4)] + [("Rz", t)], ls, "ls", 20 + t)
            if i == 1:
                if t == S - 2:
                    send(verifier(rr, t + 1), T.c0[:], ls, "c0", ["ls"], turn=3)
                    lands(("cc", 0), "c0")
                send(rr, T.l0[:, 16 * t + 16:16 * t + 32], ls, "l%d" % (t + 1), ["ls"], turn=3 * (t == S - 2))
                lands(("l0", t + 1), "l%d" % (t + 1))

        def passed():
            n = 16 if t == S - 2 else 8
            send(verifier(rr, t + 1), T.XC[:, 0:16] if t == S - 2 else Y(256, 264), T.X[:, 16 * t:16 * t + n], "x%d" % (t + 1), [("X", t)], turn=3 * (t == S - 2))
            lands(("Yr", t + 1), "x%d" % (t + 1))

        def once(i):
            if (t, i) == (0, 0):
                dma("S", T.Q[:], T.qt[:], "dq2", r=[("left", 3)], w=["Q"], lag=7.0)
                op("G", lambda: gp.affine_select(T.DM[:, 1152:2048], T.DM[:, 1152:2048], [[0, 7], [-1, 128]], Op.not_equal, 2048.0, 0, 1),
                   r=[("DM", x) for x in range(9, 16)] + [("left", 3)], w=["DMb"])
            if (t, i) == (0, 1) or (t > 0 and i == 2):
                late(i + t - (t > 0))

        for m in range(0 if last else 3):
            lands(("Rl", t, m), "r%d%d" % (t, m))
        named = dict(pick=pick, listed=listed, emitted=emitted, repeat=repeat, scatter=scatter, cand=cand, half=half, gather=gather,
                     halves=halves, state=state, thresh=thresh, compare=compare, keys=keys, diffs=diffs, signs=signs, places=places,
                     ranked=ranked, tokens=tokens, commit=commit, chain=chain, reseat=reseat, results=results, roots=roots,
                     passed=passed, once=once, prepare=prepare, best=best_lists, mark=root_mark)
        for call in (LAST if last else STEP).replace("\n", " ").split(","):
            words, n0 = call.split(), len(nodes)
            named[words[0]](*[x if x in "VA" else int(x) for x in words[1:]])
            for nd in nodes[n0:]:
                nd["tag"] = (t, " ".join(words))
                nd["haste"] = HASTE[last].get(" ".join(words[:2]), HASTE[last].get(words[0], 0.0))
        RK = [("Rl", t, m) for m in range(3)]

    lands("YL0", "yn0")
    lands("YL1", "yn1")
    lands("XL", "fin")
    dma("S", T.yn[:, 0:176], T.YL[:, 0:176], "dout", r=["YL0"])
    dma("S", T.yn[:, 176:256], T.YL[:, 176:256], "dout", r=["YL1"])
    dma("S", T.yx[:], T.YL[:, 256:264], "dout", r=["YL1"])
    dma("A", T.yt[:, 24:32], T.YL[0:128:16, 272:280], "dout", r=["XL"])
    for nd in arrange(nodes, tables):
        emit(nd)
    for s in sorted(cnt):
        if max(waited[e].get(s, 0) for e in qu) < cnt[s]:
            need("S" if s == "dout" else "G", (s, cnt[s]))
